import numpy as np
import ml_dtypes


def mxq(x, axis, fmt="e4m3"):
    dtype, down = {"e4m3": (ml_dtypes.float8_e4m3fn, 7), "e5m2": (ml_dtypes.float8_e5m2, 14)}[fmt]
    v = np.moveaxis(np.asarray(x, np.float32).astype(ml_dtypes.bfloat16).astype(np.float64), axis, -1)
    blocks = v.reshape(v.shape[:-1] + (-1, 32))
    amax = np.abs(blocks).max(-1, keepdims=True)
    byte = np.maximum(np.where(amax > 0, np.frexp(amax)[1] - 1 + 127, 0) - down, 1)
    scale = np.exp2(byte - 127.0)
    codes = (blocks / scale).astype(np.float32).astype(dtype).astype(np.float64)
    return np.moveaxis((codes * scale).reshape(v.shape), -1, axis)


WIDE = False


def mx_kscale(k):
    if not WIDE:
        return np.ones(k)
    levels = np.array([10, -10, 5, -5, 0])
    if k % 512:
        return np.exp2(np.random.permutation(np.resize(levels, k // 32))).repeat(32)
    a = np.empty((k // 512, 16))
    for p in range(k // 512):
        a[p, :8] = np.random.permutation(np.resize(levels, 8))
        for g in range(8):
            far = levels[np.abs(levels - a[p, g]) >= 10]
            a[p, g + 8] = far[np.random.randint(len(far))]
    return np.exp2(a.ravel()).repeat(32)


def f64(x):
    return np.asarray(x).astype(np.float64)


def striped(idx):
    return np.tile(np.asarray(idx).reshape(-1, 16).T, (8, 1)).astype(np.uint16)


def unstriped(offs):
    return offs[:16].T.reshape(-1).astype(np.int64)


E2M1 = np.array([0.0, 0.5, 1.0, 1.5, 2.0, 3.0, 4.0, 6.0, -0.0, -0.5, -1.0, -1.5, -2.0, -3.0, -4.0, -6.0])


def pack_weight(w, fmt):
    k, n = w.shape
    w = f64(np.asarray(w, np.float32).astype(ml_dtypes.bfloat16)).reshape(k // 32, 32, n)
    amax = np.abs(w).max(1)
    if fmt == "e4m3":
        byte = np.frexp(amax)[1] - 1 + 127 - 7
    else:
        mant, ex = np.frexp(amax / 6.0)
        byte = np.where(mant > 0.5, ex, ex - 1) + 127
    byte = np.clip(np.where(amax > 0, byte, 1), 1, 254)
    scaled = (w * np.exp2(127.0 - byte)[:, None, :]).reshape(k, n).astype(np.float32)
    by_word = np.ascontiguousarray(scaled.reshape(k // 512, 128, 4, n).transpose(0, 1, 3, 2))
    if fmt == "e4m3":
        words = by_word.astype(ml_dtypes.float8_e4m3fn).view(np.uint8)
    else:
        c = by_word.astype(ml_dtypes.float4_e2m1fn).view(np.uint8) & 0xF
        words = (c[..., 0::2] | (c[..., 1::2] << 4)).reshape(k // 512, 128, 2 * n)
    return np.ascontiguousarray(words), np.ascontiguousarray(byte.astype(np.uint8).reshape(k // 512, 16, n))


def unpack_weight(words, scales, fmt):
    g, _, n = scales.shape
    words = np.ascontiguousarray(words).reshape(g, 128, n, -1)
    if fmt == "e4m3":
        vals = words.view(ml_dtypes.float8_e4m3fn).astype(np.float64)
    else:
        nib = np.empty((g, 128, n, 4), np.uint8)
        nib[..., 0::2] = words & 0xF
        nib[..., 1::2] = words >> 4
        vals = E2M1[nib]
    vals = vals * np.repeat(np.exp2(scales.astype(np.float64) - 127.0), 8, axis=1)[..., None]
    return vals.transpose(0, 1, 3, 2).reshape(g * 512, n)


B, N, T, D, DV, NQ = 1, 512, 2048, 1024, 256, 128
CAP = 2.0


def setup_inputs():
    n = np.random.standard_normal
    idx = np.sort(np.random.permutation(T)[:B * N].reshape(B, N), axis=1).reshape(-1)
    s = mx_kscale(D)[:, None]
    u = np.ones(T)
    u[idx] = mx_kscale(B * N)
    r = np.random.uniform(0.5, 2.0, T)
    qp = [pack_weight(x, "e4m3") for x in n((B, D, NQ)) * s * (1.00 / np.sqrt(D))]
    k = n((D, T)) / s
    v = n((DV, T)) / (u * r)
    kp = pack_weight(k, "e2m1")
    return {
        "q_words": np.stack([x[0] for x in qp]),
        "q_scales": np.stack([x[1] for x in qp]),
        "k_words": np.ascontiguousarray(kp[0].reshape(D // 1024, 2, 128, T, 2).transpose(0, 2, 3, 1, 4)).reshape(D // 1024, 128, T, 4),
        "k_scales": kp[1],
        "vT": v.astype(np.float32),
        "vs": np.tile(u * r, (128, 1)).astype(np.float32),
        "offs": striped(idx),
    }


def reference(q_words, q_scales, k_words, k_scales, vT, vs, offs):
    idx = unstriped(offs)
    k = unpack_weight(k_words.reshape(D // 1024, 128, T, 2, 2).transpose(0, 3, 1, 2, 4).reshape(D // 512, 128, 2 * T), k_scales, "e2m1")
    v = f64(vT)
    pick = lambda x: x[:, idx].reshape(x.shape[0], B, N).transpose(1, 0, 2)
    q = np.stack([unpack_weight(q_words[b], q_scales[b], "e4m3") for b in range(B)])
    score = q.transpose(0, 2, 1) @ pick(k)
    score = CAP * np.tanh(score / CAP)
    m = score.max(-1, keepdims=True)
    p = np.exp(score - m)
    total = p.sum(-1, keepdims=True)
    w = p * pick(f64(vs))[:, :1, :]
    y = mxq(w, 2, "e4m3") @ mxq(pick(v).transpose(0, 2, 1), 1, "e4m3")
    y = y / total
    return y

@@ -1,0 +1,166 @@
+from contextlib import ExitStack
+
+import concourse.mybir as mybir
+from concourse.masks import make_identity
+
+N, T, D, DV, NQ = 512, 2048, 1024, 256, 128
+CAP = 2.0
+FLOPS = 2 * NQ * N * (D + DV)
+
+F32 = mybir.dt.float32
+BF16 = mybir.dt.bfloat16
+I32 = mybir.dt.int32
+U32 = mybir.dt.uint32
+U16 = mybir.dt.uint16
+U8 = mybir.dt.uint8
+FP8X4 = mybir.dt.float8_e4m3fn_x4
+FP4X4 = mybir.dt.float4_e2m1fn_x4
+ACT = mybir.ActivationFunctionType
+ALU = mybir.AluOpType
+
+P = 128
+PASSES = D // 512
+HALVES = DV // P
+VS_ROW = 8
+
+
+def tile_attend_soft_cap_srtq128n512t2048_kernel(tc, q_words, q_scales, k_words, k_scales, vT, vs, offs, out):
+    nc = tc.nc
+    with ExitStack() as ctx:
+        sb = ctx.enter_context(tc.tile_pool(name="sb", bufs=1))
+        ps = ctx.enter_context(tc.psum_pool(name="ps", bufs=1))
+
+        offsets = sb.tile([P, N // 16], U16, name="offsets")
+        kw_pool = sb.tile([P, T], I32, name="kw_pool")
+        ks_pool = sb.tile([P, T], U8, name="ks_pool", tag="late_load")
+        ks1 = sb.tile([P, N], U8, name="ks1", align_bytes=64)
+        v_pool = [sb.tile([P, T], F32, name="v_pool0")]
+        vs_pool = sb.tile([P, T], F32, name="vs_pool")
+        qw = sb.tile([P, PASSES, NQ], I32, name="qw", align_bytes=64)
+        qs = sb.tile([P, PASSES, NQ], U8, name="qs", align_bytes=64)
+        ident = sb.tile([P, P], F32, name="ident")
+        warm_in = sb.tile([P, 1], F32, name="warm_in")
+        warm = sb.tile([P, 1], F32, name="warm")
+
+        nc.vector.memset(ks_pool[:].bitcast(I32), 0)
+        nc.vector.memset(warm_in[:], 0.0)
+        nc.vector.memset(ks1[:].bitcast(I32), 0)
+        nc.vector.memset(vs_pool[:], 0.0)
+        nc.gpsimd.memset(qs[:].bitcast(I32), 0)
+
+        nc.sync.dma_start(offsets[:], offs)
+        nc.sync.dma_start(kw_pool[:], k_words[0].rearrange("g t b -> g (t b)").bitcast(I32))
+        nc.sync.dma_start(qw[:], q_words[0].rearrange("o g q r -> g o (q r)").bitcast(I32))
+        nc.sync.dma_start(v_pool[0][:], vT[0:P, :])
+        ks_rows = k_scales.rearrange("o (quad r) t -> r quad o t", r=4)
+        for r in range(4):
+            nc.scalar.dma_start(ks_pool[r:P:16, :].bitcast(I32), ks_rows[r].bitcast(I32))
+        nc.scalar.activation(warm[:], warm_in[:], ACT.Exp)
+        nc.scalar.dma_start(vs_pool[VS_ROW : VS_ROW + 1, :], vs[0:1, :])
+        for quad in range(4):
+            nc.gpsimd.dma_start(
+                qs[32 * quad : 32 * quad + 4, :, :].bitcast(I32),
+                q_scales[0][:, 4 * quad : 4 * quad + 4, :].rearrange("o f q -> f o q").bitcast(I32),
+            )
+        make_identity(nc, ident[:])
+
+        ks0 = sb.tile([P, N], U8, name="ks0", align_bytes=64)
+        nc.vector.tensor_copy(ks0[:], ks_pool[:].indirect(offsets[:]))
+        nc.scalar.dma_start(ks1[0 : P - 16, :].bitcast(I32), ks0[16:P, :].bitcast(I32))
+        ks = [ks0, ks1]
+        v_pool.append(sb.tile([P, T], F32, name="v_pool1", tag="late_load"))
+        nc.sync.dma_start(v_pool[1][:], vT[P : 2 * P, :])
+        kw_pairs = sb.tile([P, N], U32, name="kw_pairs", tag="after_parting")
+        nc.vector.tensor_copy(kw_pairs[:], kw_pool[:].bitcast(U32).indirect(offsets[:]))
+        kw = sb.tile([P, PASSES, 2 * N], U8, name="kw", align_bytes=64)
+        nc.vector.tensor_copy(kw[:].bitcast(U16), kw_pairs[:].bitcast(U16).rearrange("p (n o) -> p o n", o=PASSES))
+
+        scores = ps.tile([P, N], F32, name="scores")
+        for o in range(PASSES):
+            nc.tensor.matmul_mx(
+                out=scores[:],
+                lhsT=qw[:, o, :].bitcast(FP8X4),
+                lhsT_scale=qs[:, o, :],
+                rhs=kw[:, o, :].bitcast(FP4X4),
+                rhs_scale=ks[o][:],
+                start=(o == 0),
+                stop=(o == PASSES - 1),
+            )
+
+        v_grouped = sb.tile([P, DV, 4], BF16, name="v_grouped", align_bytes=64)
+        v_codes = sb.tile([P, DV], U32, name="v_codes", align_bytes=64)
+        v_scales = sb.tile([P, DV], U8, name="v_scales", align_bytes=64)
+
+        def turn_values(h):
+            picked = sb.tile([P, N], BF16, name="v_picked%d" % h, tag=("v_picked", "after_max")[h])
+            nc.vector.tensor_copy(picked[:], v_pool[h][:].indirect(offsets[:]))
+            pairs = picked[:].bitcast(F32)
+            turned = ps.tile([P, 2, P], F32, name="v_turned%d" % h)
+            for u in range(2):
+                nc.tensor.transpose(turned[:, u, :], pairs[:, u : N // 2 : 2], ident[:])
+            nc.scalar.copy(v_grouped[:, h * P : (h + 1) * P, :].bitcast(F32), turned[:].rearrange("p u e -> p e u"))
+
+        def quantise_values(h):
+            cols = slice(h * P, (h + 1) * P)
+            nc.vector.quantize_mx(
+                out=v_codes[:, cols].bitcast(FP8X4),
+                scales=v_scales[:, cols],
+                in_=v_grouped[:, cols, :].rearrange("p e t -> p (e t)"),
+            )
+
+        capped = sb.tile([P, 4, P], F32, name="capped", tag="after_max")
+        nc.scalar.activation(capped[:], scores[:].rearrange("q (s t) -> q t s", t=4), ACT.Tanh, scale=1.0 / CAP)
+
+        vs_picked = sb.tile([P, N], F32, name="vs_picked", tag="after_parting")
+        nc.vector.tensor_copy(vs_picked[:], vs_pool[:].indirect(offsets[:]))
+        vs_turned = ps.tile([P, 4, P], F32, name="vs_turned")
+        for t in range(4):
+            nc.tensor.transpose(vs_turned[:, t, :], vs_picked[:, t:N:4], ident[:])
+        vs_cols = sb.tile([P, 4], F32, name="vs_cols")
+        nc.scalar.copy(vs_cols[:], vs_turned[:, :, VS_ROW])
+
+        turn_values(0)
+
+        scaled = sb.tile([P, N], F32, name="scaled")
+        neg_max = sb.tile([P, 1], F32, name="neg_max")
+        nc.vector.tensor_scalar(
+            scaled[:], capped[:].rearrange("q t s -> q (t s)"), -CAP, None, ALU.mult, ALU.min, accum_out=neg_max[:]
+        )
+        p = sb.tile([P, 4, P], F32, name="p")
+        total = sb.tile([P, 1], F32, name="total")
+        nc.scalar.activation(
+            p[:].rearrange("q t s -> q (t s)"), scaled[:], ACT.Exp, bias=neg_max[:], scale=-1.0, accum_out=total[:]
+        )
+
+        turn_values(1)
+
+        p_turned = ps.tile([P, 4, P], F32, name="p_turned")
+        for t in range(4):
+            nc.tensor.transpose(p_turned[:, t, :], p[:, t, :], ident[:])
+        w = sb.tile([P, NQ, 4], BF16, name="w", align_bytes=64)
+        nc.vector.tensor_tensor(
+            w[:], p_turned[:].rearrange("s t q -> s q t"), vs_cols[:].unsqueeze(1).to_broadcast([P, NQ, 4]), ALU.mult
+        )
+        quantise_values(0)
+        w_codes = sb.tile([P, NQ], U32, name="w_codes", align_bytes=64)
+        w_scales = sb.tile([P, NQ], U8, name="w_scales", align_bytes=64)
+        nc.vector.quantize_mx(
+            out=w_codes[:].bitcast(FP8X4), scales=w_scales[:], in_=w[:].rearrange("s q t -> s (q t)")
+        )
+        quantise_values(1)
+        inv_total = sb.tile([P, 1], F32, name="inv_total")
+        nc.vector.reciprocal(inv_total[:], total[:])
+
+        sums = ps.tile([P, DV], F32, name="sums")
+        nc.tensor.matmul_mx(
+            out=sums[:],
+            lhsT=w_codes[:].bitcast(FP8X4),
+            lhsT_scale=w_scales[:],
+            rhs=v_codes[:].bitcast(FP8X4),
+            rhs_scale=v_scales[:],
+            start=True,
+            stop=True,
+        )
+        y = sb.tile([P, DV], F32, name="y")
+        nc.scalar.activation(y[:], sums[:], ACT.Copy, scale=inv_total[:])
+        nc.sync.dma_start(out[0], y[:])

@@ -20,7 +20,7 @@ ALU = mybir.AluOpType
 
 P = 128
 PASSES = D // 512
-HALVES = DV // P
+H = N // 2
 VS_ROW = 8
 
 
@@ -32,10 +32,9 @@ def tile_attend_soft_cap_srtq128n512t2048_kernel(tc, q_words, q_scales, k_words,
 
         offsets = sb.tile([P, N // 16], U16, name="offsets")
         kw_pool = sb.tile([P, T], I32, name="kw_pool")
-        ks_pool = sb.tile([P, T], U8, name="ks_pool", tag="late_load")
+        ks_pool = sb.tile([P, T], U8, name="ks_pool", tag="after_ks")
         ks1 = sb.tile([P, N], U8, name="ks1", align_bytes=64)
-        v_pool = [sb.tile([P, T], F32, name="v_pool0")]
-        vs_pool = sb.tile([P, T], F32, name="vs_pool")
+        vs_pool = sb.tile([P, T], F32, name="vs_pool", tag="values1", align_bytes=64)
         qw = sb.tile([P, PASSES, NQ], I32, name="qw", align_bytes=64)
         qs = sb.tile([P, PASSES, NQ], U8, name="qs", align_bytes=64)
         ident = sb.tile([P, P], F32, name="ident")
@@ -43,124 +42,151 @@ def tile_attend_soft_cap_srtq128n512t2048_kernel(tc, q_words, q_scales, k_words,
         warm = sb.tile([P, 1], F32, name="warm")
 
         nc.vector.memset(ks_pool[:].bitcast(I32), 0)
-        nc.vector.memset(warm_in[:], 0.0)
-        nc.vector.memset(ks1[:].bitcast(I32), 0)
         nc.vector.memset(vs_pool[:], 0.0)
-        nc.gpsimd.memset(qs[:].bitcast(I32), 0)
+        nc.vector.memset(warm_in[:], 0.0)
+        nc.vector.memset(qs[:].bitcast(I32), 0)
+        nc.vector.memset(ks1[:].bitcast(I32), 0)
+        make_identity(nc, ident[:])
 
         nc.sync.dma_start(offsets[:], offs)
-        nc.sync.dma_start(kw_pool[:], k_words[0].rearrange("g t b -> g (t b)").bitcast(I32))
         nc.sync.dma_start(qw[:], q_words[0].rearrange("o g q r -> g o (q r)").bitcast(I32))
-        nc.sync.dma_start(v_pool[0][:], vT[0:P, :])
         ks_rows = k_scales.rearrange("o (quad r) t -> r quad o t", r=4)
         for r in range(4):
-            nc.scalar.dma_start(ks_pool[r:P:16, :].bitcast(I32), ks_rows[r].bitcast(I32))
+            nc.sync.dma_start(ks_pool[r:P:16, :].bitcast(I32), ks_rows[r].bitcast(I32))
+        nc.sync.dma_start(vs_pool[VS_ROW : VS_ROW + 1, :], vs[0:1, :])
+        nc.sync.dma_start(kw_pool[:], k_words[0].rearrange("g t b -> g (t b)").bitcast(I32))
         nc.scalar.activation(warm[:], warm_in[:], ACT.Exp)
-        nc.scalar.dma_start(vs_pool[VS_ROW : VS_ROW + 1, :], vs[0:1, :])
         for quad in range(4):
-            nc.gpsimd.dma_start(
+            nc.sync.dma_start(
                 qs[32 * quad : 32 * quad + 4, :, :].bitcast(I32),
                 q_scales[0][:, 4 * quad : 4 * quad + 4, :].rearrange("o f q -> f o q").bitcast(I32),
             )
-        make_identity(nc, ident[:])
+        v_pool = [sb.tile([P, T], F32, name="v_pool0", tag="values0", align_bytes=64)]
+        nc.sync.dma_start(v_pool[0][:], vT[0:P, :])
 
         ks0 = sb.tile([P, N], U8, name="ks0", align_bytes=64)
         nc.vector.tensor_copy(ks0[:], ks_pool[:].indirect(offsets[:]))
         nc.scalar.dma_start(ks1[0 : P - 16, :].bitcast(I32), ks0[16:P, :].bitcast(I32))
         ks = [ks0, ks1]
-        v_pool.append(sb.tile([P, T], F32, name="v_pool1", tag="late_load"))
+        vs_picked = sb.tile([P, N], F32, name="vs_picked", tag="after_ks")
+        nc.vector.tensor_copy(vs_picked[:], vs_pool[:].indirect(offsets[:]))
+        v_pool.append(sb.tile([P, T], F32, name="v_pool1", tag="values1", align_bytes=64))
         nc.sync.dma_start(v_pool[1][:], vT[P : 2 * P, :])
-        kw_pairs = sb.tile([P, N], U32, name="kw_pairs", tag="after_parting")
-        nc.vector.tensor_copy(kw_pairs[:], kw_pool[:].bitcast(U32).indirect(offsets[:]))
-        kw = sb.tile([P, PASSES, 2 * N], U8, name="kw", align_bytes=64)
-        nc.vector.tensor_copy(kw[:].bitcast(U16), kw_pairs[:].bitcast(U16).rearrange("p (n o) -> p o n", o=PASSES))
+        vs_turned = ps.tile([P, 4, P], F32, name="vs_turned")
+        for t in range(4):
+            nc.tensor.transpose(vs_turned[:, t, :], vs_picked[:, t:N:4], ident[:])
+        vs_cols = sb.tile([P, 4], F32, name="vs_cols", tag="after_mult", align_bytes=64)
+        nc.scalar.copy(vs_cols[:], vs_turned[:, :, VS_ROW])
 
-        scores = ps.tile([P, N], F32, name="scores")
-        for o in range(PASSES):
-            nc.tensor.matmul_mx(
-                out=scores[:],
-                lhsT=qw[:, o, :].bitcast(FP8X4),
-                lhsT_scale=qs[:, o, :],
-                rhs=kw[:, o, :].bitcast(FP4X4),
-                rhs_scale=ks[o][:],
-                start=(o == 0),
-                stop=(o == PASSES - 1),
+        kw_pairs = sb.tile([P, 2, H], U32, name="kw_pairs", tag="parted0")
+        for a in range(2):
+            nc.vector.tensor_copy(
+                kw_pairs[:, a, :], kw_pool[:].bitcast(U32).indirect(offsets[:, a * H // 16 : (a + 1) * H // 16])
             )
+        scores = []
+        for a in range(2):
+            kw = sb.tile([P, PASSES, 2 * H], U8, name="kw%d" % a, align_bytes=64)
+            nc.vector.tensor_copy(
+                kw[:].bitcast(U16), kw_pairs[:, a, :].bitcast(U16).rearrange("p (n o) -> p o n", o=PASSES)
+            )
+            scores.append(ps.tile([P, H], F32, name="scores%d" % a))
+            for g in range(H // P):
+                for o in range(PASSES):
+                    nc.tensor.matmul_mx(
+                        out=scores[a][:, g * P : (g + 1) * P],
+                        lhsT=qw[:, o, :].bitcast(FP8X4),
+                        lhsT_scale=qs[:, o, :],
+                        rhs=kw[:, o, 2 * g * P : 2 * (g + 1) * P].bitcast(FP4X4),
+                        rhs_scale=ks[o][:, a * H + g * P : a * H + (g + 1) * P],
+                        start=(o == 0),
+                        stop=(o == PASSES - 1),
+                    )
 
-        v_grouped = sb.tile([P, DV, 4], BF16, name="v_grouped", align_bytes=64)
-        v_codes = sb.tile([P, DV], U32, name="v_codes", align_bytes=64)
-        v_scales = sb.tile([P, DV], U8, name="v_scales", align_bytes=64)
-
-        def turn_values(h):
-            picked = sb.tile([P, N], BF16, name="v_picked%d" % h, tag=("v_picked", "after_max")[h])
+        def turn_values(h, tag):
+            picked = sb.tile([P, N], BF16, name="v_picked%d" % h, tag=tag)
             nc.vector.tensor_copy(picked[:], v_pool[h][:].indirect(offsets[:]))
             pairs = picked[:].bitcast(F32)
             turned = ps.tile([P, 2, P], F32, name="v_turned%d" % h)
             for u in range(2):
                 nc.tensor.transpose(turned[:, u, :], pairs[:, u : N // 2 : 2], ident[:])
-            nc.scalar.copy(v_grouped[:, h * P : (h + 1) * P, :].bitcast(F32), turned[:].rearrange("p u e -> p e u"))
+            return turned
 
-        def quantise_values(h):
-            cols = slice(h * P, (h + 1) * P)
+        def group_values(h, turned, tag):
+            grouped = sb.tile([P, P, 4], BF16, name="v_grouped%d" % h, tag=tag, align_bytes=64)
+            nc.scalar.copy(grouped[:].bitcast(F32), turned[:].rearrange("p u e -> p e u"))
+            return grouped
+
+        def quantise(name, grouped, tag):
+            codes = sb.tile([P, P], U32, name=name + "_codes", tag=tag, align_bytes=64)
+            scales = sb.tile([P, P], U8, name=name + "_scales", align_bytes=64)
             nc.vector.quantize_mx(
-                out=v_codes[:, cols].bitcast(FP8X4),
-                scales=v_scales[:, cols],
-                in_=v_grouped[:, cols, :].rearrange("p e t -> p (e t)"),
+                out=codes[:].bitcast(FP8X4), scales=scales[:], in_=grouped[:].rearrange("p e t -> p (e t)")
+            )
+            return codes, scales
+
+        capped = []
+        for a in range(2):
+            capped.append(sb.tile([P, 4, H // 4], F32, name="capped%d" % a, tag="capped%d" % a))
+            nc.scalar.activation(
+                capped[a][:], scores[a][:].rearrange("q (s t) -> q t s", t=4), ACT.Tanh, scale=1.0 / CAP
             )
 
-        capped = sb.tile([P, 4, P], F32, name="capped", tag="after_max")
-        nc.scalar.activation(capped[:], scores[:].rearrange("q (s t) -> q t s", t=4), ACT.Tanh, scale=1.0 / CAP)
+        v_turned = [turn_values(0, "parted0")]
 
-        vs_picked = sb.tile([P, N], F32, name="vs_picked", tag="after_parting")
-        nc.vector.tensor_copy(vs_picked[:], vs_pool[:].indirect(offsets[:]))
-        vs_turned = ps.tile([P, 4, P], F32, name="vs_turned")
-        for t in range(4):
-            nc.tensor.transpose(vs_turned[:, t, :], vs_picked[:, t:N:4], ident[:])
-        vs_cols = sb.tile([P, 4], F32, name="vs_cols")
-        nc.scalar.copy(vs_cols[:], vs_turned[:, :, VS_ROW])
-
-        turn_values(0)
-
-        scaled = sb.tile([P, N], F32, name="scaled")
-        neg_max = sb.tile([P, 1], F32, name="neg_max")
-        nc.vector.tensor_scalar(
-            scaled[:], capped[:].rearrange("q t s -> q (t s)"), -CAP, None, ALU.mult, ALU.min, accum_out=neg_max[:]
-        )
-        p = sb.tile([P, 4, P], F32, name="p")
-        total = sb.tile([P, 1], F32, name="total")
-        nc.scalar.activation(
-            p[:].rearrange("q t s -> q (t s)"), scaled[:], ACT.Exp, bias=neg_max[:], scale=-1.0, accum_out=total[:]
-        )
-
-        turn_values(1)
-
+        scaled = sb.tile([P, 4, P], F32, name="scaled", tag="values0", align_bytes=64)
+        neg_max = []
+        for a in range(2):
+            neg_max.append(sb.tile([P, 1], F32, name="neg_max%d" % a))
+            nc.vector.tensor_scalar(
+                scaled[:, :, a * H // 4 : (a + 1) * H // 4],
+                capped[a][:],
+                -CAP,
+                neg_max[0][:] if a else None,
+                ALU.mult,
+                ALU.min,
+                accum_out=neg_max[a][:],
+            )
         p_turned = ps.tile([P, 4, P], F32, name="p_turned")
-        for t in range(4):
-            nc.tensor.transpose(p_turned[:, t, :], p[:, t, :], ident[:])
-        w = sb.tile([P, NQ, 4], BF16, name="w", align_bytes=64)
+        totals = []
+        for u in range(2):
+            p = sb.tile([P, 2, P], F32, name="p%d" % u)
+            totals.append(sb.tile([P, 1], F32, name="total%d" % u))
+            nc.scalar.activation(
+                p[:], scaled[:, 2 * u : 2 * u + 2, :], ACT.Exp, bias=neg_max[1][:], scale=-1.0, accum_out=totals[u][:]
+            )
+            for t in range(2):
+                nc.tensor.transpose(p_turned[:, 2 * u + t, :], p[:, t, :], ident[:])
+
+        v_grouped = [group_values(0, v_turned[0], "values0")]
+        v_turned.append(turn_values(1, "capped1"))
+        v_grouped.append(group_values(1, v_turned[1], "grouped1"))
+
+        w = sb.tile([P, NQ, 4], BF16, name="w", tag="values1", align_bytes=64)
         nc.vector.tensor_tensor(
             w[:], p_turned[:].rearrange("s t q -> s q t"), vs_cols[:].unsqueeze(1).to_broadcast([P, NQ, 4]), ALU.mult
         )
-        quantise_values(0)
-        w_codes = sb.tile([P, NQ], U32, name="w_codes", align_bytes=64)
-        w_scales = sb.tile([P, NQ], U8, name="w_scales", align_bytes=64)
-        nc.vector.quantize_mx(
-            out=w_codes[:].bitcast(FP8X4), scales=w_scales[:], in_=w[:].rearrange("s q t -> s (q t)")
-        )
-        quantise_values(1)
+        v_mx = [quantise("v0", v_grouped[0], "after_mult")]
+        w_codes, w_scales = quantise("w", w, "w_codes")
+        v_mx.append(quantise("v1", v_grouped[1], "v1_codes"))
+        total = sb.tile([P, 1], F32, name="total", tag="values0", align_bytes=64)
+        nc.vector.tensor_tensor(total[:], totals[0][:], totals[1][:], ALU.add)
         inv_total = sb.tile([P, 1], F32, name="inv_total")
         nc.vector.reciprocal(inv_total[:], total[:])
 
-        sums = ps.tile([P, DV], F32, name="sums")
-        nc.tensor.matmul_mx(
-            out=sums[:],
-            lhsT=w_codes[:].bitcast(FP8X4),
-            lhsT_scale=w_scales[:],
-            rhs=v_codes[:].bitcast(FP8X4),
-            rhs_scale=v_scales[:],
-            start=True,
-            stop=True,
-        )
-        y = sb.tile([P, DV], F32, name="y")
-        nc.scalar.activation(y[:], sums[:], ACT.Copy, scale=inv_total[:])
-        nc.sync.dma_start(out[0], y[:])
+        for h in range(2):
+            sums = ps.tile([P, P], F32, name="sums%d" % h)
+            nc.tensor.matmul_mx(
+                out=sums[:],
+                lhsT=w_codes[:].bitcast(FP8X4),
+                lhsT_scale=w_scales[:],
+                rhs=v_mx[h][0][:].bitcast(FP8X4),
+                rhs_scale=v_mx[h][1][:],
+                start=True,
+                stop=True,
+            )
+            y = sb.tile([P, P], F32, name="y%d" % h)
+            if h == 0:
+                nc.scalar.activation(y[:], sums[:], ACT.Copy, scale=inv_total[:])
+            else:
+                nc.vector.tensor_scalar(y[:], sums[:], inv_total[:], None, ALU.mult)
+            nc.sync.dma_start(out[0][:, h * P : (h + 1) * P], y[:])

@@ -22,6 +22,8 @@ P = 128
 PASSES = D // 512
 H = N // 2
 VS_ROW = 8
+KW_SPLIT = 512
+V_SPLIT = 768
 
 
 def tile_attend_soft_cap_srtq128n512t2048_kernel(tc, q_words, q_scales, k_words, k_scales, vT, vs, offs, out):
@@ -34,40 +36,47 @@ def tile_attend_soft_cap_srtq128n512t2048_kernel(tc, q_words, q_scales, k_words,
         kw_pool = sb.tile([P, T], I32, name="kw_pool")
         ks_pool = sb.tile([P, T], U8, name="ks_pool", tag="after_ks")
         ks1 = sb.tile([P, N], U8, name="ks1", align_bytes=64)
-        vs_pool = sb.tile([P, T], F32, name="vs_pool", tag="values1", align_bytes=64)
+        vs_pool = sb.tile([P, T], F32, name="vs_pool")
         qw = sb.tile([P, PASSES, NQ], I32, name="qw", align_bytes=64)
         qs = sb.tile([P, PASSES, NQ], U8, name="qs", align_bytes=64)
         ident = sb.tile([P, P], F32, name="ident")
         warm_in = sb.tile([P, 1], F32, name="warm_in")
         warm = sb.tile([P, 1], F32, name="warm")
 
-        nc.vector.memset(ks_pool[:].bitcast(I32), 0)
-        nc.vector.memset(vs_pool[:], 0.0)
-        nc.vector.memset(warm_in[:], 0.0)
         nc.vector.memset(qs[:].bitcast(I32), 0)
+        nc.vector.memset(ks_pool[:].bitcast(I32), 0)
+        nc.vector.memset(vs_pool[:].bitcast(I32), 0)
+        nc.vector.memset(warm_in[:], 0.0)
         nc.vector.memset(ks1[:].bitcast(I32), 0)
         make_identity(nc, ident[:])
 
-        nc.sync.dma_start(offsets[:], offs)
-        nc.sync.dma_start(qw[:], q_words[0].rearrange("o g q r -> g o (q r)").bitcast(I32))
-        ks_rows = k_scales.rearrange("o (quad r) t -> r quad o t", r=4)
-        for r in range(4):
-            nc.sync.dma_start(ks_pool[r:P:16, :].bitcast(I32), ks_rows[r].bitcast(I32))
-        nc.sync.dma_start(vs_pool[VS_ROW : VS_ROW + 1, :], vs[0:1, :])
-        nc.sync.dma_start(kw_pool[:], k_words[0].rearrange("g t b -> g (t b)").bitcast(I32))
-        nc.scalar.activation(warm[:], warm_in[:], ACT.Exp)
-        for quad in range(4):
+        def load_query_scales(quad):
             nc.sync.dma_start(
                 qs[32 * quad : 32 * quad + 4, :, :].bitcast(I32),
                 q_scales[0][:, 4 * quad : 4 * quad + 4, :].rearrange("o f q -> f o q").bitcast(I32),
             )
+
+        nc.sync.dma_start(offsets[:], offs)
+        load_query_scales(0)
+        ks_rows = k_scales.rearrange("o (quad r) t -> r quad o t", r=4)
+        for r in range(4):
+            nc.sync.dma_start(ks_pool[r:P:16, :].bitcast(I32), ks_rows[r].bitcast(I32))
+        key_words = k_words[0].rearrange("g t b -> g (t b)").bitcast(I32)
+        nc.sync.dma_start(kw_pool[:, :KW_SPLIT], key_words[:, :KW_SPLIT])
+        nc.sync.dma_start(vs_pool[VS_ROW : VS_ROW + 1, :], vs[0:1, :])
+        nc.sync.dma_start(kw_pool[:, KW_SPLIT:], key_words[:, KW_SPLIT:])
+        nc.sync.dma_start(qw[:], q_words[0].rearrange("o g q r -> g o (q r)").bitcast(I32))
+        for quad in range(1, 4):
+            load_query_scales(quad)
+        nc.scalar.activation(warm[:], warm_in[:], ACT.Exp)
         v_pool = [sb.tile([P, T], F32, name="v_pool0", tag="values0", align_bytes=64)]
-        nc.sync.dma_start(v_pool[0][:], vT[0:P, :])
+        nc.sync.dma_start(v_pool[0][:, :V_SPLIT], vT[0:P, :V_SPLIT])
 
         ks0 = sb.tile([P, N], U8, name="ks0", align_bytes=64)
         nc.vector.tensor_copy(ks0[:], ks_pool[:].indirect(offsets[:]))
-        nc.scalar.dma_start(ks1[0 : P - 16, :].bitcast(I32), ks0[16:P, :].bitcast(I32))
+        nc.sync.dma_start(ks1[0 : P - 16, :].bitcast(I32), ks0[16:P, :].bitcast(I32))
         ks = [ks0, ks1]
+        nc.sync.dma_start(v_pool[0][:, V_SPLIT:], vT[0:P, V_SPLIT:])
         vs_picked = sb.tile([P, N], F32, name="vs_picked", tag="after_ks")
         nc.vector.tensor_copy(vs_picked[:], vs_pool[:].indirect(offsets[:]))
         v_pool.append(sb.tile([P, T], F32, name="v_pool1", tag="values1", align_bytes=64))

@@ -19,11 +19,14 @@ ACT = mybir.ActivationFunctionType
 ALU = mybir.AluOpType
 
 P = 128
-PASSES = D // 512
-H = N // 2
+PACK = 4
+QUADRANT = 32
+PASSES = D // (P * PACK)
+HALF = N // 2
+SECOND_PASS_SHIFT = 16
 VS_ROW = 8
-KW_SPLIT = 512
-V_SPLIT = 768
+KEY_SPLIT = 640
+VALUE_SPLIT = 1024
 
 
 def tile_attend_soft_cap_srtq128n512t2048_kernel(tc, q_words, q_scales, k_words, k_scales, vT, vs, offs, out):
@@ -33,169 +36,163 @@ def tile_attend_soft_cap_srtq128n512t2048_kernel(tc, q_words, q_scales, k_words,
         ps = ctx.enter_context(tc.psum_pool(name="ps", bufs=1))
 
         offsets = sb.tile([P, N // 16], U16, name="offsets")
-        kw_pool = sb.tile([P, T], I32, name="kw_pool")
-        ks_pool = sb.tile([P, T], U8, name="ks_pool", tag="after_ks")
-        ks1 = sb.tile([P, N], U8, name="ks1", align_bytes=64)
+        k_word_pool = sb.tile([P, T], I32, name="k_word_pool")
+        k_scale_pool = sb.tile([P, T], U8, name="k_scale_pool", tag="vs_gather_after_scale_gather")
+        k_plane1 = sb.tile([P, N], U8, name="k_plane1", align_bytes=64)
         vs_pool = sb.tile([P, T], F32, name="vs_pool")
-        qw = sb.tile([P, PASSES, NQ], I32, name="qw", align_bytes=64)
-        qs = sb.tile([P, PASSES, NQ], U8, name="qs", align_bytes=64)
+        q_codes = sb.tile([P, PASSES, NQ], I32, name="q_codes", align_bytes=64)
+        q_planes = sb.tile([P, PASSES, NQ], U8, name="q_planes", align_bytes=64)
         ident = sb.tile([P, P], F32, name="ident")
         warm_in = sb.tile([P, 1], F32, name="warm_in")
-        warm = sb.tile([P, 1], F32, name="warm")
+        warm_out = sb.tile([P, 1], F32, name="warm_out")
 
-        nc.vector.memset(qs[:].bitcast(I32), 0)
-        nc.vector.memset(ks_pool[:].bitcast(I32), 0)
+        nc.vector.memset(k_scale_pool[:].bitcast(I32), 0)
         nc.vector.memset(vs_pool[:].bitcast(I32), 0)
+        nc.vector.memset(q_planes[:].bitcast(I32), 0)
         nc.vector.memset(warm_in[:], 0.0)
-        nc.vector.memset(ks1[:].bitcast(I32), 0)
+        nc.vector.memset(k_plane1[:].bitcast(I32), 0)
         make_identity(nc, ident[:])
-
-        def load_query_scales(quad):
-            nc.sync.dma_start(
-                qs[32 * quad : 32 * quad + 4, :, :].bitcast(I32),
-                q_scales[0][:, 4 * quad : 4 * quad + 4, :].rearrange("o f q -> f o q").bitcast(I32),
-            )
+        nc.scalar.activation(warm_out[:], warm_in[:], ACT.Exp)
 
         nc.sync.dma_start(offsets[:], offs)
-        load_query_scales(0)
-        ks_rows = k_scales.rearrange("o (quad r) t -> r quad o t", r=4)
-        for r in range(4):
-            nc.sync.dma_start(ks_pool[r:P:16, :].bitcast(I32), ks_rows[r].bitcast(I32))
-        key_words = k_words[0].rearrange("g t b -> g (t b)").bitcast(I32)
-        nc.sync.dma_start(kw_pool[:, :KW_SPLIT], key_words[:, :KW_SPLIT])
+        nc.sync.dma_start(q_codes[:], q_words[0].rearrange("o g q r -> g o (q r)").bitcast(I32))
+        k_scale_rows = k_scales.rearrange("o (quad r) t -> r quad o t", r=PACK)
+        for r in range(PACK):
+            nc.sync.dma_start(k_scale_pool[r:P:SECOND_PASS_SHIFT, :].bitcast(I32), k_scale_rows[r].bitcast(I32))
+        k_word_rows = k_words[0].rearrange("g t b -> g (t b)").bitcast(I32)
+        nc.sync.dma_start(k_word_pool[:, :KEY_SPLIT], k_word_rows[:, :KEY_SPLIT])
         nc.sync.dma_start(vs_pool[VS_ROW : VS_ROW + 1, :], vs[0:1, :])
-        nc.sync.dma_start(kw_pool[:, KW_SPLIT:], key_words[:, KW_SPLIT:])
-        nc.sync.dma_start(qw[:], q_words[0].rearrange("o g q r -> g o (q r)").bitcast(I32))
-        for quad in range(1, 4):
-            load_query_scales(quad)
-        nc.scalar.activation(warm[:], warm_in[:], ACT.Exp)
-        v_pool = [sb.tile([P, T], F32, name="v_pool0", tag="values0", align_bytes=64)]
-        nc.sync.dma_start(v_pool[0][:, :V_SPLIT], vT[0:P, :V_SPLIT])
+        nc.sync.dma_start(k_word_pool[:, KEY_SPLIT:], k_word_rows[:, KEY_SPLIT:])
+        for quad in range(P // QUADRANT):
+            nc.sync.dma_start(
+                q_planes[QUADRANT * quad : QUADRANT * quad + PACK, :, :].bitcast(I32),
+                q_scales[0][:, PACK * quad : PACK * (quad + 1), :].rearrange("o f q -> f o q").bitcast(I32),
+            )
+        v_pool0 = sb.tile([P, T], F32, name="v_pool0", tag="max_copy_sum_after_first_value_gather", align_bytes=64)
+        nc.sync.dma_start(v_pool0[:, :VALUE_SPLIT], vT[0:P, :VALUE_SPLIT])
 
-        ks0 = sb.tile([P, N], U8, name="ks0", align_bytes=64)
-        nc.vector.tensor_copy(ks0[:], ks_pool[:].indirect(offsets[:]))
-        nc.sync.dma_start(ks1[0 : P - 16, :].bitcast(I32), ks0[16:P, :].bitcast(I32))
-        ks = [ks0, ks1]
-        nc.sync.dma_start(v_pool[0][:, V_SPLIT:], vT[0:P, V_SPLIT:])
-        vs_picked = sb.tile([P, N], F32, name="vs_picked", tag="after_ks")
+        k_plane0 = sb.tile([P, N], U8, name="k_plane0", align_bytes=64)
+        nc.vector.tensor_copy(k_plane0[:], k_scale_pool[:].indirect(offsets[:]))
+        nc.sync.dma_start(
+            k_plane1[0 : P - SECOND_PASS_SHIFT, :].bitcast(I32), k_plane0[SECOND_PASS_SHIFT:P, :].bitcast(I32)
+        )
+        k_planes = (k_plane0, k_plane1)
+        nc.sync.dma_start(v_pool0[:, VALUE_SPLIT:], vT[0:P, VALUE_SPLIT:])
+
+        vs_picked = sb.tile([P, N], F32, name="vs_picked", tag="vs_gather_after_scale_gather")
         nc.vector.tensor_copy(vs_picked[:], vs_pool[:].indirect(offsets[:]))
-        v_pool.append(sb.tile([P, T], F32, name="v_pool1", tag="values1", align_bytes=64))
-        nc.sync.dma_start(v_pool[1][:], vT[P : 2 * P, :])
-        vs_turned = ps.tile([P, 4, P], F32, name="vs_turned")
-        for t in range(4):
-            nc.tensor.transpose(vs_turned[:, t, :], vs_picked[:, t:N:4], ident[:])
-        vs_cols = sb.tile([P, 4], F32, name="vs_cols", tag="after_mult", align_bytes=64)
+        v_pool1 = sb.tile([P, T], F32, name="v_pool1", tag="weights_after_second_value_gather", align_bytes=64)
+        nc.sync.dma_start(v_pool1[:], vT[P : 2 * P, :])
+        vs_turned = ps.tile([P, PACK, P], F32, name="vs_turned")
+        for t in range(PACK):
+            nc.tensor.transpose(vs_turned[:, t, :], vs_picked[:, t:N:PACK], ident[:])
+        vs_cols = sb.tile([P, PACK], F32, name="vs_cols", tag="first_value_codes_after_weights", align_bytes=64)
         nc.scalar.copy(vs_cols[:], vs_turned[:, :, VS_ROW])
 
-        kw_pairs = sb.tile([P, 2, H], U32, name="kw_pairs", tag="parted0")
-        for a in range(2):
-            nc.vector.tensor_copy(
-                kw_pairs[:, a, :], kw_pool[:].bitcast(U32).indirect(offsets[:, a * H // 16 : (a + 1) * H // 16])
-            )
+        k_pairs = sb.tile([P, 2, HALF], U32, name="k_pairs", tag="first_value_gather_after_parting")
+        for half in range(2):
+            columns = slice(half * HALF // 16, (half + 1) * HALF // 16)
+            nc.vector.tensor_copy(k_pairs[:, half, :], k_word_pool[:].bitcast(U32).indirect(offsets[:, columns]))
         scores = []
-        for a in range(2):
-            kw = sb.tile([P, PASSES, 2 * H], U8, name="kw%d" % a, align_bytes=64)
+        for half in range(2):
+            k_codes = sb.tile([P, PASSES, 2 * HALF], U8, name="k_codes%d" % half, align_bytes=64)
             nc.vector.tensor_copy(
-                kw[:].bitcast(U16), kw_pairs[:, a, :].bitcast(U16).rearrange("p (n o) -> p o n", o=PASSES)
+                k_codes[:].bitcast(U16), k_pairs[:, half, :].bitcast(U16).rearrange("p (n o) -> p o n", o=PASSES)
             )
-            scores.append(ps.tile([P, H], F32, name="scores%d" % a))
-            for g in range(H // P):
+            scores.append(ps.tile([P, HALF], F32, name="scores%d" % half))
+            for first in range(0, HALF, P):
                 for o in range(PASSES):
                     nc.tensor.matmul_mx(
-                        out=scores[a][:, g * P : (g + 1) * P],
-                        lhsT=qw[:, o, :].bitcast(FP8X4),
-                        lhsT_scale=qs[:, o, :],
-                        rhs=kw[:, o, 2 * g * P : 2 * (g + 1) * P].bitcast(FP4X4),
-                        rhs_scale=ks[o][:, a * H + g * P : a * H + (g + 1) * P],
+                        out=scores[half][:, first : first + P],
+                        lhsT=q_codes[:, o, :].bitcast(FP8X4),
+                        lhsT_scale=q_planes[:, o, :],
+                        rhs=k_codes[:, o, 2 * first : 2 * (first + P)].bitcast(FP4X4),
+                        rhs_scale=k_planes[o][:, half * HALF + first : half * HALF + first + P],
                         start=(o == 0),
                         stop=(o == PASSES - 1),
                     )
 
-        def turn_values(h, tag):
-            picked = sb.tile([P, N], BF16, name="v_picked%d" % h, tag=tag)
-            nc.vector.tensor_copy(picked[:], v_pool[h][:].indirect(offsets[:]))
-            pairs = picked[:].bitcast(F32)
-            turned = ps.tile([P, 2, P], F32, name="v_turned%d" % h)
+        def turn_values(name, pool, tag):
+            picked = sb.tile([P, N], BF16, name=name + "_picked", tag=tag)
+            nc.vector.tensor_copy(picked[:], pool[:].indirect(offsets[:]))
+            slot_pairs = picked[:].bitcast(F32)
+            turned = ps.tile([P, 2, P], F32, name=name + "_turned")
             for u in range(2):
-                nc.tensor.transpose(turned[:, u, :], pairs[:, u : N // 2 : 2], ident[:])
+                nc.tensor.transpose(turned[:, u, :], slot_pairs[:, u : N // 2 : 2], ident[:])
             return turned
 
-        def group_values(h, turned, tag):
-            grouped = sb.tile([P, P, 4], BF16, name="v_grouped%d" % h, tag=tag, align_bytes=64)
-            nc.scalar.copy(grouped[:].bitcast(F32), turned[:].rearrange("p u e -> p e u"))
+        def group_values(name, turned, tag):
+            grouped = sb.tile([P, P, PACK], BF16, name=name + "_grouped", tag=tag, align_bytes=64)
+            nc.scalar.copy(grouped[:].bitcast(F32), turned[:].rearrange("s u e -> s e u"))
             return grouped
 
         def quantise(name, grouped, tag):
             codes = sb.tile([P, P], U32, name=name + "_codes", tag=tag, align_bytes=64)
-            scales = sb.tile([P, P], U8, name=name + "_scales", align_bytes=64)
+            plane = sb.tile([P, P], U8, name=name + "_plane", align_bytes=64)
             nc.vector.quantize_mx(
-                out=codes[:].bitcast(FP8X4), scales=scales[:], in_=grouped[:].rearrange("p e t -> p (e t)")
+                out=codes[:].bitcast(FP8X4), scales=plane[:], in_=grouped[:].rearrange("s c t -> s (c t)")
             )
-            return codes, scales
+            return codes, plane
 
-        capped = []
-        for a in range(2):
-            capped.append(sb.tile([P, 4, H // 4], F32, name="capped%d" % a, tag="capped%d" % a))
+        capped = sb.tile([P, PACK, P], F32, name="capped", tag="second_value_gather_after_max")
+        for half in range(2):
             nc.scalar.activation(
-                capped[a][:], scores[a][:].rearrange("q (s t) -> q t s", t=4), ACT.Tanh, scale=1.0 / CAP
+                capped[:, :, half * HALF // PACK : (half + 1) * HALF // PACK],
+                scores[half][:].rearrange("q (s t) -> q t s", t=PACK),
+                ACT.Tanh,
+                scale=1.0 / CAP,
             )
 
-        v_turned = [turn_values(0, "parted0")]
+        v0_turned = turn_values("v0", v_pool0, "first_value_gather_after_parting")
 
-        scaled = sb.tile([P, 4, P], F32, name="scaled", tag="values0", align_bytes=64)
-        neg_max = []
-        for a in range(2):
-            neg_max.append(sb.tile([P, 1], F32, name="neg_max%d" % a))
-            nc.vector.tensor_scalar(
-                scaled[:, :, a * H // 4 : (a + 1) * H // 4],
-                capped[a][:],
-                -CAP,
-                neg_max[0][:] if a else None,
-                ALU.mult,
-                ALU.min,
-                accum_out=neg_max[a][:],
-            )
-        p_turned = ps.tile([P, 4, P], F32, name="p_turned")
-        totals = []
+        neg_c = sb.tile([P, PACK, P], F32, name="neg_c", tag="max_copy_sum_after_first_value_gather", align_bytes=64)
+        neg_m = sb.tile([P, 1], F32, name="neg_m")
+        nc.vector.tensor_scalar(neg_c[:], capped[:], -CAP, None, ALU.mult, ALU.min, accum_out=neg_m[:])
+
+        p_turned = ps.tile([P, PACK, NQ], F32, name="p_turned")
+        part_sums = []
         for u in range(2):
             p = sb.tile([P, 2, P], F32, name="p%d" % u)
-            totals.append(sb.tile([P, 1], F32, name="total%d" % u))
+            part_sums.append(sb.tile([P, 1], F32, name="part_sum%d" % u))
             nc.scalar.activation(
-                p[:], scaled[:, 2 * u : 2 * u + 2, :], ACT.Exp, bias=neg_max[1][:], scale=-1.0, accum_out=totals[u][:]
+                p[:], neg_c[:, 2 * u : 2 * u + 2, :], ACT.Exp, bias=neg_m[:], scale=-1.0, accum_out=part_sums[u][:]
             )
             for t in range(2):
                 nc.tensor.transpose(p_turned[:, 2 * u + t, :], p[:, t, :], ident[:])
 
-        v_grouped = [group_values(0, v_turned[0], "values0")]
-        v_turned.append(turn_values(1, "capped1"))
-        v_grouped.append(group_values(1, v_turned[1], "grouped1"))
+        v0_grouped = group_values("v0", v0_turned, "max_copy_sum_after_first_value_gather")
+        v1_turned = turn_values("v1", v_pool1, "second_value_gather_after_max")
+        v1_grouped = group_values("v1", v1_turned, "v1_grouped")
 
-        w = sb.tile([P, NQ, 4], BF16, name="w", tag="values1", align_bytes=64)
+        w = sb.tile([P, NQ, PACK], BF16, name="w", tag="weights_after_second_value_gather", align_bytes=64)
         nc.vector.tensor_tensor(
-            w[:], p_turned[:].rearrange("s t q -> s q t"), vs_cols[:].unsqueeze(1).to_broadcast([P, NQ, 4]), ALU.mult
+            w[:],
+            p_turned[:].rearrange("s t q -> s q t"),
+            vs_cols[:].unsqueeze(1).to_broadcast([P, NQ, PACK]),
+            ALU.mult,
         )
-        v_mx = [quantise("v0", v_grouped[0], "after_mult")]
-        w_codes, w_scales = quantise("w", w, "w_codes")
-        v_mx.append(quantise("v1", v_grouped[1], "v1_codes"))
-        total = sb.tile([P, 1], F32, name="total", tag="values0", align_bytes=64)
-        nc.vector.tensor_tensor(total[:], totals[0][:], totals[1][:], ALU.add)
-        inv_total = sb.tile([P, 1], F32, name="inv_total")
-        nc.vector.reciprocal(inv_total[:], total[:])
+        v0_mx = quantise("v0", v0_grouped, "first_value_codes_after_weights")
+        w_codes, w_plane = quantise("w", w, "w_codes")
+        v1_mx = quantise("v1", v1_grouped, "v1_codes")
+        row_sum = sb.tile([P, 1], F32, name="row_sum", tag="max_copy_sum_after_first_value_gather", align_bytes=64)
+        nc.vector.tensor_tensor(row_sum[:], part_sums[0][:], part_sums[1][:], ALU.add)
+        inv_row_sum = sb.tile([P, 1], F32, name="inv_row_sum")
+        nc.vector.reciprocal(inv_row_sum[:], row_sum[:])
 
-        for h in range(2):
+        for h, (v_codes, v_plane) in enumerate((v0_mx, v1_mx)):
             sums = ps.tile([P, P], F32, name="sums%d" % h)
             nc.tensor.matmul_mx(
                 out=sums[:],
                 lhsT=w_codes[:].bitcast(FP8X4),
-                lhsT_scale=w_scales[:],
-                rhs=v_mx[h][0][:].bitcast(FP8X4),
-                rhs_scale=v_mx[h][1][:],
+                lhsT_scale=w_plane[:],
+                rhs=v_codes[:].bitcast(FP8X4),
+                rhs_scale=v_plane[:],
                 start=True,
                 stop=True,
             )
             y = sb.tile([P, P], F32, name="y%d" % h)
             if h == 0:
-                nc.scalar.activation(y[:], sums[:], ACT.Copy, scale=inv_total[:])
+                nc.scalar.activation(y[:], sums[:], ACT.Copy, scale=inv_row_sum[:])
             else:
-                nc.vector.tensor_scalar(y[:], sums[:], inv_total[:], None, ALU.mult)
+                nc.vector.tensor_scalar(y[:], sums[:], inv_row_sum[:], None, ALU.mult)
             nc.sync.dma_start(out[0][:, h * P : (h + 1) * P], y[:])

@@ -24,9 +24,8 @@ QUADRANT = 32
 PASSES = D // (P * PACK)
 HALF = N // 2
 SECOND_PASS_SHIFT = 16
-VS_ROW = 8
-KEY_SPLIT = 640
-VALUE_SPLIT = 1024
+VS_ROW = P - 1
+VALUE_SPLIT = 1536
 
 
 def tile_attend_soft_cap_srtq128n512t2048_kernel(tc, q_words, q_scales, k_words, k_scales, vT, vs, offs, out):
@@ -37,7 +36,7 @@ def tile_attend_soft_cap_srtq128n512t2048_kernel(tc, q_words, q_scales, k_words,
 
         offsets = sb.tile([P, N // 16], U16, name="offsets")
         k_word_pool = sb.tile([P, T], I32, name="k_word_pool")
-        k_scale_pool = sb.tile([P, T], U8, name="k_scale_pool", tag="vs_gather_after_scale_gather")
+        k_scale_pool = sb.tile([P, T], U8, name="k_scale_pool")
         k_plane1 = sb.tile([P, N], U8, name="k_plane1", align_bytes=64)
         vs_pool = sb.tile([P, T], F32, name="vs_pool")
         q_codes = sb.tile([P, PASSES, NQ], I32, name="q_codes", align_bytes=64)
@@ -47,22 +46,21 @@ def tile_attend_soft_cap_srtq128n512t2048_kernel(tc, q_words, q_scales, k_words,
         warm_out = sb.tile([P, 1], F32, name="warm_out")
 
         nc.vector.memset(k_scale_pool[:].bitcast(I32), 0)
-        nc.vector.memset(vs_pool[:].bitcast(I32), 0)
-        nc.vector.memset(q_planes[:].bitcast(I32), 0)
         nc.vector.memset(warm_in[:], 0.0)
+        nc.vector.memset(q_planes[:].bitcast(I32), 0)
         nc.vector.memset(k_plane1[:].bitcast(I32), 0)
+        nc.vector.memset(vs_pool[0:VS_ROW, :], 0.0)
         make_identity(nc, ident[:])
         nc.scalar.activation(warm_out[:], warm_in[:], ACT.Exp)
 
         nc.sync.dma_start(offsets[:], offs)
+        nc.sync.dma_start(vs_pool[VS_ROW : VS_ROW + 1, :], vs[0:1, :])
         nc.sync.dma_start(q_codes[:], q_words[0].rearrange("o g q r -> g o (q r)").bitcast(I32))
         k_scale_rows = k_scales.rearrange("o (quad r) t -> r quad o t", r=PACK)
         for r in range(PACK):
             nc.sync.dma_start(k_scale_pool[r:P:SECOND_PASS_SHIFT, :].bitcast(I32), k_scale_rows[r].bitcast(I32))
         k_word_rows = k_words[0].rearrange("g t b -> g (t b)").bitcast(I32)
-        nc.sync.dma_start(k_word_pool[:, :KEY_SPLIT], k_word_rows[:, :KEY_SPLIT])
-        nc.sync.dma_start(vs_pool[VS_ROW : VS_ROW + 1, :], vs[0:1, :])
-        nc.sync.dma_start(k_word_pool[:, KEY_SPLIT:], k_word_rows[:, KEY_SPLIT:])
+        nc.sync.dma_start(k_word_pool[:], k_word_rows)
         for quad in range(P // QUADRANT):
             nc.sync.dma_start(
                 q_planes[QUADRANT * quad : QUADRANT * quad + PACK, :, :].bitcast(I32),
@@ -70,6 +68,9 @@ def tile_attend_soft_cap_srtq128n512t2048_kernel(tc, q_words, q_scales, k_words,
             )
         v_pool0 = sb.tile([P, T], F32, name="v_pool0", tag="max_copy_sum_after_first_value_gather", align_bytes=64)
         nc.sync.dma_start(v_pool0[:, :VALUE_SPLIT], vT[0:P, :VALUE_SPLIT])
+
+        vs_picked = sb.tile([P, N], F32, name="vs_picked")
+        nc.vector.tensor_copy(vs_picked[:], vs_pool[:].indirect(offsets[:]))
 
         k_plane0 = sb.tile([P, N], U8, name="k_plane0", align_bytes=64)
         nc.vector.tensor_copy(k_plane0[:], k_scale_pool[:].indirect(offsets[:]))
@@ -79,8 +80,6 @@ def tile_attend_soft_cap_srtq128n512t2048_kernel(tc, q_words, q_scales, k_words,
         k_planes = (k_plane0, k_plane1)
         nc.sync.dma_start(v_pool0[:, VALUE_SPLIT:], vT[0:P, VALUE_SPLIT:])
 
-        vs_picked = sb.tile([P, N], F32, name="vs_picked", tag="vs_gather_after_scale_gather")
-        nc.vector.tensor_copy(vs_picked[:], vs_pool[:].indirect(offsets[:]))
         v_pool1 = sb.tile([P, T], F32, name="v_pool1", tag="weights_after_second_value_gather", align_bytes=64)
         nc.sync.dma_start(v_pool1[:], vT[P : 2 * P, :])
         vs_turned = ps.tile([P, PACK, P], F32, name="vs_turned")

@@ -25,7 +25,6 @@ PASSES = D // (P * PACK)
 HALF = N // 2
 SECOND_PASS_SHIFT = 16
 VS_ROW = P - 1
-VALUE_SPLIT = 1536
 
 
 def tile_attend_soft_cap_srtq128n512t2048_kernel(tc, q_words, q_scales, k_words, k_scales, vT, vs, offs, out):
@@ -36,7 +35,7 @@ def tile_attend_soft_cap_srtq128n512t2048_kernel(tc, q_words, q_scales, k_words,
 
         offsets = sb.tile([P, N // 16], U16, name="offsets")
         k_word_pool = sb.tile([P, T], I32, name="k_word_pool")
-        k_scale_pool = sb.tile([P, T], U8, name="k_scale_pool")
+        k_scale_pool = sb.tile([P, T], U8, name="k_scale_pool", tag="weights_after_second_value_gather", align_bytes=64)
         k_plane1 = sb.tile([P, N], U8, name="k_plane1", align_bytes=64)
         vs_pool = sb.tile([P, T], F32, name="vs_pool")
         q_codes = sb.tile([P, PASSES, NQ], I32, name="q_codes", align_bytes=64)
@@ -56,29 +55,30 @@ def tile_attend_soft_cap_srtq128n512t2048_kernel(tc, q_words, q_scales, k_words,
         nc.sync.dma_start(offsets[:], offs)
         nc.sync.dma_start(vs_pool[VS_ROW : VS_ROW + 1, :], vs[0:1, :])
         nc.sync.dma_start(q_codes[:], q_words[0].rearrange("o g q r -> g o (q r)").bitcast(I32))
+        k_word_rows = k_words[0].rearrange("g t b -> g (t b)").bitcast(I32)
         k_scale_rows = k_scales.rearrange("o (quad r) t -> r quad o t", r=PACK)
         for r in range(PACK):
             nc.sync.dma_start(k_scale_pool[r:P:SECOND_PASS_SHIFT, :].bitcast(I32), k_scale_rows[r].bitcast(I32))
-        k_word_rows = k_words[0].rearrange("g t b -> g (t b)").bitcast(I32)
         nc.sync.dma_start(k_word_pool[:], k_word_rows)
         for quad in range(P // QUADRANT):
             nc.sync.dma_start(
                 q_planes[QUADRANT * quad : QUADRANT * quad + PACK, :, :].bitcast(I32),
                 q_scales[0][:, PACK * quad : PACK * (quad + 1), :].rearrange("o f q -> f o q").bitcast(I32),
             )
-        v_pool0 = sb.tile([P, T], F32, name="v_pool0", tag="max_copy_sum_after_first_value_gather", align_bytes=64)
-        nc.sync.dma_start(v_pool0[:, :VALUE_SPLIT], vT[0:P, :VALUE_SPLIT])
+        v_pool0 = sb.tile([P, T], F32, name="v_pool0", tag="max_after_first_value_gather", align_bytes=64)
+        nc.sync.dma_start(v_pool0[:], vT[0:P, :])
 
         vs_picked = sb.tile([P, N], F32, name="vs_picked")
         nc.vector.tensor_copy(vs_picked[:], vs_pool[:].indirect(offsets[:]))
 
         k_plane0 = sb.tile([P, N], U8, name="k_plane0", align_bytes=64)
         nc.vector.tensor_copy(k_plane0[:], k_scale_pool[:].indirect(offsets[:]))
-        nc.sync.dma_start(
-            k_plane1[0 : P - SECOND_PASS_SHIFT, :].bitcast(I32), k_plane0[SECOND_PASS_SHIFT:P, :].bitcast(I32)
-        )
+        for first, count in ((0, 64), (64, 32), (96, 16)):
+            nc.sync.dma_start(
+                k_plane1[first : first + count, :].bitcast(I32),
+                k_plane0[SECOND_PASS_SHIFT + first : SECOND_PASS_SHIFT + first + count, :].bitcast(I32),
+            )
         k_planes = (k_plane0, k_plane1)
-        nc.sync.dma_start(v_pool0[:, VALUE_SPLIT:], vT[0:P, VALUE_SPLIT:])
 
         v_pool1 = sb.tile([P, T], F32, name="v_pool1", tag="weights_after_second_value_gather", align_bytes=64)
         nc.sync.dma_start(v_pool1[:], vT[P : 2 * P, :])
@@ -92,30 +92,31 @@ def tile_attend_soft_cap_srtq128n512t2048_kernel(tc, q_words, q_scales, k_words,
         for half in range(2):
             columns = slice(half * HALF // 16, (half + 1) * HALF // 16)
             nc.vector.tensor_copy(k_pairs[:, half, :], k_word_pool[:].bitcast(U32).indirect(offsets[:, columns]))
-        scores = []
+        k_codes = []
         for half in range(2):
-            k_codes = sb.tile([P, PASSES, 2 * HALF], U8, name="k_codes%d" % half, align_bytes=64)
+            k_codes.append(sb.tile([P, PASSES, 2 * HALF], U8, name="k_codes%d" % half, align_bytes=64))
             nc.vector.tensor_copy(
-                k_codes[:].bitcast(U16), k_pairs[:, half, :].bitcast(U16).rearrange("p (n o) -> p o n", o=PASSES)
+                k_codes[half][:].bitcast(U16), k_pairs[:, half, :].bitcast(U16).rearrange("p (n o) -> p o n", o=PASSES)
             )
-            scores.append(ps.tile([P, HALF], F32, name="scores%d" % half))
-            for first in range(0, HALF, P):
-                for o in range(PASSES):
-                    nc.tensor.matmul_mx(
-                        out=scores[half][:, first : first + P],
-                        lhsT=q_codes[:, o, :].bitcast(FP8X4),
-                        lhsT_scale=q_planes[:, o, :],
-                        rhs=k_codes[:, o, 2 * first : 2 * (first + P)].bitcast(FP4X4),
-                        rhs_scale=k_planes[o][:, half * HALF + first : half * HALF + first + P],
-                        start=(o == 0),
-                        stop=(o == PASSES - 1),
-                    )
+        scores = [ps.tile([P, P], F32, name="scores%d" % j, tag="bank%d" % j) for j in range(N // P)]
+        for o in range(PASSES):
+            for j in range(N // P):
+                half, first = divmod(j * P, HALF)
+                nc.tensor.matmul_mx(
+                    out=scores[j][:],
+                    lhsT=q_codes[:, o, :].bitcast(FP8X4),
+                    lhsT_scale=q_planes[:, o, :],
+                    rhs=k_codes[half][:, o, 2 * first : 2 * (first + P)].bitcast(FP4X4),
+                    rhs_scale=k_planes[o][:, j * P : (j + 1) * P],
+                    start=(o == 0),
+                    stop=(o == PASSES - 1),
+                )
 
-        def turn_values(name, pool, tag):
+        def turn_values(name, pool, tag, bank):
             picked = sb.tile([P, N], BF16, name=name + "_picked", tag=tag)
             nc.vector.tensor_copy(picked[:], pool[:].indirect(offsets[:]))
             slot_pairs = picked[:].bitcast(F32)
-            turned = ps.tile([P, 2, P], F32, name=name + "_turned")
+            turned = ps.tile([P, 2, P], F32, name=name + "_turned", tag=bank)
             for u in range(2):
                 nc.tensor.transpose(turned[:, u, :], slot_pairs[:, u : N // 2 : 2], ident[:])
             return turned
@@ -134,17 +135,17 @@ def tile_attend_soft_cap_srtq128n512t2048_kernel(tc, q_words, q_scales, k_words,
             return codes, plane
 
         capped = sb.tile([P, PACK, P], F32, name="capped", tag="second_value_gather_after_max")
-        for half in range(2):
+        for j in range(N // P):
             nc.scalar.activation(
-                capped[:, :, half * HALF // PACK : (half + 1) * HALF // PACK],
-                scores[half][:].rearrange("q (s t) -> q t s", t=PACK),
+                capped[:, :, j * P // PACK : (j + 1) * P // PACK],
+                scores[j][:].rearrange("q (s t) -> q t s", t=PACK),
                 ACT.Tanh,
                 scale=1.0 / CAP,
             )
 
-        v0_turned = turn_values("v0", v_pool0, "first_value_gather_after_parting")
+        v0_turned = turn_values("v0", v_pool0, "first_value_gather_after_parting", "bank3")
 
-        neg_c = sb.tile([P, PACK, P], F32, name="neg_c", tag="max_copy_sum_after_first_value_gather", align_bytes=64)
+        neg_c = sb.tile([P, PACK, P], F32, name="neg_c", tag="max_after_first_value_gather", align_bytes=64)
         neg_m = sb.tile([P, 1], F32, name="neg_m")
         nc.vector.tensor_scalar(neg_c[:], capped[:], -CAP, None, ALU.mult, ALU.min, accum_out=neg_m[:])
 
@@ -159,8 +160,10 @@ def tile_attend_soft_cap_srtq128n512t2048_kernel(tc, q_words, q_scales, k_words,
             for t in range(2):
                 nc.tensor.transpose(p_turned[:, 2 * u + t, :], p[:, t, :], ident[:])
 
-        v0_grouped = group_values("v0", v0_turned, "max_copy_sum_after_first_value_gather")
-        v1_turned = turn_values("v1", v_pool1, "second_value_gather_after_max")
+        row_sum = sb.tile([P, 1], F32, name="row_sum")
+        nc.scalar.activation(row_sum[:], part_sums[0][:], ACT.Identity, bias=part_sums[1][:])
+        v0_grouped = group_values("v0", v0_turned, "max_after_first_value_gather")
+        v1_turned = turn_values("v1", v_pool1, "second_value_gather_after_max", "bank2")
         v1_grouped = group_values("v1", v1_turned, "v1_grouped")
 
         w = sb.tile([P, NQ, PACK], BF16, name="w", tag="weights_after_second_value_gather", align_bytes=64)
@@ -171,15 +174,13 @@ def tile_attend_soft_cap_srtq128n512t2048_kernel(tc, q_words, q_scales, k_words,
             ALU.mult,
         )
         v0_mx = quantise("v0", v0_grouped, "first_value_codes_after_weights")
+        inv_row_sum = sb.tile([P, 1], F32, name="inv_row_sum", tag="max_after_first_value_gather", align_bytes=64)
+        nc.vector.reciprocal(inv_row_sum[:], row_sum[:])
         w_codes, w_plane = quantise("w", w, "w_codes")
         v1_mx = quantise("v1", v1_grouped, "v1_codes")
-        row_sum = sb.tile([P, 1], F32, name="row_sum", tag="max_copy_sum_after_first_value_gather", align_bytes=64)
-        nc.vector.tensor_tensor(row_sum[:], part_sums[0][:], part_sums[1][:], ALU.add)
-        inv_row_sum = sb.tile([P, 1], F32, name="inv_row_sum")
-        nc.vector.reciprocal(inv_row_sum[:], row_sum[:])
 
         for h, (v_codes, v_plane) in enumerate((v0_mx, v1_mx)):
-            sums = ps.tile([P, P], F32, name="sums%d" % h)
+            sums = ps.tile([P, P], F32, name="sums%d" % h, tag="bank%d" % h)
             nc.tensor.matmul_mx(
                 out=sums[:],
                 lhsT=w_codes[:].bitcast(FP8X4),

@@ -23,8 +23,9 @@ PACK = 4
 QUADRANT = 32
 PASSES = D // (P * PACK)
 HALF = N // 2
-SECOND_PASS_SHIFT = 16
 VS_ROW = P - 1
+KEY_SPLIT = 384
+VALUE_SPLIT = 768
 
 
 def tile_attend_soft_cap_srtq128n512t2048_kernel(tc, q_words, q_scales, k_words, k_scales, vT, vs, offs, out):
@@ -35,60 +36,52 @@ def tile_attend_soft_cap_srtq128n512t2048_kernel(tc, q_words, q_scales, k_words,
 
         offsets = sb.tile([P, N // 16], U16, name="offsets")
         k_word_pool = sb.tile([P, T], I32, name="k_word_pool")
-        k_scale_pool = sb.tile([P, T], U8, name="k_scale_pool", tag="weights_after_second_value_gather", align_bytes=64)
-        k_plane1 = sb.tile([P, N], U8, name="k_plane1", align_bytes=64)
+        k_scale_pool = sb.tile([P, PASSES, T], U8, name="k_scale_pool")
         vs_pool = sb.tile([P, T], F32, name="vs_pool")
         q_codes = sb.tile([P, PASSES, NQ], I32, name="q_codes", align_bytes=64)
         q_planes = sb.tile([P, PASSES, NQ], U8, name="q_planes", align_bytes=64)
         ident = sb.tile([P, P], F32, name="ident")
-        warm_in = sb.tile([P, 1], F32, name="warm_in")
-        warm_out = sb.tile([P, 1], F32, name="warm_out")
 
         nc.vector.memset(k_scale_pool[:].bitcast(I32), 0)
-        nc.vector.memset(warm_in[:], 0.0)
         nc.vector.memset(q_planes[:].bitcast(I32), 0)
-        nc.vector.memset(k_plane1[:].bitcast(I32), 0)
         nc.vector.memset(vs_pool[0:VS_ROW, :], 0.0)
         make_identity(nc, ident[:])
-        nc.scalar.activation(warm_out[:], warm_in[:], ACT.Exp)
 
         nc.sync.dma_start(offsets[:], offs)
         nc.sync.dma_start(vs_pool[VS_ROW : VS_ROW + 1, :], vs[0:1, :])
-        nc.sync.dma_start(q_codes[:], q_words[0].rearrange("o g q r -> g o (q r)").bitcast(I32))
         k_word_rows = k_words[0].rearrange("g t b -> g (t b)").bitcast(I32)
+        nc.sync.dma_start(k_word_pool[:, :KEY_SPLIT], k_word_rows[:, :KEY_SPLIT])
         k_scale_rows = k_scales.rearrange("o (quad r) t -> r quad o t", r=PACK)
         for r in range(PACK):
-            nc.sync.dma_start(k_scale_pool[r:P:SECOND_PASS_SHIFT, :].bitcast(I32), k_scale_rows[r].bitcast(I32))
-        nc.sync.dma_start(k_word_pool[:], k_word_rows)
+            nc.sync.dma_start(k_scale_pool[r:P:QUADRANT, :, :].bitcast(I32), k_scale_rows[r].bitcast(I32))
+        nc.sync.dma_start(k_word_pool[:, KEY_SPLIT:], k_word_rows[:, KEY_SPLIT:])
+        v_pool0 = sb.tile([P, T], F32, name="v_pool0", tag="max_after_first_value_gather", align_bytes=64)
+        nc.sync.dma_start(v_pool0[:, :VALUE_SPLIT], vT[0:P, :VALUE_SPLIT])
+        nc.sync.dma_start(q_codes[:], q_words[0].rearrange("o g q r -> g o (q r)").bitcast(I32))
         for quad in range(P // QUADRANT):
             nc.sync.dma_start(
                 q_planes[QUADRANT * quad : QUADRANT * quad + PACK, :, :].bitcast(I32),
                 q_scales[0][:, PACK * quad : PACK * (quad + 1), :].rearrange("o f q -> f o q").bitcast(I32),
             )
-        v_pool0 = sb.tile([P, T], F32, name="v_pool0", tag="max_after_first_value_gather", align_bytes=64)
-        nc.sync.dma_start(v_pool0[:], vT[0:P, :])
+        nc.sync.dma_start(v_pool0[:, VALUE_SPLIT:], vT[0:P, VALUE_SPLIT:])
 
         vs_picked = sb.tile([P, N], F32, name="vs_picked")
         nc.vector.tensor_copy(vs_picked[:], vs_pool[:].indirect(offsets[:]))
 
-        k_plane0 = sb.tile([P, N], U8, name="k_plane0", align_bytes=64)
-        nc.vector.tensor_copy(k_plane0[:], k_scale_pool[:].indirect(offsets[:]))
-        for first, count in ((0, 64), (64, 32), (96, 16)):
-            nc.sync.dma_start(
-                k_plane1[first : first + count, :].bitcast(I32),
-                k_plane0[SECOND_PASS_SHIFT + first : SECOND_PASS_SHIFT + first + count, :].bitcast(I32),
-            )
-        k_planes = (k_plane0, k_plane1)
+        k_planes = []
+        for o in range(PASSES):
+            k_planes.append(sb.tile([P, N], U8, name="k_plane%d" % o, align_bytes=64))
+            nc.vector.tensor_copy(k_planes[o][:], k_scale_pool[:, o, :].indirect(offsets[:]))
 
         v_pool1 = sb.tile([P, T], F32, name="v_pool1", tag="weights_after_second_value_gather", align_bytes=64)
         nc.sync.dma_start(v_pool1[:], vT[P : 2 * P, :])
         vs_turned = ps.tile([P, PACK, P], F32, name="vs_turned")
         for t in range(PACK):
             nc.tensor.transpose(vs_turned[:, t, :], vs_picked[:, t:N:PACK], ident[:])
-        vs_cols = sb.tile([P, PACK], F32, name="vs_cols", tag="first_value_codes_after_weights", align_bytes=64)
+        vs_cols = sb.tile([P, PACK], F32, name="vs_cols", tag="reciprocal_after_weights", align_bytes=64)
         nc.scalar.copy(vs_cols[:], vs_turned[:, :, VS_ROW])
 
-        k_pairs = sb.tile([P, 2, HALF], U32, name="k_pairs", tag="first_value_gather_after_parting")
+        k_pairs = sb.tile([P, 2, HALF], U32, name="k_pairs", tag="first_value_gather_after_parting", align_bytes=64)
         for half in range(2):
             columns = slice(half * HALF // 16, (half + 1) * HALF // 16)
             nc.vector.tensor_copy(k_pairs[:, half, :], k_word_pool[:].bitcast(U32).indirect(offsets[:, columns]))
@@ -99,8 +92,8 @@ def tile_attend_soft_cap_srtq128n512t2048_kernel(tc, q_words, q_scales, k_words,
                 k_codes[half][:].bitcast(U16), k_pairs[:, half, :].bitcast(U16).rearrange("p (n o) -> p o n", o=PASSES)
             )
         scores = [ps.tile([P, P], F32, name="scores%d" % j, tag="bank%d" % j) for j in range(N // P)]
-        for o in range(PASSES):
-            for j in range(N // P):
+        for j in range(N // P):
+            for o in range(PASSES):
                 half, first = divmod(j * P, HALF)
                 nc.tensor.matmul_mx(
                     out=scores[j][:],
@@ -113,7 +106,7 @@ def tile_attend_soft_cap_srtq128n512t2048_kernel(tc, q_words, q_scales, k_words,
                 )
 
         def turn_values(name, pool, tag, bank):
-            picked = sb.tile([P, N], BF16, name=name + "_picked", tag=tag)
+            picked = sb.tile([P, N], BF16, name=name + "_picked", tag=tag, align_bytes=64)
             nc.vector.tensor_copy(picked[:], pool[:].indirect(offsets[:]))
             slot_pairs = picked[:].bitcast(F32)
             turned = ps.tile([P, 2, P], F32, name=name + "_turned", tag=bank)
@@ -134,7 +127,7 @@ def tile_attend_soft_cap_srtq128n512t2048_kernel(tc, q_words, q_scales, k_words,
             )
             return codes, plane
 
-        capped = sb.tile([P, PACK, P], F32, name="capped", tag="second_value_gather_after_max")
+        capped = sb.tile([P, PACK, P], F32, name="capped", tag="second_value_gather_after_max", align_bytes=64)
         for j in range(N // P):
             nc.scalar.activation(
                 capped[:, :, j * P // PACK : (j + 1) * P // PACK],
@@ -143,7 +136,8 @@ def tile_attend_soft_cap_srtq128n512t2048_kernel(tc, q_words, q_scales, k_words,
                 scale=1.0 / CAP,
             )
 
-        v0_turned = turn_values("v0", v_pool0, "first_value_gather_after_parting", "bank3")
+        v0_turned = turn_values("v0", v_pool0, "first_value_gather_after_parting", "bank0")
+        v0_grouped = group_values("v0", v0_turned, "v0_grouped")
 
         neg_c = sb.tile([P, PACK, P], F32, name="neg_c", tag="max_after_first_value_gather", align_bytes=64)
         neg_m = sb.tile([P, 1], F32, name="neg_m")
@@ -152,7 +146,7 @@ def tile_attend_soft_cap_srtq128n512t2048_kernel(tc, q_words, q_scales, k_words,
         p_turned = ps.tile([P, PACK, NQ], F32, name="p_turned")
         part_sums = []
         for u in range(2):
-            p = sb.tile([P, 2, P], F32, name="p%d" % u)
+            p = sb.tile([P, 2, P], F32, name="p%d" % u, tag=("first_value_gather_after_parting", "p1")[u], align_bytes=64)
             part_sums.append(sb.tile([P, 1], F32, name="part_sum%d" % u))
             nc.scalar.activation(
                 p[:], neg_c[:, 2 * u : 2 * u + 2, :], ACT.Exp, bias=neg_m[:], scale=-1.0, accum_out=part_sums[u][:]
@@ -162,8 +156,8 @@ def tile_attend_soft_cap_srtq128n512t2048_kernel(tc, q_words, q_scales, k_words,
 
         row_sum = sb.tile([P, 1], F32, name="row_sum")
         nc.scalar.activation(row_sum[:], part_sums[0][:], ACT.Identity, bias=part_sums[1][:])
-        v0_grouped = group_values("v0", v0_turned, "max_after_first_value_gather")
         v1_turned = turn_values("v1", v_pool1, "second_value_gather_after_max", "bank2")
+        v0_mx = quantise("v0", v0_grouped, "second_value_gather_after_max")
         v1_grouped = group_values("v1", v1_turned, "v1_grouped")
 
         w = sb.tile([P, NQ, PACK], BF16, name="w", tag="weights_after_second_value_gather", align_bytes=64)
@@ -173,12 +167,12 @@ def tile_attend_soft_cap_srtq128n512t2048_kernel(tc, q_words, q_scales, k_words,
             vs_cols[:].unsqueeze(1).to_broadcast([P, NQ, PACK]),
             ALU.mult,
         )
-        v0_mx = quantise("v0", v0_grouped, "first_value_codes_after_weights")
-        inv_row_sum = sb.tile([P, 1], F32, name="inv_row_sum", tag="max_after_first_value_gather", align_bytes=64)
+        inv_row_sum = sb.tile([P, 1], F32, name="inv_row_sum", tag="reciprocal_after_weights", align_bytes=64)
         nc.vector.reciprocal(inv_row_sum[:], row_sum[:])
+        v1_mx = quantise("v1", v1_grouped, "reciprocal_after_weights_too")
         w_codes, w_plane = quantise("w", w, "w_codes")
-        v1_mx = quantise("v1", v1_grouped, "v1_codes")
 
+        y = sb.tile([P, 2, P], F32, name="y")
         for h, (v_codes, v_plane) in enumerate((v0_mx, v1_mx)):
             sums = ps.tile([P, P], F32, name="sums%d" % h, tag="bank%d" % h)
             nc.tensor.matmul_mx(
@@ -190,9 +184,8 @@ def tile_attend_soft_cap_srtq128n512t2048_kernel(tc, q_words, q_scales, k_words,
                 start=True,
                 stop=True,
             )
-            y = sb.tile([P, P], F32, name="y%d" % h)
             if h == 0:
-                nc.scalar.activation(y[:], sums[:], ACT.Copy, scale=inv_row_sum[:])
+                nc.scalar.activation(y[:, h, :], sums[:], ACT.Copy, scale=inv_row_sum[:])
             else:
-                nc.vector.tensor_scalar(y[:], sums[:], inv_row_sum[:], None, ALU.mult)
-            nc.sync.dma_start(out[0][:, h * P : (h + 1) * P], y[:])
+                nc.vector.tensor_scalar(y[:, h, :], sums[:], inv_row_sum[:], None, ALU.mult)
+        nc.sync.dma_start(out[0], y[:].rearrange("q h e -> q (h e)"))

@@ -22,10 +22,9 @@ P = 128
 PACK = 4
 QUADRANT = 32
 PASSES = D // (P * PACK)
-HALF = N // 2
+SHIFT = QUADRANT // PASSES
 VS_ROW = P - 1
-KEY_SPLIT = 384
-VALUE_SPLIT = 768
+KEY_SPLIT = 768
 
 
 def tile_attend_soft_cap_srtq128n512t2048_kernel(tc, q_words, q_scales, k_words, k_scales, vT, vs, offs, out):
@@ -36,7 +35,8 @@ def tile_attend_soft_cap_srtq128n512t2048_kernel(tc, q_words, q_scales, k_words,
 
         offsets = sb.tile([P, N // 16], U16, name="offsets")
         k_word_pool = sb.tile([P, T], I32, name="k_word_pool")
-        k_scale_pool = sb.tile([P, PASSES, T], U8, name="k_scale_pool")
+        k_scale_pool = sb.tile([P, T], U8, name="k_scale_pool", tag="second_values_after_scale_gather", align_bytes=64)
+        k_plane1 = sb.tile([P, N], U8, name="k_plane1", align_bytes=64)
         vs_pool = sb.tile([P, T], F32, name="vs_pool")
         q_codes = sb.tile([P, PASSES, NQ], I32, name="q_codes", align_bytes=64)
         q_planes = sb.tile([P, PASSES, NQ], U8, name="q_planes", align_bytes=64)
@@ -45,6 +45,7 @@ def tile_attend_soft_cap_srtq128n512t2048_kernel(tc, q_words, q_scales, k_words,
         nc.vector.memset(k_scale_pool[:].bitcast(I32), 0)
         nc.vector.memset(q_planes[:].bitcast(I32), 0)
         nc.vector.memset(vs_pool[0:VS_ROW, :], 0.0)
+        nc.vector.memset(k_plane1[:].bitcast(I32), 0)
         make_identity(nc, ident[:])
 
         nc.sync.dma_start(offsets[:], offs)
@@ -53,27 +54,27 @@ def tile_attend_soft_cap_srtq128n512t2048_kernel(tc, q_words, q_scales, k_words,
         nc.sync.dma_start(k_word_pool[:, :KEY_SPLIT], k_word_rows[:, :KEY_SPLIT])
         k_scale_rows = k_scales.rearrange("o (quad r) t -> r quad o t", r=PACK)
         for r in range(PACK):
-            nc.sync.dma_start(k_scale_pool[r:P:QUADRANT, :, :].bitcast(I32), k_scale_rows[r].bitcast(I32))
+            nc.sync.dma_start(k_scale_pool[r:P:SHIFT, :].bitcast(I32), k_scale_rows[r].bitcast(I32))
         nc.sync.dma_start(k_word_pool[:, KEY_SPLIT:], k_word_rows[:, KEY_SPLIT:])
         v_pool0 = sb.tile([P, T], F32, name="v_pool0", tag="max_after_first_value_gather", align_bytes=64)
-        nc.sync.dma_start(v_pool0[:, :VALUE_SPLIT], vT[0:P, :VALUE_SPLIT])
         nc.sync.dma_start(q_codes[:], q_words[0].rearrange("o g q r -> g o (q r)").bitcast(I32))
         for quad in range(P // QUADRANT):
             nc.sync.dma_start(
                 q_planes[QUADRANT * quad : QUADRANT * quad + PACK, :, :].bitcast(I32),
                 q_scales[0][:, PACK * quad : PACK * (quad + 1), :].rearrange("o f q -> f o q").bitcast(I32),
             )
-        nc.sync.dma_start(v_pool0[:, VALUE_SPLIT:], vT[0:P, VALUE_SPLIT:])
+        nc.sync.dma_start(v_pool0[:], vT[0:P, :])
 
         vs_picked = sb.tile([P, N], F32, name="vs_picked")
         nc.vector.tensor_copy(vs_picked[:], vs_pool[:].indirect(offsets[:]))
 
-        k_planes = []
-        for o in range(PASSES):
-            k_planes.append(sb.tile([P, N], U8, name="k_plane%d" % o, align_bytes=64))
-            nc.vector.tensor_copy(k_planes[o][:], k_scale_pool[:, o, :].indirect(offsets[:]))
+        k_plane0 = sb.tile([P, N], U8, name="k_plane0", align_bytes=64)
+        nc.vector.tensor_copy(k_plane0[:], k_scale_pool[:].indirect(offsets[:]))
+        for r in range(PACK):
+            nc.sync.dma_start(k_plane1[r:P:QUADRANT, :].bitcast(I32), k_plane0[SHIFT + r : P : QUADRANT, :].bitcast(I32))
+        k_planes = (k_plane0, k_plane1)
 
-        v_pool1 = sb.tile([P, T], F32, name="v_pool1", tag="weights_after_second_value_gather", align_bytes=64)
+        v_pool1 = sb.tile([P, T], F32, name="v_pool1", tag="second_values_after_scale_gather", align_bytes=64)
         nc.sync.dma_start(v_pool1[:], vT[P : 2 * P, :])
         vs_turned = ps.tile([P, PACK, P], F32, name="vs_turned")
         for t in range(PACK):
@@ -81,25 +82,18 @@ def tile_attend_soft_cap_srtq128n512t2048_kernel(tc, q_words, q_scales, k_words,
         vs_cols = sb.tile([P, PACK], F32, name="vs_cols", tag="reciprocal_after_weights", align_bytes=64)
         nc.scalar.copy(vs_cols[:], vs_turned[:, :, VS_ROW])
 
-        k_pairs = sb.tile([P, 2, HALF], U32, name="k_pairs", tag="first_value_gather_after_parting", align_bytes=64)
-        for half in range(2):
-            columns = slice(half * HALF // 16, (half + 1) * HALF // 16)
-            nc.vector.tensor_copy(k_pairs[:, half, :], k_word_pool[:].bitcast(U32).indirect(offsets[:, columns]))
-        k_codes = []
-        for half in range(2):
-            k_codes.append(sb.tile([P, PASSES, 2 * HALF], U8, name="k_codes%d" % half, align_bytes=64))
-            nc.vector.tensor_copy(
-                k_codes[half][:].bitcast(U16), k_pairs[:, half, :].bitcast(U16).rearrange("p (n o) -> p o n", o=PASSES)
-            )
+        k_pairs = sb.tile([P, N], U32, name="k_pairs", tag="first_value_gather_after_parting", align_bytes=64)
+        nc.vector.tensor_copy(k_pairs[:], k_word_pool[:].bitcast(U32).indirect(offsets[:]))
+        k_codes = sb.tile([P, PASSES, 2 * N], U8, name="k_codes", align_bytes=64)
+        nc.vector.tensor_copy(k_codes[:].bitcast(U16), k_pairs[:].bitcast(U16).rearrange("p (n o) -> p o n", o=PASSES))
         scores = [ps.tile([P, P], F32, name="scores%d" % j, tag="bank%d" % j) for j in range(N // P)]
-        for j in range(N // P):
-            for o in range(PASSES):
-                half, first = divmod(j * P, HALF)
+        for o in range(PASSES):
+            for j in range(N // P):
                 nc.tensor.matmul_mx(
                     out=scores[j][:],
                     lhsT=q_codes[:, o, :].bitcast(FP8X4),
                     lhsT_scale=q_planes[:, o, :],
-                    rhs=k_codes[half][:, o, 2 * first : 2 * (first + P)].bitcast(FP4X4),
+                    rhs=k_codes[:, o, 2 * j * P : 2 * (j + 1) * P].bitcast(FP4X4),
                     rhs_scale=k_planes[o][:, j * P : (j + 1) * P],
                     start=(o == 0),
                     stop=(o == PASSES - 1),
@@ -137,7 +131,6 @@ def tile_attend_soft_cap_srtq128n512t2048_kernel(tc, q_words, q_scales, k_words,
             )
 
         v0_turned = turn_values("v0", v_pool0, "first_value_gather_after_parting", "bank0")
-        v0_grouped = group_values("v0", v0_turned, "v0_grouped")
 
         neg_c = sb.tile([P, PACK, P], F32, name="neg_c", tag="max_after_first_value_gather", align_bytes=64)
         neg_m = sb.tile([P, 1], F32, name="neg_m")
@@ -146,7 +139,7 @@ def tile_attend_soft_cap_srtq128n512t2048_kernel(tc, q_words, q_scales, k_words,
         p_turned = ps.tile([P, PACK, NQ], F32, name="p_turned")
         part_sums = []
         for u in range(2):
-            p = sb.tile([P, 2, P], F32, name="p%d" % u, tag=("first_value_gather_after_parting", "p1")[u], align_bytes=64)
+            p = sb.tile([P, 2, P], F32, name="p%d" % u, align_bytes=64)
             part_sums.append(sb.tile([P, 1], F32, name="part_sum%d" % u))
             nc.scalar.activation(
                 p[:], neg_c[:, 2 * u : 2 * u + 2, :], ACT.Exp, bias=neg_m[:], scale=-1.0, accum_out=part_sums[u][:]
@@ -156,21 +149,22 @@ def tile_attend_soft_cap_srtq128n512t2048_kernel(tc, q_words, q_scales, k_words,
 
         row_sum = sb.tile([P, 1], F32, name="row_sum")
         nc.scalar.activation(row_sum[:], part_sums[0][:], ACT.Identity, bias=part_sums[1][:])
+        v0_grouped = group_values("v0", v0_turned, "max_after_first_value_gather")
         v1_turned = turn_values("v1", v_pool1, "second_value_gather_after_max", "bank2")
-        v0_mx = quantise("v0", v0_grouped, "second_value_gather_after_max")
         v1_grouped = group_values("v1", v1_turned, "v1_grouped")
 
-        w = sb.tile([P, NQ, PACK], BF16, name="w", tag="weights_after_second_value_gather", align_bytes=64)
+        w = sb.tile([P, NQ, PACK], BF16, name="w", tag="second_values_after_scale_gather", align_bytes=64)
         nc.vector.tensor_tensor(
             w[:],
             p_turned[:].rearrange("s t q -> s q t"),
             vs_cols[:].unsqueeze(1).to_broadcast([P, NQ, PACK]),
             ALU.mult,
         )
-        inv_row_sum = sb.tile([P, 1], F32, name="inv_row_sum", tag="reciprocal_after_weights", align_bytes=64)
+        v0_mx = quantise("v0", v0_grouped, "reciprocal_after_weights")
+        inv_row_sum = sb.tile([P, 1], F32, name="inv_row_sum", tag="max_after_first_value_gather", align_bytes=64)
         nc.vector.reciprocal(inv_row_sum[:], row_sum[:])
-        v1_mx = quantise("v1", v1_grouped, "reciprocal_after_weights_too")
         w_codes, w_plane = quantise("w", w, "w_codes")
+        v1_mx = quantise("v1", v1_grouped, "second_values_after_scale_gather")
 
         y = sb.tile([P, 2, P], F32, name="y")
         for h, (v_codes, v_plane) in enumerate((v0_mx, v1_mx)):

@@ -24,7 +24,8 @@ QUADRANT = 32
 PASSES = D // (P * PACK)
 SHIFT = QUADRANT // PASSES
 VS_ROW = P - 1
-KEY_SPLIT = 768
+VALUE_SPLIT = 768
+KEY_SPLIT = 448
 
 
 def tile_attend_soft_cap_srtq128n512t2048_kernel(tc, q_words, q_scales, k_words, k_scales, vT, vs, offs, out):
@@ -48,30 +49,30 @@ def tile_attend_soft_cap_srtq128n512t2048_kernel(tc, q_words, q_scales, k_words,
         nc.vector.memset(k_plane1[:].bitcast(I32), 0)
         make_identity(nc, ident[:])
 
-        nc.sync.dma_start(offsets[:], offs)
-        nc.sync.dma_start(vs_pool[VS_ROW : VS_ROW + 1, :], vs[0:1, :])
         k_word_rows = k_words[0].rearrange("g t b -> g (t b)").bitcast(I32)
         nc.sync.dma_start(k_word_pool[:, :KEY_SPLIT], k_word_rows[:, :KEY_SPLIT])
+        nc.sync.dma_start(offsets[:], offs)
+        nc.sync.dma_start(vs_pool[VS_ROW : VS_ROW + 1, :], vs[0:1, :])
         k_scale_rows = k_scales.rearrange("o (quad r) t -> r quad o t", r=PACK)
         for r in range(PACK):
             nc.sync.dma_start(k_scale_pool[r:P:SHIFT, :].bitcast(I32), k_scale_rows[r].bitcast(I32))
         nc.sync.dma_start(k_word_pool[:, KEY_SPLIT:], k_word_rows[:, KEY_SPLIT:])
         v_pool0 = sb.tile([P, T], F32, name="v_pool0", tag="max_after_first_value_gather", align_bytes=64)
+        nc.sync.dma_start(v_pool0[:, :VALUE_SPLIT], vT[0:P, :VALUE_SPLIT])
         nc.sync.dma_start(q_codes[:], q_words[0].rearrange("o g q r -> g o (q r)").bitcast(I32))
         for quad in range(P // QUADRANT):
             nc.sync.dma_start(
                 q_planes[QUADRANT * quad : QUADRANT * quad + PACK, :, :].bitcast(I32),
                 q_scales[0][:, PACK * quad : PACK * (quad + 1), :].rearrange("o f q -> f o q").bitcast(I32),
             )
-        nc.sync.dma_start(v_pool0[:], vT[0:P, :])
+        nc.sync.dma_start(v_pool0[:, VALUE_SPLIT:], vT[0:P, VALUE_SPLIT:])
 
         vs_picked = sb.tile([P, N], F32, name="vs_picked")
         nc.vector.tensor_copy(vs_picked[:], vs_pool[:].indirect(offsets[:]))
 
         k_plane0 = sb.tile([P, N], U8, name="k_plane0", align_bytes=64)
         nc.vector.tensor_copy(k_plane0[:], k_scale_pool[:].indirect(offsets[:]))
-        for r in range(PACK):
-            nc.sync.dma_start(k_plane1[r:P:QUADRANT, :].bitcast(I32), k_plane0[SHIFT + r : P : QUADRANT, :].bitcast(I32))
+        nc.sync.dma_start(k_plane1[: P - SHIFT, :].bitcast(I32), k_plane0[SHIFT:, :].bitcast(I32))
         k_planes = (k_plane0, k_plane1)
 
         v_pool1 = sb.tile([P, T], F32, name="v_pool1", tag="second_values_after_scale_gather", align_bytes=64)

@@ -52,10 +52,10 @@ def tile_attend_soft_cap_srtq128n512t2048_kernel(tc, q_words, q_scales, k_words,
         k_word_rows = k_words[0].rearrange("g t b -> g (t b)").bitcast(I32)
         nc.sync.dma_start(k_word_pool[:, :KEY_SPLIT], k_word_rows[:, :KEY_SPLIT])
         nc.sync.dma_start(offsets[:], offs)
-        nc.sync.dma_start(vs_pool[VS_ROW : VS_ROW + 1, :], vs[0:1, :])
         k_scale_rows = k_scales.rearrange("o (quad r) t -> r quad o t", r=PACK)
         for r in range(PACK):
             nc.sync.dma_start(k_scale_pool[r:P:SHIFT, :].bitcast(I32), k_scale_rows[r].bitcast(I32))
+        nc.sync.dma_start(vs_pool[VS_ROW : VS_ROW + 1, :], vs[0:1, :])
         nc.sync.dma_start(k_word_pool[:, KEY_SPLIT:], k_word_rows[:, KEY_SPLIT:])
         v_pool0 = sb.tile([P, T], F32, name="v_pool0", tag="max_after_first_value_gather", align_bytes=64)
         nc.sync.dma_start(v_pool0[:, :VALUE_SPLIT], vT[0:P, :VALUE_SPLIT])
@@ -67,13 +67,13 @@ def tile_attend_soft_cap_srtq128n512t2048_kernel(tc, q_words, q_scales, k_words,
             )
         nc.sync.dma_start(v_pool0[:, VALUE_SPLIT:], vT[0:P, VALUE_SPLIT:])
 
-        vs_picked = sb.tile([P, N], F32, name="vs_picked")
-        nc.vector.tensor_copy(vs_picked[:], vs_pool[:].indirect(offsets[:]))
-
         k_plane0 = sb.tile([P, N], U8, name="k_plane0", align_bytes=64)
         nc.vector.tensor_copy(k_plane0[:], k_scale_pool[:].indirect(offsets[:]))
         nc.sync.dma_start(k_plane1[: P - SHIFT, :].bitcast(I32), k_plane0[SHIFT:, :].bitcast(I32))
         k_planes = (k_plane0, k_plane1)
+
+        vs_picked = sb.tile([P, N], F32, name="vs_picked")
+        nc.vector.tensor_copy(vs_picked[:], vs_pool[:].indirect(offsets[:]))
 
         v_pool1 = sb.tile([P, T], F32, name="v_pool1", tag="second_values_after_scale_gather", align_bytes=64)
         nc.sync.dma_start(v_pool1[:], vT[P : 2 * P, :])
@@ -83,7 +83,7 @@ def tile_attend_soft_cap_srtq128n512t2048_kernel(tc, q_words, q_scales, k_words,
         vs_cols = sb.tile([P, PACK], F32, name="vs_cols", tag="reciprocal_after_weights", align_bytes=64)
         nc.scalar.copy(vs_cols[:], vs_turned[:, :, VS_ROW])
 
-        k_pairs = sb.tile([P, N], U32, name="k_pairs", tag="first_value_gather_after_parting", align_bytes=64)
+        k_pairs = sb.tile([P, N], U32, name="k_pairs", align_bytes=64)
         nc.vector.tensor_copy(k_pairs[:], k_word_pool[:].bitcast(U32).indirect(offsets[:]))
         k_codes = sb.tile([P, PASSES, 2 * N], U8, name="k_codes", align_bytes=64)
         nc.vector.tensor_copy(k_codes[:].bitcast(U16), k_pairs[:].bitcast(U16).rearrange("p (n o) -> p o n", o=PASSES))
@@ -122,7 +122,7 @@ def tile_attend_soft_cap_srtq128n512t2048_kernel(tc, q_words, q_scales, k_words,
             )
             return codes, plane
 
-        capped = sb.tile([P, PACK, P], F32, name="capped", tag="second_value_gather_after_max", align_bytes=64)
+        capped = sb.tile([P, PACK, P], F32, name="capped", align_bytes=64)
         for j in range(N // P):
             nc.scalar.activation(
                 capped[:, :, j * P // PACK : (j + 1) * P // PACK],
@@ -131,7 +131,7 @@ def tile_attend_soft_cap_srtq128n512t2048_kernel(tc, q_words, q_scales, k_words,
                 scale=1.0 / CAP,
             )
 
-        v0_turned = turn_values("v0", v_pool0, "first_value_gather_after_parting", "bank0")
+        v0_turned = turn_values("v0", v_pool0, "v0_picked", "bank0")
 
         neg_c = sb.tile([P, PACK, P], F32, name="neg_c", tag="max_after_first_value_gather", align_bytes=64)
         neg_m = sb.tile([P, 1], F32, name="neg_m")
@@ -152,6 +152,7 @@ def tile_attend_soft_cap_srtq128n512t2048_kernel(tc, q_words, q_scales, k_words,
         nc.scalar.activation(row_sum[:], part_sums[0][:], ACT.Identity, bias=part_sums[1][:])
         v0_grouped = group_values("v0", v0_turned, "max_after_first_value_gather")
         v1_turned = turn_values("v1", v_pool1, "second_value_gather_after_max", "bank2")
+        v0_mx = quantise("v0", v0_grouped, "second_value_gather_after_max")
         v1_grouped = group_values("v1", v1_turned, "v1_grouped")
 
         w = sb.tile([P, NQ, PACK], BF16, name="w", tag="second_values_after_scale_gather", align_bytes=64)
@@ -161,11 +162,10 @@ def tile_attend_soft_cap_srtq128n512t2048_kernel(tc, q_words, q_scales, k_words,
             vs_cols[:].unsqueeze(1).to_broadcast([P, NQ, PACK]),
             ALU.mult,
         )
-        v0_mx = quantise("v0", v0_grouped, "reciprocal_after_weights")
-        inv_row_sum = sb.tile([P, 1], F32, name="inv_row_sum", tag="max_after_first_value_gather", align_bytes=64)
+        inv_row_sum = sb.tile([P, 1], F32, name="inv_row_sum", tag="reciprocal_after_weights", align_bytes=64)
         nc.vector.reciprocal(inv_row_sum[:], row_sum[:])
+        v1_mx = quantise("v1", v1_grouped, "reciprocal_after_weights_too")
         w_codes, w_plane = quantise("w", w, "w_codes")
-        v1_mx = quantise("v1", v1_grouped, "second_values_after_scale_gather")
 
         y = sb.tile([P, 2, P], F32, name="y")
         for h, (v_codes, v_plane) in enumerate((v0_mx, v1_mx)):

@@ -24,7 +24,7 @@ QUADRANT = 32
 PASSES = D // (P * PACK)
 SHIFT = QUADRANT // PASSES
 VS_ROW = P - 1
-VALUE_SPLIT = 768
+VALUE_SPLIT = 1536
 KEY_SPLIT = 448
 
 
@@ -58,24 +58,28 @@ def tile_attend_soft_cap_srtq128n512t2048_kernel(tc, q_words, q_scales, k_words,
         nc.sync.dma_start(vs_pool[VS_ROW : VS_ROW + 1, :], vs[0:1, :])
         nc.sync.dma_start(k_word_pool[:, KEY_SPLIT:], k_word_rows[:, KEY_SPLIT:])
         v_pool0 = sb.tile([P, T], F32, name="v_pool0", tag="max_after_first_value_gather", align_bytes=64)
-        nc.sync.dma_start(v_pool0[:, :VALUE_SPLIT], vT[0:P, :VALUE_SPLIT])
         nc.sync.dma_start(q_codes[:], q_words[0].rearrange("o g q r -> g o (q r)").bitcast(I32))
         for quad in range(P // QUADRANT):
             nc.sync.dma_start(
                 q_planes[QUADRANT * quad : QUADRANT * quad + PACK, :, :].bitcast(I32),
                 q_scales[0][:, PACK * quad : PACK * (quad + 1), :].rearrange("o f q -> f o q").bitcast(I32),
             )
-        nc.sync.dma_start(v_pool0[:, VALUE_SPLIT:], vT[0:P, VALUE_SPLIT:])
+        nc.sync.dma_start(v_pool0[:, :VALUE_SPLIT], vT[0:P, :VALUE_SPLIT])
 
         k_plane0 = sb.tile([P, N], U8, name="k_plane0", align_bytes=64)
         nc.vector.tensor_copy(k_plane0[:], k_scale_pool[:].indirect(offsets[:]))
-        nc.sync.dma_start(k_plane1[: P - SHIFT, :].bitcast(I32), k_plane0[SHIFT:, :].bitcast(I32))
+        for first, count in ((0, 2 * QUADRANT), (2 * QUADRANT, PACK), (3 * QUADRANT, PACK)):
+            nc.sync.dma_start(
+                k_plane1[first : first + count, :].bitcast(I32),
+                k_plane0[first + SHIFT : first + SHIFT + count, :].bitcast(I32),
+            )
         k_planes = (k_plane0, k_plane1)
 
         vs_picked = sb.tile([P, N], F32, name="vs_picked")
         nc.vector.tensor_copy(vs_picked[:], vs_pool[:].indirect(offsets[:]))
 
         v_pool1 = sb.tile([P, T], F32, name="v_pool1", tag="second_values_after_scale_gather", align_bytes=64)
+        nc.sync.dma_start(v_pool0[:, VALUE_SPLIT:], vT[0:P, VALUE_SPLIT:])
         nc.sync.dma_start(v_pool1[:], vT[P : 2 * P, :])
         vs_turned = ps.tile([P, PACK, P], F32, name="vs_turned")
         for t in range(PACK):

@@ -23,8 +23,9 @@ PACK = 4
 QUADRANT = 32
 PASSES = D // (P * PACK)
 SHIFT = QUADRANT // PASSES
+HALF = N // 2
 VS_ROW = P - 1
-VALUE_SPLIT = 1536
+VALUE_SPLIT = 1792
 KEY_SPLIT = 448
 
 
@@ -52,19 +53,22 @@ def tile_attend_soft_cap_srtq128n512t2048_kernel(tc, q_words, q_scales, k_words,
         k_word_rows = k_words[0].rearrange("g t b -> g (t b)").bitcast(I32)
         nc.sync.dma_start(k_word_pool[:, :KEY_SPLIT], k_word_rows[:, :KEY_SPLIT])
         nc.sync.dma_start(offsets[:], offs)
+        nc.sync.dma_start(vs_pool[VS_ROW : VS_ROW + 1, :], vs[0:1, :])
         k_scale_rows = k_scales.rearrange("o (quad r) t -> r quad o t", r=PACK)
         for r in range(PACK):
             nc.sync.dma_start(k_scale_pool[r:P:SHIFT, :].bitcast(I32), k_scale_rows[r].bitcast(I32))
-        nc.sync.dma_start(vs_pool[VS_ROW : VS_ROW + 1, :], vs[0:1, :])
         nc.sync.dma_start(k_word_pool[:, KEY_SPLIT:], k_word_rows[:, KEY_SPLIT:])
         v_pool0 = sb.tile([P, T], F32, name="v_pool0", tag="max_after_first_value_gather", align_bytes=64)
-        nc.sync.dma_start(q_codes[:], q_words[0].rearrange("o g q r -> g o (q r)").bitcast(I32))
         for quad in range(P // QUADRANT):
             nc.sync.dma_start(
                 q_planes[QUADRANT * quad : QUADRANT * quad + PACK, :, :].bitcast(I32),
                 q_scales[0][:, PACK * quad : PACK * (quad + 1), :].rearrange("o f q -> f o q").bitcast(I32),
             )
+        nc.sync.dma_start(q_codes[:], q_words[0].rearrange("o g q r -> g o (q r)").bitcast(I32))
         nc.sync.dma_start(v_pool0[:, :VALUE_SPLIT], vT[0:P, :VALUE_SPLIT])
+
+        vs_picked = sb.tile([P, N], F32, name="vs_picked")
+        nc.vector.tensor_copy(vs_picked[:], vs_pool[:].indirect(offsets[:]))
 
         k_plane0 = sb.tile([P, N], U8, name="k_plane0", align_bytes=64)
         nc.vector.tensor_copy(k_plane0[:], k_scale_pool[:].indirect(offsets[:]))
@@ -75,9 +79,6 @@ def tile_attend_soft_cap_srtq128n512t2048_kernel(tc, q_words, q_scales, k_words,
             )
         k_planes = (k_plane0, k_plane1)
 
-        vs_picked = sb.tile([P, N], F32, name="vs_picked")
-        nc.vector.tensor_copy(vs_picked[:], vs_pool[:].indirect(offsets[:]))
-
         v_pool1 = sb.tile([P, T], F32, name="v_pool1", tag="second_values_after_scale_gather", align_bytes=64)
         nc.sync.dma_start(v_pool0[:, VALUE_SPLIT:], vT[0:P, VALUE_SPLIT:])
         nc.sync.dma_start(v_pool1[:], vT[P : 2 * P, :])
@@ -87,18 +88,25 @@ def tile_attend_soft_cap_srtq128n512t2048_kernel(tc, q_words, q_scales, k_words,
         vs_cols = sb.tile([P, PACK], F32, name="vs_cols", tag="reciprocal_after_weights", align_bytes=64)
         nc.scalar.copy(vs_cols[:], vs_turned[:, :, VS_ROW])
 
-        k_pairs = sb.tile([P, N], U32, name="k_pairs", align_bytes=64)
-        nc.vector.tensor_copy(k_pairs[:], k_word_pool[:].bitcast(U32).indirect(offsets[:]))
-        k_codes = sb.tile([P, PASSES, 2 * N], U8, name="k_codes", align_bytes=64)
-        nc.vector.tensor_copy(k_codes[:].bitcast(U16), k_pairs[:].bitcast(U16).rearrange("p (n o) -> p o n", o=PASSES))
+        k_pairs = sb.tile([P, 2, HALF], U32, name="k_pairs", align_bytes=64)
+        for half in range(2):
+            columns = slice(half * HALF // 16, (half + 1) * HALF // 16)
+            nc.vector.tensor_copy(k_pairs[:, half, :], k_word_pool[:].bitcast(U32).indirect(offsets[:, columns]))
+        k_codes = []
+        for half in range(2):
+            k_codes.append(sb.tile([P, PASSES, 2 * HALF], U8, name="k_codes%d" % half, align_bytes=64))
+            nc.vector.tensor_copy(
+                k_codes[half][:].bitcast(U16), k_pairs[:, half, :].bitcast(U16).rearrange("p (n o) -> p o n", o=PASSES)
+            )
         scores = [ps.tile([P, P], F32, name="scores%d" % j, tag="bank%d" % j) for j in range(N // P)]
         for o in range(PASSES):
             for j in range(N // P):
+                half, first = divmod(j * P, HALF)
                 nc.tensor.matmul_mx(
                     out=scores[j][:],
                     lhsT=q_codes[:, o, :].bitcast(FP8X4),
                     lhsT_scale=q_planes[:, o, :],
-                    rhs=k_codes[:, o, 2 * j * P : 2 * (j + 1) * P].bitcast(FP4X4),
+                    rhs=k_codes[half][:, o, 2 * first : 2 * (first + P)].bitcast(FP4X4),
                     rhs_scale=k_planes[o][:, j * P : (j + 1) * P],
                     start=(o == 0),
                     stop=(o == PASSES - 1),
@@ -168,8 +176,8 @@ def tile_attend_soft_cap_srtq128n512t2048_kernel(tc, q_words, q_scales, k_words,
         )
         inv_row_sum = sb.tile([P, 1], F32, name="inv_row_sum", tag="reciprocal_after_weights", align_bytes=64)
         nc.vector.reciprocal(inv_row_sum[:], row_sum[:])
-        v1_mx = quantise("v1", v1_grouped, "reciprocal_after_weights_too")
         w_codes, w_plane = quantise("w", w, "w_codes")
+        v1_mx = quantise("v1", v1_grouped, "v1_codes")
 
         y = sb.tile([P, 2, P], F32, name="y")
         for h, (v_codes, v_plane) in enumerate((v0_mx, v1_mx)):
@@ -187,4 +195,4 @@ def tile_attend_soft_cap_srtq128n512t2048_kernel(tc, q_words, q_scales, k_words,
                 nc.scalar.activation(y[:, h, :], sums[:], ACT.Copy, scale=inv_row_sum[:])
             else:
                 nc.vector.tensor_scalar(y[:, h, :], sums[:], inv_row_sum[:], None, ALU.mult)
-        nc.sync.dma_start(out[0], y[:].rearrange("q h e -> q (h e)"))
+            nc.sync.dma_start(out[0][:, h * P : (h + 1) * P], y[:, h, :])

@@ -25,7 +25,7 @@ PASSES = D // (P * PACK)
 SHIFT = QUADRANT // PASSES
 HALF = N // 2
 VS_ROW = P - 1
-VALUE_SPLIT = 1792
+VALUE_SPLIT = 1536
 KEY_SPLIT = 448
 
 

@@ -23,31 +23,41 @@ PACK = 4
 QUADRANT = 32
 PASSES = D // (P * PACK)
 SHIFT = QUADRANT // PASSES
-HALF = N // 2
+GROUPS = N // P
+COLUMN = 16
 VS_ROW = P - 1
-VALUE_SPLIT = 1536
+VALUE_SPLIT = 1280
 KEY_SPLIT = 448
+LAST_VALUES_ON_SCALAR = 192
 
 
 def tile_attend_soft_cap_srtq128n512t2048_kernel(tc, q_words, q_scales, k_words, k_scales, vT, vs, offs, out):
     nc = tc.nc
     with ExitStack() as ctx:
         sb = ctx.enter_context(tc.tile_pool(name="sb", bufs=1))
+        reused = ctx.enter_context(tc.tile_pool(name="reused", bufs=1))
         ps = ctx.enter_context(tc.psum_pool(name="ps", bufs=1))
 
-        offsets = sb.tile([P, N // 16], U16, name="offsets")
+        offsets = sb.tile([P, N // COLUMN], U16, name="offsets")
         k_word_pool = sb.tile([P, T], I32, name="k_word_pool")
-        k_scale_pool = sb.tile([P, T], U8, name="k_scale_pool", tag="second_values_after_scale_gather", align_bytes=64)
+        k_scale_pool = reused.tile([P, T], U8, name="k_scale_pool", align_bytes=64, offset=0)
         k_plane1 = sb.tile([P, N], U8, name="k_plane1", align_bytes=64)
         vs_pool = sb.tile([P, T], F32, name="vs_pool")
         q_codes = sb.tile([P, PASSES, NQ], I32, name="q_codes", align_bytes=64)
         q_planes = sb.tile([P, PASSES, NQ], U8, name="q_planes", align_bytes=64)
         ident = sb.tile([P, P], F32, name="ident")
 
+        def listed(pool, first, count):
+            return pool.indirect(offsets[:, first // COLUMN : (first + count) // COLUMN])
+
         nc.vector.memset(k_scale_pool[:].bitcast(I32), 0)
         nc.vector.memset(q_planes[:].bitcast(I32), 0)
         nc.vector.memset(vs_pool[0:VS_ROW, :], 0.0)
         nc.vector.memset(k_plane1[:].bitcast(I32), 0)
+        warm_in = sb.tile([P, 1], F32, name="warm_in")
+        warm_out = sb.tile([P, 1], F32, name="warm_out")
+        nc.gpsimd.memset(warm_in[:], 0.0)
+        nc.scalar.activation(warm_out[:], warm_in[:], ACT.Tanh)
         make_identity(nc, ident[:])
 
         k_word_rows = k_words[0].rearrange("g t b -> g (t b)").bitcast(I32)
@@ -58,7 +68,7 @@ def tile_attend_soft_cap_srtq128n512t2048_kernel(tc, q_words, q_scales, k_words,
         for r in range(PACK):
             nc.sync.dma_start(k_scale_pool[r:P:SHIFT, :].bitcast(I32), k_scale_rows[r].bitcast(I32))
         nc.sync.dma_start(k_word_pool[:, KEY_SPLIT:], k_word_rows[:, KEY_SPLIT:])
-        v_pool0 = sb.tile([P, T], F32, name="v_pool0", tag="max_after_first_value_gather", align_bytes=64)
+        v_pool0 = sb.tile([P, T], F32, name="v_pool0")
         for quad in range(P // QUADRANT):
             nc.sync.dma_start(
                 q_planes[QUADRANT * quad : QUADRANT * quad + PACK, :, :].bitcast(I32),
@@ -67,87 +77,101 @@ def tile_attend_soft_cap_srtq128n512t2048_kernel(tc, q_words, q_scales, k_words,
         nc.sync.dma_start(q_codes[:], q_words[0].rearrange("o g q r -> g o (q r)").bitcast(I32))
         nc.sync.dma_start(v_pool0[:, :VALUE_SPLIT], vT[0:P, :VALUE_SPLIT])
 
-        vs_picked = sb.tile([P, N], F32, name="vs_picked")
-        nc.vector.tensor_copy(vs_picked[:], vs_pool[:].indirect(offsets[:]))
-
         k_plane0 = sb.tile([P, N], U8, name="k_plane0", align_bytes=64)
-        nc.vector.tensor_copy(k_plane0[:], k_scale_pool[:].indirect(offsets[:]))
+        nc.vector.tensor_copy(k_plane0[:], listed(k_scale_pool[:], 0, N))
         for first, count in ((0, 2 * QUADRANT), (2 * QUADRANT, PACK), (3 * QUADRANT, PACK)):
             nc.sync.dma_start(
                 k_plane1[first : first + count, :].bitcast(I32),
                 k_plane0[first + SHIFT : first + SHIFT + count, :].bitcast(I32),
             )
         k_planes = (k_plane0, k_plane1)
-
-        v_pool1 = sb.tile([P, T], F32, name="v_pool1", tag="second_values_after_scale_gather", align_bytes=64)
+        v_pool1 = reused.tile([P, T], F32, name="v_pool1", align_bytes=64, offset=0)
         nc.sync.dma_start(v_pool0[:, VALUE_SPLIT:], vT[0:P, VALUE_SPLIT:])
         nc.sync.dma_start(v_pool1[:], vT[P : 2 * P, :])
+
+        vs_picked = sb.tile([P, N], F32, name="vs_picked")
+        nc.scalar.activation(vs_picked[:], listed(vs_pool[:], 0, N), ACT.Copy)
         vs_turned = ps.tile([P, PACK, P], F32, name="vs_turned")
         for t in range(PACK):
             nc.tensor.transpose(vs_turned[:, t, :], vs_picked[:, t:N:PACK], ident[:])
-        vs_cols = sb.tile([P, PACK], F32, name="vs_cols", tag="reciprocal_after_weights", align_bytes=64)
+        vs_cols = sb.tile([P, PACK], F32, name="vs_cols", tag="reciprocal_after_weights")
         nc.scalar.copy(vs_cols[:], vs_turned[:, :, VS_ROW])
 
-        k_pairs = sb.tile([P, 2, HALF], U32, name="k_pairs", align_bytes=64)
-        for half in range(2):
-            columns = slice(half * HALF // 16, (half + 1) * HALF // 16)
-            nc.vector.tensor_copy(k_pairs[:, half, :], k_word_pool[:].bitcast(U32).indirect(offsets[:, columns]))
-        k_codes = []
-        for half in range(2):
-            k_codes.append(sb.tile([P, PASSES, 2 * HALF], U8, name="k_codes%d" % half, align_bytes=64))
-            nc.vector.tensor_copy(
-                k_codes[half][:].bitcast(U16), k_pairs[:, half, :].bitcast(U16).rearrange("p (n o) -> p o n", o=PASSES)
-            )
-        scores = [ps.tile([P, P], F32, name="scores%d" % j, tag="bank%d" % j) for j in range(N // P)]
-        for o in range(PASSES):
-            for j in range(N // P):
-                half, first = divmod(j * P, HALF)
-                nc.tensor.matmul_mx(
-                    out=scores[j][:],
-                    lhsT=q_codes[:, o, :].bitcast(FP8X4),
-                    lhsT_scale=q_planes[:, o, :],
-                    rhs=k_codes[half][:, o, 2 * first : 2 * (first + P)].bitcast(FP4X4),
-                    rhs_scale=k_planes[o][:, j * P : (j + 1) * P],
-                    start=(o == 0),
-                    stop=(o == PASSES - 1),
+        k_pairs = [sb.tile([P, P], U32, name="k_pairs%d" % j, align_bytes=64) for j in range(GROUPS)]
+        k_codes = [
+            sb.tile([P, PASSES, 2 * P], U8, name="k_codes%d" % j, tag="k_codes%d" % j, align_bytes=64)
+            for j in range(GROUPS)
+        ]
+        for j in range(GROUPS + 1):
+            if j < GROUPS:
+                nc.vector.tensor_copy(k_pairs[j][:], listed(k_word_pool[:].bitcast(U32), j * P, P))
+            if j > 0:
+                nc.vector.tensor_copy(
+                    k_codes[j - 1][:].bitcast(U16),
+                    k_pairs[j - 1][:].bitcast(U16).rearrange("p (n o) -> p o n", o=PASSES),
                 )
 
-        def turn_values(name, pool, tag, bank):
-            picked = sb.tile([P, N], BF16, name=name + "_picked", tag=tag, align_bytes=64)
-            nc.vector.tensor_copy(picked[:], pool[:].indirect(offsets[:]))
+        scores = [ps.tile([P, P], F32, name="scores%d" % j, tag="bank%d" % j) for j in range(GROUPS)]
+        last = GROUPS - 1
+        order = [(j, 0) for j in range(last)] + [(j, 1) for j in range(GROUPS)] + [(last, 0)]
+        for j, o in order:
+            opens = (o == 0) != (j == last)
+            nc.tensor.matmul_mx(
+                out=scores[j][:],
+                lhsT=q_codes[:, o, :].bitcast(FP8X4),
+                lhsT_scale=q_planes[:, o, :],
+                rhs=k_codes[j][:, o, :].bitcast(FP4X4),
+                rhs_scale=k_planes[o][:, j * P : (j + 1) * P],
+                start=opens,
+                stop=not opens,
+            )
+
+        capped = sb.tile([P, PACK, P], F32, name="capped", align_bytes=64)
+        width = P // PACK
+        for j in range(GROUPS):
+            nc.scalar.activation(
+                capped[:, :, j * width : (j + 1) * width],
+                scores[j][:].rearrange("q (s t) -> q t s", t=PACK),
+                ACT.Tanh,
+                scale=1.0 / CAP,
+            )
+
+        neg_c = sb.tile([P, PACK, P], F32, name="neg_c", align_bytes=64)
+        neg_m_half = sb.tile([P, 1], F32, name="neg_m_half")
+        neg_m = sb.tile([P, 1], F32, name="neg_m")
+        half = P // 2
+        nc.vector.tensor_scalar(
+            neg_c[:, :, :half], capped[:, :, :half], -CAP, None, ALU.mult, ALU.min, accum_out=neg_m_half[:]
+        )
+        nc.vector.tensor_scalar(
+            neg_c[:, :, half:], capped[:, :, half:], -CAP, neg_m_half[:], ALU.mult, ALU.min, accum_out=neg_m[:]
+        )
+
+        def turn_values(name, picked, bank):
             slot_pairs = picked[:].bitcast(F32)
             turned = ps.tile([P, 2, P], F32, name=name + "_turned", tag=bank)
             for u in range(2):
                 nc.tensor.transpose(turned[:, u, :], slot_pairs[:, u : N // 2 : 2], ident[:])
             return turned
 
-        def group_values(name, turned, tag):
-            grouped = sb.tile([P, P, PACK], BF16, name=name + "_grouped", tag=tag, align_bytes=64)
+        def group_values(turned, grouped):
             nc.scalar.copy(grouped[:].bitcast(F32), turned[:].rearrange("s u e -> s e u"))
             return grouped
 
-        def quantise(name, grouped, tag):
-            codes = sb.tile([P, P], U32, name=name + "_codes", tag=tag, align_bytes=64)
+        def quantise(name, grouped, codes):
             plane = sb.tile([P, P], U8, name=name + "_plane", align_bytes=64)
             nc.vector.quantize_mx(
                 out=codes[:].bitcast(FP8X4), scales=plane[:], in_=grouped[:].rearrange("s c t -> s (c t)")
             )
             return codes, plane
 
-        capped = sb.tile([P, PACK, P], F32, name="capped", align_bytes=64)
-        for j in range(N // P):
-            nc.scalar.activation(
-                capped[:, :, j * P // PACK : (j + 1) * P // PACK],
-                scores[j][:].rearrange("q (s t) -> q t s", t=PACK),
-                ACT.Tanh,
-                scale=1.0 / CAP,
-            )
+        v0_codes = reused.tile([P, P], U32, name="v0_codes", align_bytes=64, offset=2 * N)
+        v1_codes = sb.tile([P, P], U32, name="v1_codes", align_bytes=64)
+        w_codes = sb.tile([P, P], U32, name="w_codes", align_bytes=64)
 
-        v0_turned = turn_values("v0", v_pool0, "v0_picked", "bank0")
-
-        neg_c = sb.tile([P, PACK, P], F32, name="neg_c", tag="max_after_first_value_gather", align_bytes=64)
-        neg_m = sb.tile([P, 1], F32, name="neg_m")
-        nc.vector.tensor_scalar(neg_c[:], capped[:], -CAP, None, ALU.mult, ALU.min, accum_out=neg_m[:])
+        v0_picked = sb.tile([P, N], BF16, name="v0_picked", tag="k_codes%d" % last, align_bytes=64)
+        nc.scalar.activation(v0_picked[:], listed(v_pool0[:], 0, N), ACT.Copy)
+        v0_turned = turn_values("v0", v0_picked, "bank0")
 
         p_turned = ps.tile([P, PACK, NQ], F32, name="p_turned")
         part_sums = []
@@ -160,28 +184,32 @@ def tile_attend_soft_cap_srtq128n512t2048_kernel(tc, q_words, q_scales, k_words,
             for t in range(2):
                 nc.tensor.transpose(p_turned[:, 2 * u + t, :], p[:, t, :], ident[:])
 
-        row_sum = sb.tile([P, 1], F32, name="row_sum")
+        v1_picked = sb.tile([P, N], BF16, name="v1_picked", align_bytes=64)
+        split = LAST_VALUES_ON_SCALAR
+        nc.scalar.activation(v1_picked[:, :split], listed(v_pool1[:], 0, split), ACT.Copy)
+        nc.vector.tensor_copy(v1_picked[:, split:], listed(v_pool1[:], split, N - split))
+        v0_grouped = group_values(v0_turned, reused.tile([P, P, PACK], BF16, name="v0_grouped", align_bytes=64, offset=4 * N))
+        row_sum = reused.tile([P, 1], F32, name="row_sum", align_bytes=64, offset=6 * N)
         nc.scalar.activation(row_sum[:], part_sums[0][:], ACT.Identity, bias=part_sums[1][:])
-        v0_grouped = group_values("v0", v0_turned, "max_after_first_value_gather")
-        v1_turned = turn_values("v1", v_pool1, "second_value_gather_after_max", "bank2")
-        v0_mx = quantise("v0", v0_grouped, "second_value_gather_after_max")
-        v1_grouped = group_values("v1", v1_turned, "v1_grouped")
+        v1_turned = turn_values("v1", v1_picked, "bank2")
+        v1_grouped = group_values(v1_turned, sb.tile([P, P, PACK], BF16, name="v1_grouped", align_bytes=64))
 
-        w = sb.tile([P, NQ, PACK], BF16, name="w", tag="second_values_after_scale_gather", align_bytes=64)
+        w = reused.tile([P, NQ, PACK], BF16, name="w", align_bytes=64, offset=0)
         nc.vector.tensor_tensor(
             w[:],
             p_turned[:].rearrange("s t q -> s q t"),
             vs_cols[:].unsqueeze(1).to_broadcast([P, NQ, PACK]),
             ALU.mult,
         )
-        inv_row_sum = sb.tile([P, 1], F32, name="inv_row_sum", tag="reciprocal_after_weights", align_bytes=64)
+        v0_mx = quantise("v0", v0_grouped, v0_codes)
+        w_codes, w_plane = quantise("w", w, w_codes)
+        inv_row_sum = sb.tile([P, 1], F32, name="inv_row_sum", tag="reciprocal_after_weights")
         nc.vector.reciprocal(inv_row_sum[:], row_sum[:])
-        w_codes, w_plane = quantise("w", w, "w_codes")
-        v1_mx = quantise("v1", v1_grouped, "v1_codes")
+        v1_mx = quantise("v1", v1_grouped, v1_codes)
 
         y = sb.tile([P, 2, P], F32, name="y")
         for h, (v_codes, v_plane) in enumerate((v0_mx, v1_mx)):
-            sums = ps.tile([P, P], F32, name="sums%d" % h, tag="bank%d" % h)
+            sums = ps.tile([P, P], F32, name="sums%d" % h, tag="bank%d" % (2 * h + 1))
             nc.tensor.matmul_mx(
                 out=sums[:],
                 lhsT=w_codes[:].bitcast(FP8X4),

@@ -26,9 +26,9 @@ SHIFT = QUADRANT // PASSES
 GROUPS = N // P
 COLUMN = 16
 VS_ROW = P - 1
-VALUE_SPLIT = 1280
+VALUE_SPLIT = 1184
 KEY_SPLIT = 448
-LAST_VALUES_ON_SCALAR = 192
+LAST_VALUES_ON_SCALAR = 256
 
 
 def tile_attend_soft_cap_srtq128n512t2048_kernel(tc, q_words, q_scales, k_words, k_scales, vT, vs, offs, out):

@@ -26,8 +26,9 @@ SHIFT = QUADRANT // PASSES
 GROUPS = N // P
 COLUMN = 16
 VS_ROW = P - 1
-VALUE_SPLIT = 1184
+VALUE_SPLIT = 1248
 KEY_SPLIT = 448
+FIRST_VALUES_ON_SCALAR = 384
 LAST_VALUES_ON_SCALAR = 256
 
 
@@ -102,20 +103,30 @@ def tile_attend_soft_cap_srtq128n512t2048_kernel(tc, q_words, q_scales, k_words,
             sb.tile([P, PASSES, 2 * P], U8, name="k_codes%d" % j, tag="k_codes%d" % j, align_bytes=64)
             for j in range(GROUPS)
         ]
-        for j in range(GROUPS + 1):
-            if j < GROUPS:
-                nc.vector.tensor_copy(k_pairs[j][:], listed(k_word_pool[:].bitcast(U32), j * P, P))
-            if j > 0:
-                nc.vector.tensor_copy(
-                    k_codes[j - 1][:].bitcast(U16),
-                    k_pairs[j - 1][:].bitcast(U16).rearrange("p (n o) -> p o n", o=PASSES),
-                )
+
+        def gather_keys(j):
+            nc.vector.tensor_copy(k_pairs[j][:], listed(k_word_pool[:].bitcast(U32), j * P, P))
+
+        def part_keys(j):
+            nc.vector.tensor_copy(
+                k_codes[j][:].bitcast(U16), k_pairs[j][:].bitcast(U16).rearrange("p (n o) -> p o n", o=PASSES)
+            )
+
+        gather_keys(0)
+        gather_keys(1)
+        part_keys(0)
+        gather_keys(2)
+        gather_keys(3)
+        for j in range(1, GROUPS):
+            part_keys(j)
 
         scores = [ps.tile([P, P], F32, name="scores%d" % j, tag="bank%d" % j) for j in range(GROUPS)]
         last = GROUPS - 1
-        order = [(j, 0) for j in range(last)] + [(j, 1) for j in range(GROUPS)] + [(last, 0)]
+        early = GROUPS // 2
+        order = [(j, o) for o in range(PASSES) for j in range(early)]
+        order += [(j, o) for j in range(early, GROUPS) for o in reversed(range(PASSES))]
         for j, o in order:
-            opens = (o == 0) != (j == last)
+            opens = (o == 0) == (j < early)
             nc.tensor.matmul_mx(
                 out=scores[j][:],
                 lhsT=q_codes[:, o, :].bitcast(FP8X4),
@@ -170,7 +181,9 @@ def tile_attend_soft_cap_srtq128n512t2048_kernel(tc, q_words, q_scales, k_words,
         w_codes = sb.tile([P, P], U32, name="w_codes", align_bytes=64)
 
         v0_picked = sb.tile([P, N], BF16, name="v0_picked", tag="k_codes%d" % last, align_bytes=64)
-        nc.scalar.activation(v0_picked[:], listed(v_pool0[:], 0, N), ACT.Copy)
+        split = FIRST_VALUES_ON_SCALAR
+        nc.scalar.activation(v0_picked[:, :split], listed(v_pool0[:], 0, split), ACT.Copy)
+        nc.vector.tensor_copy(v0_picked[:, split:], listed(v_pool0[:], split, N - split))
         v0_turned = turn_values("v0", v0_picked, "bank0")
 
         p_turned = ps.tile([P, PACK, NQ], F32, name="p_turned")

@@ -55,10 +55,6 @@ def tile_attend_soft_cap_srtq128n512t2048_kernel(tc, q_words, q_scales, k_words,
         nc.vector.memset(q_planes[:].bitcast(I32), 0)
         nc.vector.memset(vs_pool[0:VS_ROW, :], 0.0)
         nc.vector.memset(k_plane1[:].bitcast(I32), 0)
-        warm_in = sb.tile([P, 1], F32, name="warm_in")
-        warm_out = sb.tile([P, 1], F32, name="warm_out")
-        nc.gpsimd.memset(warm_in[:], 0.0)
-        nc.scalar.activation(warm_out[:], warm_in[:], ACT.Tanh)
         make_identity(nc, ident[:])
 
         k_word_rows = k_words[0].rearrange("g t b -> g (t b)").bitcast(I32)

@@ -26,10 +26,10 @@ SHIFT = QUADRANT // PASSES
 GROUPS = N // P
 COLUMN = 16
 VS_ROW = P - 1
-VALUE_SPLIT = 1248
+VALUE_SPLIT = 1184
 KEY_SPLIT = 448
 FIRST_VALUES_ON_SCALAR = 384
-LAST_VALUES_ON_SCALAR = 256
+LAST_VALUES_ON_SCALAR = 224
 
 
 def tile_attend_soft_cap_srtq128n512t2048_kernel(tc, q_words, q_scales, k_words, k_scales, vT, vs, offs, out):

@@ -22,12 +22,11 @@ P = 128
 PACK = 4
 QUADRANT = 32
 PASSES = D // (P * PACK)
-SHIFT = QUADRANT // PASSES
 GROUPS = N // P
 COLUMN = 16
 VS_ROW = P - 1
-VALUE_SPLIT = 1184
-KEY_SPLIT = 448
+VALUE_SPLIT = 1216
+KEY_SPLIT = 512
 FIRST_VALUES_ON_SCALAR = 384
 LAST_VALUES_ON_SCALAR = 224
 
@@ -42,7 +41,7 @@ def tile_attend_soft_cap_srtq128n512t2048_kernel(tc, q_words, q_scales, k_words,
         offsets = sb.tile([P, N // COLUMN], U16, name="offsets")
         k_word_pool = sb.tile([P, T], I32, name="k_word_pool")
         k_scale_pool = reused.tile([P, T], U8, name="k_scale_pool", align_bytes=64, offset=0)
-        k_plane1 = sb.tile([P, N], U8, name="k_plane1", align_bytes=64)
+        k_planes = sb.tile([P, PASSES, N], U8, name="k_planes", align_bytes=64)
         vs_pool = sb.tile([P, T], F32, name="vs_pool")
         q_codes = sb.tile([P, PASSES, NQ], I32, name="q_codes", align_bytes=64)
         q_planes = sb.tile([P, PASSES, NQ], U8, name="q_planes", align_bytes=64)
@@ -51,37 +50,41 @@ def tile_attend_soft_cap_srtq128n512t2048_kernel(tc, q_words, q_scales, k_words,
         def listed(pool, first, count):
             return pool.indirect(offsets[:, first // COLUMN : (first + count) // COLUMN])
 
-        nc.vector.memset(k_scale_pool[:].bitcast(I32), 0)
         nc.vector.memset(q_planes[:].bitcast(I32), 0)
+        nc.vector.memset(k_scale_pool[:].bitcast(I32), 0)
         nc.vector.memset(vs_pool[0:VS_ROW, :], 0.0)
-        nc.vector.memset(k_plane1[:].bitcast(I32), 0)
+        nc.vector.memset(k_planes[:].bitcast(I32), 0)
         make_identity(nc, ident[:])
 
         k_word_rows = k_words[0].rearrange("g t b -> g (t b)").bitcast(I32)
         nc.sync.dma_start(k_word_pool[:, :KEY_SPLIT], k_word_rows[:, :KEY_SPLIT])
         nc.sync.dma_start(offsets[:], offs)
         nc.sync.dma_start(vs_pool[VS_ROW : VS_ROW + 1, :], vs[0:1, :])
-        k_scale_rows = k_scales.rearrange("o (quad r) t -> r quad o t", r=PACK)
-        for r in range(PACK):
-            nc.sync.dma_start(k_scale_pool[r:P:SHIFT, :].bitcast(I32), k_scale_rows[r].bitcast(I32))
-        nc.sync.dma_start(k_word_pool[:, KEY_SPLIT:], k_word_rows[:, KEY_SPLIT:])
-        v_pool0 = sb.tile([P, T], F32, name="v_pool0")
-        for quad in range(P // QUADRANT):
+
+        def load_query_plane(quad):
             nc.sync.dma_start(
                 q_planes[QUADRANT * quad : QUADRANT * quad + PACK, :, :].bitcast(I32),
                 q_scales[0][:, PACK * quad : PACK * (quad + 1), :].rearrange("o f q -> f o q").bitcast(I32),
             )
-        nc.sync.dma_start(q_codes[:], q_words[0].rearrange("o g q r -> g o (q r)").bitcast(I32))
-        nc.sync.dma_start(v_pool0[:, :VALUE_SPLIT], vT[0:P, :VALUE_SPLIT])
 
-        k_plane0 = sb.tile([P, N], U8, name="k_plane0", align_bytes=64)
-        nc.vector.tensor_copy(k_plane0[:], listed(k_scale_pool[:], 0, N))
-        for first, count in ((0, 2 * QUADRANT), (2 * QUADRANT, PACK), (3 * QUADRANT, PACK)):
+        load_query_plane(0)
+        nc.sync.dma_start(k_scale_pool[0:P:PACK, :].bitcast(I32), k_scales.rearrange("o f t -> f o t").bitcast(I32))
+        load_query_plane(1)
+        nc.sync.dma_start(k_word_pool[:, KEY_SPLIT:], k_word_rows[:, KEY_SPLIT:])
+        load_query_plane(2)
+        nc.sync.dma_start(q_codes[:], q_words[0].rearrange("o g q r -> g o (q r)").bitcast(I32))
+        v_pool0 = sb.tile([P, T], F32, name="v_pool0")
+        nc.sync.dma_start(v_pool0[:, :VALUE_SPLIT], vT[0:P, :VALUE_SPLIT])
+        load_query_plane(3)
+
+        k_picked = sb.tile([P, N], U8, name="k_picked", align_bytes=64)
+        nc.vector.tensor_copy(k_picked[:], listed(k_scale_pool[:], 0, N))
+        for quad in range(P // QUADRANT):
+            first = QUADRANT * quad
             nc.sync.dma_start(
-                k_plane1[first : first + count, :].bitcast(I32),
-                k_plane0[first + SHIFT : first + SHIFT + count, :].bitcast(I32),
+                k_planes[first : first + PACK, :, :].bitcast(I32),
+                k_picked[first : first + QUADRANT : PACK, :].bitcast(I32),
             )
-        k_planes = (k_plane0, k_plane1)
         v_pool1 = reused.tile([P, T], F32, name="v_pool1", align_bytes=64, offset=0)
         nc.sync.dma_start(v_pool0[:, VALUE_SPLIT:], vT[0:P, VALUE_SPLIT:])
         nc.sync.dma_start(v_pool1[:], vT[P : 2 * P, :])
@@ -118,17 +121,14 @@ def tile_attend_soft_cap_srtq128n512t2048_kernel(tc, q_words, q_scales, k_words,
 
         scores = [ps.tile([P, P], F32, name="scores%d" % j, tag="bank%d" % j) for j in range(GROUPS)]
         last = GROUPS - 1
-        early = GROUPS // 2
-        order = [(j, o) for o in range(PASSES) for j in range(early)]
-        order += [(j, o) for j in range(early, GROUPS) for o in reversed(range(PASSES))]
-        for j, o in order:
-            opens = (o == 0) == (j < early)
+        for j, o in [(j, o) for j in range(GROUPS) for o in range(PASSES)]:
+            opens = o == 0
             nc.tensor.matmul_mx(
                 out=scores[j][:],
                 lhsT=q_codes[:, o, :].bitcast(FP8X4),
                 lhsT_scale=q_planes[:, o, :],
                 rhs=k_codes[j][:, o, :].bitcast(FP4X4),
-                rhs_scale=k_planes[o][:, j * P : (j + 1) * P],
+                rhs_scale=k_planes[:, o, j * P : (j + 1) * P],
                 start=opens,
                 stop=not opens,
             )

@@ -1,7 +1,6 @@
 from contextlib import ExitStack
 
 import concourse.mybir as mybir
-from concourse.masks import make_identity
 
 N, T, D, DV, NQ = 512, 2048, 1024, 256, 128
 CAP = 2.0
@@ -25,10 +24,9 @@ PASSES = D // (P * PACK)
 GROUPS = N // P
 COLUMN = 16
 VS_ROW = P - 1
-VALUE_SPLIT = 1216
+VALUE_SPLIT = 1088
 KEY_SPLIT = 512
-FIRST_VALUES_ON_SCALAR = 384
-LAST_VALUES_ON_SCALAR = 224
+LAST_VALUES_ON_SCALAR = 352
 
 
 def tile_attend_soft_cap_srtq128n512t2048_kernel(tc, q_words, q_scales, k_words, k_scales, vT, vs, offs, out):
@@ -36,6 +34,7 @@ def tile_attend_soft_cap_srtq128n512t2048_kernel(tc, q_words, q_scales, k_words,
     with ExitStack() as ctx:
         sb = ctx.enter_context(tc.tile_pool(name="sb", bufs=1))
         reused = ctx.enter_context(tc.tile_pool(name="reused", bufs=1))
+        held = ctx.enter_context(tc.tile_pool(name="held", bufs=1))
         ps = ctx.enter_context(tc.psum_pool(name="ps", bufs=1))
 
         offsets = sb.tile([P, N // COLUMN], U16, name="offsets")
@@ -54,7 +53,10 @@ def tile_attend_soft_cap_srtq128n512t2048_kernel(tc, q_words, q_scales, k_words,
         nc.vector.memset(k_scale_pool[:].bitcast(I32), 0)
         nc.vector.memset(vs_pool[0:VS_ROW, :], 0.0)
         nc.vector.memset(k_planes[:].bitcast(I32), 0)
-        make_identity(nc, ident[:])
+        distance = sb.tile([P, P], F32, name="distance", tag="vs_picked")
+        nc.gpsimd.iota(distance[:], [[1, P]], base=0, channel_multiplier=-1, allow_small_or_imprecise_dtypes=True)
+        nc.scalar.activation(ident[:], distance[:], ACT.Abs)
+        nc.scalar.activation(ident[:], ident[:], ACT.Relu, bias=1.0, scale=-1.0)
 
         k_word_rows = k_words[0].rearrange("g t b -> g (t b)").bitcast(I32)
         nc.sync.dma_start(k_word_pool[:, :KEY_SPLIT], k_word_rows[:, :KEY_SPLIT])
@@ -89,13 +91,11 @@ def tile_attend_soft_cap_srtq128n512t2048_kernel(tc, q_words, q_scales, k_words,
         nc.sync.dma_start(v_pool0[:, VALUE_SPLIT:], vT[0:P, VALUE_SPLIT:])
         nc.sync.dma_start(v_pool1[:], vT[P : 2 * P, :])
 
-        vs_picked = sb.tile([P, N], F32, name="vs_picked")
+        vs_picked = sb.tile([P, N], F32, name="vs_picked", tag="vs_picked")
         nc.scalar.activation(vs_picked[:], listed(vs_pool[:], 0, N), ACT.Copy)
-        vs_turned = ps.tile([P, PACK, P], F32, name="vs_turned")
+        vs_turned = ps.tile([P, PACK, P], F32, name="vs_turned", tag="scales_then_values")
         for t in range(PACK):
             nc.tensor.transpose(vs_turned[:, t, :], vs_picked[:, t:N:PACK], ident[:])
-        vs_cols = sb.tile([P, PACK], F32, name="vs_cols", tag="reciprocal_after_weights")
-        nc.scalar.copy(vs_cols[:], vs_turned[:, :, VS_ROW])
 
         k_pairs = [sb.tile([P, P], U32, name="k_pairs%d" % j, align_bytes=64) for j in range(GROUPS)]
         k_codes = [
@@ -120,7 +120,6 @@ def tile_attend_soft_cap_srtq128n512t2048_kernel(tc, q_words, q_scales, k_words,
             part_keys(j)
 
         scores = [ps.tile([P, P], F32, name="scores%d" % j, tag="bank%d" % j) for j in range(GROUPS)]
-        last = GROUPS - 1
         for j, o in [(j, o) for j in range(GROUPS) for o in range(PASSES)]:
             opens = o == 0
             nc.tensor.matmul_mx(
@@ -133,7 +132,7 @@ def tile_attend_soft_cap_srtq128n512t2048_kernel(tc, q_words, q_scales, k_words,
                 stop=not opens,
             )
 
-        capped = sb.tile([P, PACK, P], F32, name="capped", align_bytes=64)
+        capped = held.tile([P, PACK, P], F32, name="capped", align_bytes=64, offset=8 * N)
         width = P // PACK
         for j in range(GROUPS):
             nc.scalar.activation(
@@ -143,7 +142,7 @@ def tile_attend_soft_cap_srtq128n512t2048_kernel(tc, q_words, q_scales, k_words,
                 scale=1.0 / CAP,
             )
 
-        neg_c = sb.tile([P, PACK, P], F32, name="neg_c", align_bytes=64)
+        neg_c = held.tile([P, PACK, P], F32, name="neg_c", align_bytes=64, offset=0)
         neg_m_half = sb.tile([P, 1], F32, name="neg_m_half")
         neg_m = sb.tile([P, 1], F32, name="neg_m")
         half = P // 2
@@ -176,11 +175,8 @@ def tile_attend_soft_cap_srtq128n512t2048_kernel(tc, q_words, q_scales, k_words,
         v1_codes = sb.tile([P, P], U32, name="v1_codes", align_bytes=64)
         w_codes = sb.tile([P, P], U32, name="w_codes", align_bytes=64)
 
-        v0_picked = sb.tile([P, N], BF16, name="v0_picked", tag="k_codes%d" % last, align_bytes=64)
-        split = FIRST_VALUES_ON_SCALAR
-        nc.scalar.activation(v0_picked[:, :split], listed(v_pool0[:], 0, split), ACT.Copy)
-        nc.vector.tensor_copy(v0_picked[:, split:], listed(v_pool0[:], split, N - split))
-        v0_turned = turn_values("v0", v0_picked, "bank0")
+        v0_picked = held.tile([P, N], BF16, name="v0_picked", align_bytes=64, offset=8 * N)
+        nc.vector.tensor_copy(v0_picked[:], listed(v_pool0[:], 0, N))
 
         p_turned = ps.tile([P, PACK, NQ], F32, name="p_turned")
         part_sums = []
@@ -193,7 +189,11 @@ def tile_attend_soft_cap_srtq128n512t2048_kernel(tc, q_words, q_scales, k_words,
             for t in range(2):
                 nc.tensor.transpose(p_turned[:, 2 * u + t, :], p[:, t, :], ident[:])
 
-        v1_picked = sb.tile([P, N], BF16, name="v1_picked", align_bytes=64)
+        vs_cols = held.tile([P, PACK], F32, name="vs_cols", align_bytes=64, offset=2 * N)
+        nc.vector.tensor_copy(vs_cols[:], vs_turned[:, :, VS_ROW])
+        v0_turned = turn_values("v0", v0_picked, "scales_then_values")
+
+        v1_picked = held.tile([P, N], BF16, name="v1_picked", align_bytes=64, offset=0)
         split = LAST_VALUES_ON_SCALAR
         nc.scalar.activation(v1_picked[:, :split], listed(v_pool1[:], 0, split), ACT.Copy)
         nc.vector.tensor_copy(v1_picked[:, split:], listed(v_pool1[:], split, N - split))
@@ -212,7 +212,7 @@ def tile_attend_soft_cap_srtq128n512t2048_kernel(tc, q_words, q_scales, k_words,
         )
         v0_mx = quantise("v0", v0_grouped, v0_codes)
         w_codes, w_plane = quantise("w", w, w_codes)
-        inv_row_sum = sb.tile([P, 1], F32, name="inv_row_sum", tag="reciprocal_after_weights")
+        inv_row_sum = held.tile([P, 1], F32, name="inv_row_sum", align_bytes=64, offset=2 * N)
         nc.vector.reciprocal(inv_row_sum[:], row_sum[:])
         v1_mx = quantise("v1", v1_grouped, v1_codes)
 

@@ -26,7 +26,8 @@ COLUMN = 16
 VS_ROW = P - 1
 VALUE_SPLIT = 1088
 KEY_SPLIT = 512
-LAST_VALUES_ON_SCALAR = 352
+FIRST_VALUES_ON_SCALAR = 224
+LAST_VALUES_ON_SCALAR = 224
 
 
 def tile_attend_soft_cap_srtq128n512t2048_kernel(tc, q_words, q_scales, k_words, k_scales, vT, vs, offs, out):
@@ -120,6 +121,7 @@ def tile_attend_soft_cap_srtq128n512t2048_kernel(tc, q_words, q_scales, k_words,
             part_keys(j)
 
         scores = [ps.tile([P, P], F32, name="scores%d" % j, tag="bank%d" % j) for j in range(GROUPS)]
+        last = GROUPS - 1
         for j, o in [(j, o) for j in range(GROUPS) for o in range(PASSES)]:
             opens = o == 0
             nc.tensor.matmul_mx(
@@ -132,7 +134,7 @@ def tile_attend_soft_cap_srtq128n512t2048_kernel(tc, q_words, q_scales, k_words,
                 stop=not opens,
             )
 
-        capped = held.tile([P, PACK, P], F32, name="capped", align_bytes=64, offset=8 * N)
+        capped = sb.tile([P, PACK, P], F32, name="capped", align_bytes=64)
         width = P // PACK
         for j in range(GROUPS):
             nc.scalar.activation(
@@ -175,8 +177,10 @@ def tile_attend_soft_cap_srtq128n512t2048_kernel(tc, q_words, q_scales, k_words,
         v1_codes = sb.tile([P, P], U32, name="v1_codes", align_bytes=64)
         w_codes = sb.tile([P, P], U32, name="w_codes", align_bytes=64)
 
-        v0_picked = held.tile([P, N], BF16, name="v0_picked", align_bytes=64, offset=8 * N)
-        nc.vector.tensor_copy(v0_picked[:], listed(v_pool0[:], 0, N))
+        v0_picked = sb.tile([P, N], BF16, name="v0_picked", tag="k_codes%d" % last, align_bytes=64)
+        split = FIRST_VALUES_ON_SCALAR
+        nc.scalar.activation(v0_picked[:, :split], listed(v_pool0[:], 0, split), ACT.Copy)
+        nc.vector.tensor_copy(v0_picked[:, split:], listed(v_pool0[:], split, N - split))
 
         p_turned = ps.tile([P, PACK, NQ], F32, name="p_turned")
         part_sums = []

@@ -24,8 +24,8 @@ PASSES = D // (P * PACK)
 GROUPS = N // P
 COLUMN = 16
 VS_ROW = P - 1
-VALUE_SPLIT = 1088
-KEY_SPLIT = 512
+VALUE_SPLIT = 1024
+KEY_SPLIT = 448
 FIRST_VALUES_ON_SCALAR = 224
 LAST_VALUES_ON_SCALAR = 224
 
@@ -50,8 +50,8 @@ def tile_attend_soft_cap_srtq128n512t2048_kernel(tc, q_words, q_scales, k_words,
         def listed(pool, first, count):
             return pool.indirect(offsets[:, first // COLUMN : (first + count) // COLUMN])
 
-        nc.vector.memset(q_planes[:].bitcast(I32), 0)
         nc.vector.memset(k_scale_pool[:].bitcast(I32), 0)
+        nc.vector.memset(q_planes[:].bitcast(I32), 0)
         nc.vector.memset(vs_pool[0:VS_ROW, :], 0.0)
         nc.vector.memset(k_planes[:].bitcast(I32), 0)
         distance = sb.tile([P, P], F32, name="distance", tag="vs_picked")
@@ -70,8 +70,8 @@ def tile_attend_soft_cap_srtq128n512t2048_kernel(tc, q_words, q_scales, k_words,
                 q_scales[0][:, PACK * quad : PACK * (quad + 1), :].rearrange("o f q -> f o q").bitcast(I32),
             )
 
-        load_query_plane(0)
         nc.sync.dma_start(k_scale_pool[0:P:PACK, :].bitcast(I32), k_scales.rearrange("o f t -> f o t").bitcast(I32))
+        load_query_plane(0)
         load_query_plane(1)
         nc.sync.dma_start(k_word_pool[:, KEY_SPLIT:], k_word_rows[:, KEY_SPLIT:])
         load_query_plane(2)

@@ -24,9 +24,12 @@ PASSES = D // (P * PACK)
 GROUPS = N // P
 COLUMN = 16
 VS_ROW = P - 1
-VALUE_SPLIT = 1024
-KEY_SPLIT = 448
-FIRST_VALUES_ON_SCALAR = 224
+QUADRANTS = P // QUADRANT
+SCALE_ROW = P - PASSES * PACK * QUADRANTS
+LAST_POOL = PASSES * NQ * PACK
+VALUE_SPLIT = 1152
+KEY_SPLIT = 1024
+FIRST_VALUES_ON_SCALAR = 256
 LAST_VALUES_ON_SCALAR = 224
 
 
@@ -43,14 +46,13 @@ def tile_attend_soft_cap_srtq128n512t2048_kernel(tc, q_words, q_scales, k_words,
         k_scale_pool = reused.tile([P, T], U8, name="k_scale_pool", align_bytes=64, offset=0)
         k_planes = sb.tile([P, PASSES, N], U8, name="k_planes", align_bytes=64)
         vs_pool = sb.tile([P, T], F32, name="vs_pool")
-        q_codes = sb.tile([P, PASSES, NQ], I32, name="q_codes", align_bytes=64)
         q_planes = sb.tile([P, PASSES, NQ], U8, name="q_planes", align_bytes=64)
         ident = sb.tile([P, P], F32, name="ident")
 
         def listed(pool, first, count):
             return pool.indirect(offsets[:, first // COLUMN : (first + count) // COLUMN])
 
-        nc.vector.memset(k_scale_pool[:].bitcast(I32), 0)
+        nc.vector.memset(k_scale_pool[0:SCALE_ROW, :].bitcast(I32), 0)
         nc.vector.memset(q_planes[:].bitcast(I32), 0)
         nc.vector.memset(vs_pool[0:VS_ROW, :], 0.0)
         nc.vector.memset(k_planes[:].bitcast(I32), 0)
@@ -59,36 +61,35 @@ def tile_attend_soft_cap_srtq128n512t2048_kernel(tc, q_words, q_scales, k_words,
         nc.scalar.activation(ident[:], distance[:], ACT.Abs)
         nc.scalar.activation(ident[:], ident[:], ACT.Relu, bias=1.0, scale=-1.0)
 
-        k_word_rows = k_words[0].rearrange("g t b -> g (t b)").bitcast(I32)
-        nc.sync.dma_start(k_word_pool[:, :KEY_SPLIT], k_word_rows[:, :KEY_SPLIT])
-        nc.sync.dma_start(offsets[:], offs)
-        nc.sync.dma_start(vs_pool[VS_ROW : VS_ROW + 1, :], vs[0:1, :])
-
         def load_query_plane(quad):
             nc.sync.dma_start(
                 q_planes[QUADRANT * quad : QUADRANT * quad + PACK, :, :].bitcast(I32),
                 q_scales[0][:, PACK * quad : PACK * (quad + 1), :].rearrange("o f q -> f o q").bitcast(I32),
             )
 
-        nc.sync.dma_start(k_scale_pool[0:P:PACK, :].bitcast(I32), k_scales.rearrange("o f t -> f o t").bitcast(I32))
-        load_query_plane(0)
-        load_query_plane(1)
-        nc.sync.dma_start(k_word_pool[:, KEY_SPLIT:], k_word_rows[:, KEY_SPLIT:])
-        load_query_plane(2)
-        nc.sync.dma_start(q_codes[:], q_words[0].rearrange("o g q r -> g o (q r)").bitcast(I32))
+        k_word_rows = k_words[0].rearrange("g t b -> g (t b)").bitcast(I32)
         v_pool0 = sb.tile([P, T], F32, name="v_pool0")
+        nc.sync.dma_start(k_scale_pool[SCALE_ROW:P, :].bitcast(I32), k_scales.rearrange("o f t -> f o t").bitcast(I32))
+        nc.sync.dma_start(offsets[:], offs)
+        nc.sync.dma_start(k_word_pool[:, :KEY_SPLIT], k_word_rows[:, :KEY_SPLIT])
+        nc.sync.dma_start(vs_pool[VS_ROW : VS_ROW + 1, :], vs[0:1, :])
+        for quad in range(QUADRANTS - 1):
+            load_query_plane(quad)
+        nc.sync.dma_start(k_word_pool[:, KEY_SPLIT:], k_word_rows[:, KEY_SPLIT:])
+        load_query_plane(QUADRANTS - 1)
         nc.sync.dma_start(v_pool0[:, :VALUE_SPLIT], vT[0:P, :VALUE_SPLIT])
-        load_query_plane(3)
 
         k_picked = sb.tile([P, N], U8, name="k_picked", align_bytes=64)
         nc.vector.tensor_copy(k_picked[:], listed(k_scale_pool[:], 0, N))
-        for quad in range(P // QUADRANT):
-            first = QUADRANT * quad
+        for quad in range(QUADRANTS):
+            first = SCALE_ROW + PASSES * PACK * quad
             nc.sync.dma_start(
-                k_planes[first : first + PACK, :, :].bitcast(I32),
-                k_picked[first : first + QUADRANT : PACK, :].bitcast(I32),
+                k_planes[QUADRANT * quad : QUADRANT * quad + PACK, :, :].bitcast(I32),
+                k_picked[first : first + PASSES * PACK, :].bitcast(I32),
             )
-        v_pool1 = reused.tile([P, T], F32, name="v_pool1", align_bytes=64, offset=0)
+        q_codes = reused.tile([P, PASSES, NQ], I32, name="q_codes", align_bytes=64, offset=0)
+        nc.sync.dma_start(q_codes[:], q_words[0].rearrange("o g q r -> g o (q r)").bitcast(I32))
+        v_pool1 = reused.tile([P, T], F32, name="v_pool1", align_bytes=64, offset=LAST_POOL)
         nc.sync.dma_start(v_pool0[:, VALUE_SPLIT:], vT[0:P, VALUE_SPLIT:])
         nc.sync.dma_start(v_pool1[:], vT[P : 2 * P, :])
 
@@ -134,7 +135,7 @@ def tile_attend_soft_cap_srtq128n512t2048_kernel(tc, q_words, q_scales, k_words,
                 stop=not opens,
             )
 
-        capped = sb.tile([P, PACK, P], F32, name="capped", align_bytes=64)
+        capped = held.tile([P, PACK, P], F32, name="capped", align_bytes=64, offset=8 * N)
         width = P // PACK
         for j in range(GROUPS):
             nc.scalar.activation(
@@ -173,14 +174,16 @@ def tile_attend_soft_cap_srtq128n512t2048_kernel(tc, q_words, q_scales, k_words,
             )
             return codes, plane
 
-        v0_codes = reused.tile([P, P], U32, name="v0_codes", align_bytes=64, offset=2 * N)
+        v0_codes = reused.tile([P, P], U32, name="v0_codes", align_bytes=64, offset=LAST_POOL + 2 * N)
         v1_codes = sb.tile([P, P], U32, name="v1_codes", align_bytes=64)
         w_codes = sb.tile([P, P], U32, name="w_codes", align_bytes=64)
 
-        v0_picked = sb.tile([P, N], BF16, name="v0_picked", tag="k_codes%d" % last, align_bytes=64)
         split = FIRST_VALUES_ON_SCALAR
-        nc.scalar.activation(v0_picked[:, :split], listed(v_pool0[:], 0, split), ACT.Copy)
+        v0_head = sb.tile([P, split], BF16, name="v0_head", tag="k_codes%d" % last, align_bytes=64)
+        nc.scalar.activation(v0_head[:], listed(v_pool0[:], 0, split), ACT.Copy)
+        v0_picked = held.tile([P, N], BF16, name="v0_picked", align_bytes=64, offset=8 * N)
         nc.vector.tensor_copy(v0_picked[:, split:], listed(v_pool0[:], split, N - split))
+        nc.vector.tensor_copy(v0_picked[:, :split], v0_head[:])
 
         p_turned = ps.tile([P, PACK, NQ], F32, name="p_turned")
         part_sums = []
@@ -201,13 +204,13 @@ def tile_attend_soft_cap_srtq128n512t2048_kernel(tc, q_words, q_scales, k_words,
         split = LAST_VALUES_ON_SCALAR
         nc.scalar.activation(v1_picked[:, :split], listed(v_pool1[:], 0, split), ACT.Copy)
         nc.vector.tensor_copy(v1_picked[:, split:], listed(v_pool1[:], split, N - split))
-        v0_grouped = group_values(v0_turned, reused.tile([P, P, PACK], BF16, name="v0_grouped", align_bytes=64, offset=4 * N))
-        row_sum = reused.tile([P, 1], F32, name="row_sum", align_bytes=64, offset=6 * N)
+        v0_grouped = group_values(v0_turned, reused.tile([P, P, PACK], BF16, name="v0_grouped", align_bytes=64, offset=LAST_POOL + 4 * N))
+        row_sum = reused.tile([P, 1], F32, name="row_sum", align_bytes=64, offset=LAST_POOL + 6 * N)
         nc.scalar.activation(row_sum[:], part_sums[0][:], ACT.Identity, bias=part_sums[1][:])
         v1_turned = turn_values("v1", v1_picked, "bank2")
         v1_grouped = group_values(v1_turned, sb.tile([P, P, PACK], BF16, name="v1_grouped", align_bytes=64))
 
-        w = reused.tile([P, NQ, PACK], BF16, name="w", align_bytes=64, offset=0)
+        w = reused.tile([P, NQ, PACK], BF16, name="w", align_bytes=64, offset=LAST_POOL)
         nc.vector.tensor_tensor(
             w[:],
             p_turned[:].rearrange("s t q -> s q t"),

@@ -27,7 +27,7 @@ VS_ROW = P - 1
 QUADRANTS = P // QUADRANT
 SCALE_ROW = P - PASSES * PACK * QUADRANTS
 LAST_POOL = PASSES * NQ * PACK
-VALUE_SPLIT = 1152
+VALUE_SPLIT = 640
 KEY_SPLIT = 1024
 FIRST_VALUES_ON_SCALAR = 256
 LAST_VALUES_ON_SCALAR = 224
@@ -42,8 +42,8 @@ def tile_attend_soft_cap_srtq128n512t2048_kernel(tc, q_words, q_scales, k_words,
         ps = ctx.enter_context(tc.psum_pool(name="ps", bufs=1))
 
         offsets = sb.tile([P, N // COLUMN], U16, name="offsets")
-        k_word_pool = sb.tile([P, T], I32, name="k_word_pool")
-        k_scale_pool = reused.tile([P, T], U8, name="k_scale_pool", align_bytes=64, offset=0)
+        k_word_pool = sb.tile([P, T], I32, name="k_word_pool", align_bytes=256)
+        k_scale_pool = reused.tile([P, T], U8, name="k_scale_pool", align_bytes=256, offset=0)
         k_planes = sb.tile([P, PASSES, N], U8, name="k_planes", align_bytes=64)
         vs_pool = sb.tile([P, T], F32, name="vs_pool")
         q_planes = sb.tile([P, PASSES, NQ], U8, name="q_planes", align_bytes=64)
@@ -61,22 +61,19 @@ def tile_attend_soft_cap_srtq128n512t2048_kernel(tc, q_words, q_scales, k_words,
         nc.scalar.activation(ident[:], distance[:], ACT.Abs)
         nc.scalar.activation(ident[:], ident[:], ACT.Relu, bias=1.0, scale=-1.0)
 
-        def load_query_plane(quad):
-            nc.sync.dma_start(
-                q_planes[QUADRANT * quad : QUADRANT * quad + PACK, :, :].bitcast(I32),
-                q_scales[0][:, PACK * quad : PACK * (quad + 1), :].rearrange("o f q -> f o q").bitcast(I32),
-            )
-
         k_word_rows = k_words[0].rearrange("g t b -> g (t b)").bitcast(I32)
-        v_pool0 = sb.tile([P, T], F32, name="v_pool0")
+        v_pool0 = sb.tile([P, T], F32, name="v_pool0", align_bytes=256)
         nc.sync.dma_start(k_scale_pool[SCALE_ROW:P, :].bitcast(I32), k_scales.rearrange("o f t -> f o t").bitcast(I32))
         nc.sync.dma_start(offsets[:], offs)
-        nc.sync.dma_start(k_word_pool[:, :KEY_SPLIT], k_word_rows[:, :KEY_SPLIT])
         nc.sync.dma_start(vs_pool[VS_ROW : VS_ROW + 1, :], vs[0:1, :])
-        for quad in range(QUADRANTS - 1):
-            load_query_plane(quad)
+        nc.sync.dma_start(k_word_pool[:, :KEY_SPLIT], k_word_rows[:, :KEY_SPLIT])
+        q_rows = sb.tile([PACK, PASSES * QUADRANTS, NQ], U8, name="q_rows", align_bytes=64)
+        nc.sync.dma_start(
+            q_rows[:].bitcast(I32), q_scales[0].rearrange("o (g r) q -> r (o g) q", r=PACK).bitcast(I32)
+        )
         nc.sync.dma_start(k_word_pool[:, KEY_SPLIT:], k_word_rows[:, KEY_SPLIT:])
-        load_query_plane(QUADRANTS - 1)
+        q_codes = sb.tile([P, PASSES, NQ], I32, name="q_codes", align_bytes=256)
+        nc.sync.dma_start(q_codes[:], q_words[0].rearrange("o g q r -> g o (q r)").bitcast(I32))
         nc.sync.dma_start(v_pool0[:, :VALUE_SPLIT], vT[0:P, :VALUE_SPLIT])
 
         k_picked = sb.tile([P, N], U8, name="k_picked", align_bytes=64)
@@ -87,9 +84,12 @@ def tile_attend_soft_cap_srtq128n512t2048_kernel(tc, q_words, q_scales, k_words,
                 k_planes[QUADRANT * quad : QUADRANT * quad + PACK, :, :].bitcast(I32),
                 k_picked[first : first + PASSES * PACK, :].bitcast(I32),
             )
-        q_codes = reused.tile([P, PASSES, NQ], I32, name="q_codes", align_bytes=64, offset=0)
-        nc.sync.dma_start(q_codes[:], q_words[0].rearrange("o g q r -> g o (q r)").bitcast(I32))
-        v_pool1 = reused.tile([P, T], F32, name="v_pool1", align_bytes=64, offset=LAST_POOL)
+        for quad in range(QUADRANTS):
+            nc.vector.tensor_copy(
+                q_planes[QUADRANT * quad : QUADRANT * quad + PACK, :, :].bitcast(I32),
+                q_rows[:, quad::QUADRANTS, :].bitcast(I32),
+            )
+        v_pool1 = reused.tile([P, T], F32, name="v_pool1", align_bytes=256, offset=LAST_POOL)
         nc.sync.dma_start(v_pool0[:, VALUE_SPLIT:], vT[0:P, VALUE_SPLIT:])
         nc.sync.dma_start(v_pool1[:], vT[P : 2 * P, :])
 

@@ -27,8 +27,7 @@ VS_ROW = P - 1
 QUADRANTS = P // QUADRANT
 SCALE_ROW = P - PASSES * PACK * QUADRANTS
 LAST_POOL = PASSES * NQ * PACK
-VALUE_SPLIT = 640
-KEY_SPLIT = 1024
+VALUE_SPLIT = 896
 FIRST_VALUES_ON_SCALAR = 256
 LAST_VALUES_ON_SCALAR = 224
 
@@ -66,12 +65,11 @@ def tile_attend_soft_cap_srtq128n512t2048_kernel(tc, q_words, q_scales, k_words,
         nc.sync.dma_start(k_scale_pool[SCALE_ROW:P, :].bitcast(I32), k_scales.rearrange("o f t -> f o t").bitcast(I32))
         nc.sync.dma_start(offsets[:], offs)
         nc.sync.dma_start(vs_pool[VS_ROW : VS_ROW + 1, :], vs[0:1, :])
-        nc.sync.dma_start(k_word_pool[:, :KEY_SPLIT], k_word_rows[:, :KEY_SPLIT])
         q_rows = sb.tile([PACK, PASSES * QUADRANTS, NQ], U8, name="q_rows", align_bytes=64)
         nc.sync.dma_start(
             q_rows[:].bitcast(I32), q_scales[0].rearrange("o (g r) q -> r (o g) q", r=PACK).bitcast(I32)
         )
-        nc.sync.dma_start(k_word_pool[:, KEY_SPLIT:], k_word_rows[:, KEY_SPLIT:])
+        nc.sync.dma_start(k_word_pool[:], k_word_rows)
         q_codes = sb.tile([P, PASSES, NQ], I32, name="q_codes", align_bytes=256)
         nc.sync.dma_start(q_codes[:], q_words[0].rearrange("o g q r -> g o (q r)").bitcast(I32))
         nc.sync.dma_start(v_pool0[:, :VALUE_SPLIT], vT[0:P, :VALUE_SPLIT])

@@ -27,7 +27,7 @@ VS_ROW = P - 1
 QUADRANTS = P // QUADRANT
 SCALE_ROW = P - PASSES * PACK * QUADRANTS
 LAST_POOL = PASSES * NQ * PACK
-VALUE_SPLIT = 896
+VALUE_SPLIT = 768
 FIRST_VALUES_ON_SCALAR = 256
 LAST_VALUES_ON_SCALAR = 224
 
@@ -45,14 +45,14 @@ def tile_attend_soft_cap_srtq128n512t2048_kernel(tc, q_words, q_scales, k_words,
         k_scale_pool = reused.tile([P, T], U8, name="k_scale_pool", align_bytes=256, offset=0)
         k_planes = sb.tile([P, PASSES, N], U8, name="k_planes", align_bytes=64)
         vs_pool = sb.tile([P, T], F32, name="vs_pool")
-        q_planes = sb.tile([P, PASSES, NQ], U8, name="q_planes", align_bytes=64)
+        q_planes = sb.tile([P, PASSES, 2, NQ], U8, name="q_planes", align_bytes=64)
         ident = sb.tile([P, P], F32, name="ident")
 
         def listed(pool, first, count):
             return pool.indirect(offsets[:, first // COLUMN : (first + count) // COLUMN])
 
-        nc.vector.memset(k_scale_pool[0:SCALE_ROW, :].bitcast(I32), 0)
         nc.vector.memset(q_planes[:].bitcast(I32), 0)
+        nc.vector.memset(k_scale_pool[0:SCALE_ROW, :].bitcast(I32), 0)
         nc.vector.memset(vs_pool[0:VS_ROW, :], 0.0)
         nc.vector.memset(k_planes[:].bitcast(I32), 0)
         distance = sb.tile([P, P], F32, name="distance", tag="vs_picked")
@@ -65,10 +65,12 @@ def tile_attend_soft_cap_srtq128n512t2048_kernel(tc, q_words, q_scales, k_words,
         nc.sync.dma_start(k_scale_pool[SCALE_ROW:P, :].bitcast(I32), k_scales.rearrange("o f t -> f o t").bitcast(I32))
         nc.sync.dma_start(offsets[:], offs)
         nc.sync.dma_start(vs_pool[VS_ROW : VS_ROW + 1, :], vs[0:1, :])
-        q_rows = sb.tile([PACK, PASSES * QUADRANTS, NQ], U8, name="q_rows", align_bytes=64)
-        nc.sync.dma_start(
-            q_rows[:].bitcast(I32), q_scales[0].rearrange("o (g r) q -> r (o g) q", r=PACK).bitcast(I32)
-        )
+        q_rows = q_scales[0].rearrange("o (h g r) q -> g r (o h) q", h=2, r=PACK).bitcast(I32)
+        for quad in range(2):
+            nc.sync.dma_start(
+                q_planes[QUADRANT * quad : QUADRANT * quad + PACK].rearrange("r o h q -> r (o h) q").bitcast(I32),
+                q_rows[quad],
+            )
         nc.sync.dma_start(k_word_pool[:], k_word_rows)
         q_codes = sb.tile([P, PASSES, NQ], I32, name="q_codes", align_bytes=256)
         nc.sync.dma_start(q_codes[:], q_words[0].rearrange("o g q r -> g o (q r)").bitcast(I32))
@@ -82,11 +84,8 @@ def tile_attend_soft_cap_srtq128n512t2048_kernel(tc, q_words, q_scales, k_words,
                 k_planes[QUADRANT * quad : QUADRANT * quad + PACK, :, :].bitcast(I32),
                 k_picked[first : first + PASSES * PACK, :].bitcast(I32),
             )
-        for quad in range(QUADRANTS):
-            nc.vector.tensor_copy(
-                q_planes[QUADRANT * quad : QUADRANT * quad + PACK, :, :].bitcast(I32),
-                q_rows[:, quad::QUADRANTS, :].bitcast(I32),
-            )
+        for o in range(PASSES):
+            nc.vector.tensor_copy(q_planes[P // 2 :, o, 0, :].bitcast(I32), q_planes[: P // 2, o, 1, :].bitcast(I32))
         v_pool1 = reused.tile([P, T], F32, name="v_pool1", align_bytes=256, offset=LAST_POOL)
         nc.sync.dma_start(v_pool0[:, VALUE_SPLIT:], vT[0:P, VALUE_SPLIT:])
         nc.sync.dma_start(v_pool1[:], vT[P : 2 * P, :])
@@ -126,7 +125,7 @@ def tile_attend_soft_cap_srtq128n512t2048_kernel(tc, q_words, q_scales, k_words,
             nc.tensor.matmul_mx(
                 out=scores[j][:],
                 lhsT=q_codes[:, o, :].bitcast(FP8X4),
-                lhsT_scale=q_planes[:, o, :],
+                lhsT_scale=q_planes[:, o, 0, :],
                 rhs=k_codes[j][:, o, :].bitcast(FP4X4),
                 rhs_scale=k_planes[:, o, j * P : (j + 1) * P],
                 start=opens,

@@ -41,8 +41,8 @@ def tile_attend_soft_cap_srtq128n512t2048_kernel(tc, q_words, q_scales, k_words,
         ps = ctx.enter_context(tc.psum_pool(name="ps", bufs=1))
 
         offsets = sb.tile([P, N // COLUMN], U16, name="offsets")
-        k_word_pool = sb.tile([P, T], I32, name="k_word_pool", align_bytes=256)
-        k_scale_pool = reused.tile([P, T], U8, name="k_scale_pool", align_bytes=256, offset=0)
+        k_word_pool = sb.tile([P, T], I32, name="k_word_pool")
+        k_scale_pool = reused.tile([P, T], U8, name="k_scale_pool", align_bytes=64, offset=0)
         k_planes = sb.tile([P, PASSES, N], U8, name="k_planes", align_bytes=64)
         vs_pool = sb.tile([P, T], F32, name="vs_pool")
         q_planes = sb.tile([P, PASSES, 2, NQ], U8, name="q_planes", align_bytes=64)
@@ -61,7 +61,7 @@ def tile_attend_soft_cap_srtq128n512t2048_kernel(tc, q_words, q_scales, k_words,
         nc.scalar.activation(ident[:], ident[:], ACT.Relu, bias=1.0, scale=-1.0)
 
         k_word_rows = k_words[0].rearrange("g t b -> g (t b)").bitcast(I32)
-        v_pool0 = sb.tile([P, T], F32, name="v_pool0", align_bytes=256)
+        v_pool0 = sb.tile([P, T], F32, name="v_pool0")
         nc.sync.dma_start(k_scale_pool[SCALE_ROW:P, :].bitcast(I32), k_scales.rearrange("o f t -> f o t").bitcast(I32))
         nc.sync.dma_start(offsets[:], offs)
         nc.sync.dma_start(vs_pool[VS_ROW : VS_ROW + 1, :], vs[0:1, :])
@@ -72,7 +72,7 @@ def tile_attend_soft_cap_srtq128n512t2048_kernel(tc, q_words, q_scales, k_words,
                 q_rows[quad],
             )
         nc.sync.dma_start(k_word_pool[:], k_word_rows)
-        q_codes = sb.tile([P, PASSES, NQ], I32, name="q_codes", align_bytes=256)
+        q_codes = sb.tile([P, PASSES, NQ], I32, name="q_codes", align_bytes=64)
         nc.sync.dma_start(q_codes[:], q_words[0].rearrange("o g q r -> g o (q r)").bitcast(I32))
         nc.sync.dma_start(v_pool0[:, :VALUE_SPLIT], vT[0:P, :VALUE_SPLIT])
 
@@ -86,7 +86,7 @@ def tile_attend_soft_cap_srtq128n512t2048_kernel(tc, q_words, q_scales, k_words,
             )
         for o in range(PASSES):
             nc.vector.tensor_copy(q_planes[P // 2 :, o, 0, :].bitcast(I32), q_planes[: P // 2, o, 1, :].bitcast(I32))
-        v_pool1 = reused.tile([P, T], F32, name="v_pool1", align_bytes=256, offset=LAST_POOL)
+        v_pool1 = reused.tile([P, T], F32, name="v_pool1", align_bytes=64, offset=LAST_POOL)
         nc.sync.dma_start(v_pool0[:, VALUE_SPLIT:], vT[0:P, VALUE_SPLIT:])
         nc.sync.dma_start(v_pool1[:], vT[P : 2 * P, :])
 

@@ -26,7 +26,9 @@ COLUMN = 16
 VS_ROW = P - 1
 QUADRANTS = P // QUADRANT
 SCALE_ROW = P - PASSES * PACK * QUADRANTS
-LAST_POOL = PASSES * NQ * PACK
+OVERLAP = 64
+SCALE_POOL = 4 * N
+LAST_POOL = SCALE_POOL + T - OVERLAP
 VALUE_SPLIT = 768
 FIRST_VALUES_ON_SCALAR = 256
 LAST_VALUES_ON_SCALAR = 224
@@ -42,7 +44,7 @@ def tile_attend_soft_cap_srtq128n512t2048_kernel(tc, q_words, q_scales, k_words,
 
         offsets = sb.tile([P, N // COLUMN], U16, name="offsets")
         k_word_pool = sb.tile([P, T], I32, name="k_word_pool")
-        k_scale_pool = reused.tile([P, T], U8, name="k_scale_pool", align_bytes=64, offset=0)
+        k_scale_pool = reused.tile([P, T], U8, name="k_scale_pool", align_bytes=64, offset=SCALE_POOL)
         k_planes = sb.tile([P, PASSES, N], U8, name="k_planes", align_bytes=64)
         vs_pool = sb.tile([P, T], F32, name="vs_pool")
         q_planes = sb.tile([P, PASSES, 2, NQ], U8, name="q_planes", align_bytes=64)
@@ -55,7 +57,7 @@ def tile_attend_soft_cap_srtq128n512t2048_kernel(tc, q_words, q_scales, k_words,
         nc.vector.memset(k_scale_pool[0:SCALE_ROW, :].bitcast(I32), 0)
         nc.vector.memset(vs_pool[0:VS_ROW, :], 0.0)
         nc.vector.memset(k_planes[:].bitcast(I32), 0)
-        distance = sb.tile([P, P], F32, name="distance", tag="vs_picked")
+        distance = reused.tile([P, P], F32, name="distance", align_bytes=64, offset=OVERLAP)
         nc.gpsimd.iota(distance[:], [[1, P]], base=0, channel_multiplier=-1, allow_small_or_imprecise_dtypes=True)
         nc.scalar.activation(ident[:], distance[:], ACT.Abs)
         nc.scalar.activation(ident[:], ident[:], ACT.Relu, bias=1.0, scale=-1.0)
@@ -90,11 +92,10 @@ def tile_attend_soft_cap_srtq128n512t2048_kernel(tc, q_words, q_scales, k_words,
         nc.sync.dma_start(v_pool0[:, VALUE_SPLIT:], vT[0:P, VALUE_SPLIT:])
         nc.sync.dma_start(v_pool1[:], vT[P : 2 * P, :])
 
-        vs_picked = sb.tile([P, N], F32, name="vs_picked", tag="vs_picked")
+        vs_picked = reused.tile([P, N], F32, name="vs_picked", align_bytes=64, offset=OVERLAP)
         nc.scalar.activation(vs_picked[:], listed(vs_pool[:], 0, N), ACT.Copy)
-        vs_turned = ps.tile([P, PACK, P], F32, name="vs_turned", tag="scales_then_values")
-        for t in range(PACK):
-            nc.tensor.transpose(vs_turned[:, t, :], vs_picked[:, t:N:PACK], ident[:])
+        vs_dealt = sb.tile([P, PACK, P], F32, name="vs_dealt")
+        nc.scalar.activation(vs_dealt[:], vs_picked[:].rearrange("p (s t) -> p t s", t=PACK), ACT.Copy)
 
         k_pairs = [sb.tile([P, P], U32, name="k_pairs%d" % j, align_bytes=64) for j in range(GROUPS)]
         k_codes = [
@@ -141,6 +142,10 @@ def tile_attend_soft_cap_srtq128n512t2048_kernel(tc, q_words, q_scales, k_words,
                 ACT.Tanh,
                 scale=1.0 / CAP,
             )
+
+        vs_turned = ps.tile([P, PACK, P], F32, name="vs_turned", tag="bank0")
+        for t in range(PACK):
+            nc.tensor.transpose(vs_turned[:, t, :], vs_dealt[:, t, :], ident[:])
 
         neg_c = held.tile([P, PACK, P], F32, name="neg_c", align_bytes=64, offset=0)
         neg_m_half = sb.tile([P, 1], F32, name="neg_m_half")
@@ -195,7 +200,7 @@ def tile_attend_soft_cap_srtq128n512t2048_kernel(tc, q_words, q_scales, k_words,
 
         vs_cols = held.tile([P, PACK], F32, name="vs_cols", align_bytes=64, offset=2 * N)
         nc.vector.tensor_copy(vs_cols[:], vs_turned[:, :, VS_ROW])
-        v0_turned = turn_values("v0", v0_picked, "scales_then_values")
+        v0_turned = turn_values("v0", v0_picked, "bank0")
 
         v1_picked = held.tile([P, N], BF16, name="v1_picked", align_bytes=64, offset=0)
         split = LAST_VALUES_ON_SCALAR

@@ -66,14 +66,14 @@ def tile_attend_soft_cap_srtq128n512t2048_kernel(tc, q_words, q_scales, k_words,
         v_pool0 = sb.tile([P, T], F32, name="v_pool0")
         nc.sync.dma_start(k_scale_pool[SCALE_ROW:P, :].bitcast(I32), k_scales.rearrange("o f t -> f o t").bitcast(I32))
         nc.sync.dma_start(offsets[:], offs)
-        nc.sync.dma_start(vs_pool[VS_ROW : VS_ROW + 1, :], vs[0:1, :])
+        nc.sync.dma_start(k_word_pool[:], k_word_rows)
         q_rows = q_scales[0].rearrange("o (h g r) q -> g r (o h) q", h=2, r=PACK).bitcast(I32)
         for quad in range(2):
             nc.sync.dma_start(
                 q_planes[QUADRANT * quad : QUADRANT * quad + PACK].rearrange("r o h q -> r (o h) q").bitcast(I32),
                 q_rows[quad],
             )
-        nc.sync.dma_start(k_word_pool[:], k_word_rows)
+        nc.sync.dma_start(vs_pool[VS_ROW : VS_ROW + 1, :], vs[0:1, :])
         q_codes = sb.tile([P, PASSES, NQ], I32, name="q_codes", align_bytes=64)
         nc.sync.dma_start(q_codes[:], q_words[0].rearrange("o g q r -> g o (q r)").bitcast(I32))
         nc.sync.dma_start(v_pool0[:, :VALUE_SPLIT], vT[0:P, :VALUE_SPLIT])
@@ -94,8 +94,6 @@ def tile_attend_soft_cap_srtq128n512t2048_kernel(tc, q_words, q_scales, k_words,
 
         vs_picked = reused.tile([P, N], F32, name="vs_picked", align_bytes=64, offset=OVERLAP)
         nc.scalar.activation(vs_picked[:], listed(vs_pool[:], 0, N), ACT.Copy)
-        vs_dealt = sb.tile([P, PACK, P], F32, name="vs_dealt")
-        nc.scalar.activation(vs_dealt[:], vs_picked[:].rearrange("p (s t) -> p t s", t=PACK), ACT.Copy)
 
         k_pairs = [sb.tile([P, P], U32, name="k_pairs%d" % j, align_bytes=64) for j in range(GROUPS)]
         k_codes = [
@@ -145,7 +143,7 @@ def tile_attend_soft_cap_srtq128n512t2048_kernel(tc, q_words, q_scales, k_words,
 
         vs_turned = ps.tile([P, PACK, P], F32, name="vs_turned", tag="bank0")
         for t in range(PACK):
-            nc.tensor.transpose(vs_turned[:, t, :], vs_dealt[:, t, :], ident[:])
+            nc.tensor.transpose(vs_turned[:, t, :], vs_picked[:, t:N:PACK], ident[:])
 
         neg_c = held.tile([P, PACK, P], F32, name="neg_c", align_bytes=64, offset=0)
         neg_m_half = sb.tile([P, 1], F32, name="neg_m_half")

@@ -30,7 +30,7 @@ OVERLAP = 64
 SCALE_POOL = 4 * N
 LAST_POOL = SCALE_POOL + T - OVERLAP
 VALUE_SPLIT = 768
-FIRST_VALUES_ON_SCALAR = 256
+FIRST_VALUES_ON_SCALAR = 192
 LAST_VALUES_ON_SCALAR = 224
 
 
@@ -47,7 +47,7 @@ def tile_attend_soft_cap_srtq128n512t2048_kernel(tc, q_words, q_scales, k_words,
         k_scale_pool = reused.tile([P, T], U8, name="k_scale_pool", align_bytes=64, offset=SCALE_POOL)
         k_planes = sb.tile([P, PASSES, N], U8, name="k_planes", align_bytes=64)
         vs_pool = sb.tile([P, T], F32, name="vs_pool")
-        q_planes = sb.tile([P, PASSES, 2, NQ], U8, name="q_planes", align_bytes=64)
+        q_planes = sb.tile([P, PASSES, NQ], U8, name="q_planes", align_bytes=64)
         ident = sb.tile([P, P], F32, name="ident")
 
         def listed(pool, first, count):
@@ -66,13 +66,11 @@ def tile_attend_soft_cap_srtq128n512t2048_kernel(tc, q_words, q_scales, k_words,
         v_pool0 = sb.tile([P, T], F32, name="v_pool0")
         nc.sync.dma_start(k_scale_pool[SCALE_ROW:P, :].bitcast(I32), k_scales.rearrange("o f t -> f o t").bitcast(I32))
         nc.sync.dma_start(offsets[:], offs)
+        q_rows = sb.tile([PACK, PASSES * QUADRANTS, NQ], U8, name="q_rows", align_bytes=64)
+        nc.sync.dma_start(
+            q_rows[:].bitcast(I32), q_scales[0].rearrange("o (g r) q -> r (o g) q", r=PACK).bitcast(I32)
+        )
         nc.sync.dma_start(k_word_pool[:], k_word_rows)
-        q_rows = q_scales[0].rearrange("o (h g r) q -> g r (o h) q", h=2, r=PACK).bitcast(I32)
-        for quad in range(2):
-            nc.sync.dma_start(
-                q_planes[QUADRANT * quad : QUADRANT * quad + PACK].rearrange("r o h q -> r (o h) q").bitcast(I32),
-                q_rows[quad],
-            )
         nc.sync.dma_start(vs_pool[VS_ROW : VS_ROW + 1, :], vs[0:1, :])
         q_codes = sb.tile([P, PASSES, NQ], I32, name="q_codes", align_bytes=64)
         nc.sync.dma_start(q_codes[:], q_words[0].rearrange("o g q r -> g o (q r)").bitcast(I32))
@@ -86,8 +84,11 @@ def tile_attend_soft_cap_srtq128n512t2048_kernel(tc, q_words, q_scales, k_words,
                 k_planes[QUADRANT * quad : QUADRANT * quad + PACK, :, :].bitcast(I32),
                 k_picked[first : first + PASSES * PACK, :].bitcast(I32),
             )
-        for o in range(PASSES):
-            nc.vector.tensor_copy(q_planes[P // 2 :, o, 0, :].bitcast(I32), q_planes[: P // 2, o, 1, :].bitcast(I32))
+        for quad in range(QUADRANTS):
+            nc.vector.tensor_copy(
+                q_planes[QUADRANT * quad : QUADRANT * quad + PACK, :, :].bitcast(I32),
+                q_rows[:, quad::QUADRANTS, :].bitcast(I32),
+            )
         v_pool1 = reused.tile([P, T], F32, name="v_pool1", align_bytes=64, offset=LAST_POOL)
         nc.sync.dma_start(v_pool0[:, VALUE_SPLIT:], vT[0:P, VALUE_SPLIT:])
         nc.sync.dma_start(v_pool1[:], vT[P : 2 * P, :])
@@ -113,9 +114,10 @@ def tile_attend_soft_cap_srtq128n512t2048_kernel(tc, q_words, q_scales, k_words,
         gather_keys(1)
         part_keys(0)
         gather_keys(2)
+        part_keys(1)
         gather_keys(3)
-        for j in range(1, GROUPS):
-            part_keys(j)
+        part_keys(2)
+        part_keys(3)
 
         scores = [ps.tile([P, P], F32, name="scores%d" % j, tag="bank%d" % j) for j in range(GROUPS)]
         last = GROUPS - 1
@@ -124,7 +126,7 @@ def tile_attend_soft_cap_srtq128n512t2048_kernel(tc, q_words, q_scales, k_words,
             nc.tensor.matmul_mx(
                 out=scores[j][:],
                 lhsT=q_codes[:, o, :].bitcast(FP8X4),
-                lhsT_scale=q_planes[:, o, 0, :],
+                lhsT_scale=q_planes[:, o, :],
                 rhs=k_codes[j][:, o, :].bitcast(FP4X4),
                 rhs_scale=k_planes[:, o, j * P : (j + 1) * P],
                 start=opens,

@@ -30,6 +30,7 @@ OVERLAP = 64
 SCALE_POOL = 4 * N
 LAST_POOL = SCALE_POOL + T - OVERLAP
 VALUE_SPLIT = 768
+KEY_SPLIT = 1024
 FIRST_VALUES_ON_SCALAR = 192
 LAST_VALUES_ON_SCALAR = 224
 
@@ -66,12 +67,13 @@ def tile_attend_soft_cap_srtq128n512t2048_kernel(tc, q_words, q_scales, k_words,
         v_pool0 = sb.tile([P, T], F32, name="v_pool0")
         nc.sync.dma_start(k_scale_pool[SCALE_ROW:P, :].bitcast(I32), k_scales.rearrange("o f t -> f o t").bitcast(I32))
         nc.sync.dma_start(offsets[:], offs)
+        nc.sync.dma_start(k_word_pool[:, :KEY_SPLIT], k_word_rows[:, :KEY_SPLIT])
         q_rows = sb.tile([PACK, PASSES * QUADRANTS, NQ], U8, name="q_rows", align_bytes=64)
         nc.sync.dma_start(
             q_rows[:].bitcast(I32), q_scales[0].rearrange("o (g r) q -> r (o g) q", r=PACK).bitcast(I32)
         )
-        nc.sync.dma_start(k_word_pool[:], k_word_rows)
         nc.sync.dma_start(vs_pool[VS_ROW : VS_ROW + 1, :], vs[0:1, :])
+        nc.sync.dma_start(k_word_pool[:, KEY_SPLIT:], k_word_rows[:, KEY_SPLIT:])
         q_codes = sb.tile([P, PASSES, NQ], I32, name="q_codes", align_bytes=64)
         nc.sync.dma_start(q_codes[:], q_words[0].rearrange("o g q r -> g o (q r)").bitcast(I32))
         nc.sync.dma_start(v_pool0[:, :VALUE_SPLIT], vT[0:P, :VALUE_SPLIT])
@@ -166,18 +168,17 @@ def tile_attend_soft_cap_srtq128n512t2048_kernel(tc, q_words, q_scales, k_words,
             return turned
 
         def group_values(turned, grouped):
-            nc.scalar.copy(grouped[:].bitcast(F32), turned[:].rearrange("s u e -> s e u"))
+            nc.scalar.copy(grouped[:].bitcast(F32), turned.rearrange("s u e -> s e u"))
             return grouped
 
         def quantise(name, grouped, codes):
-            plane = sb.tile([P, P], U8, name=name + "_plane", align_bytes=64)
+            plane = sb.tile([P, codes.shape[1]], U8, name=name + "_plane", align_bytes=64)
             nc.vector.quantize_mx(
                 out=codes[:].bitcast(FP8X4), scales=plane[:], in_=grouped[:].rearrange("s c t -> s (c t)")
             )
             return codes, plane
 
         v0_codes = reused.tile([P, P], U32, name="v0_codes", align_bytes=64, offset=LAST_POOL + 2 * N)
-        v1_codes = sb.tile([P, P], U32, name="v1_codes", align_bytes=64)
         w_codes = sb.tile([P, P], U32, name="w_codes", align_bytes=64)
 
         split = FIRST_VALUES_ON_SCALAR
@@ -206,11 +207,18 @@ def tile_attend_soft_cap_srtq128n512t2048_kernel(tc, q_words, q_scales, k_words,
         split = LAST_VALUES_ON_SCALAR
         nc.scalar.activation(v1_picked[:, :split], listed(v_pool1[:], 0, split), ACT.Copy)
         nc.vector.tensor_copy(v1_picked[:, split:], listed(v_pool1[:], split, N - split))
-        v0_grouped = group_values(v0_turned, reused.tile([P, P, PACK], BF16, name="v0_grouped", align_bytes=64, offset=LAST_POOL + 4 * N))
+        v0_grouped = group_values(v0_turned[:], reused.tile([P, P, PACK], BF16, name="v0_grouped", align_bytes=64, offset=LAST_POOL + 4 * N))
         row_sum = reused.tile([P, 1], F32, name="row_sum", align_bytes=64, offset=LAST_POOL + 6 * N)
         nc.scalar.activation(row_sum[:], part_sums[0][:], ACT.Identity, bias=part_sums[1][:])
         v1_turned = turn_values("v1", v1_picked, "bank2")
-        v1_grouped = group_values(v1_turned, sb.tile([P, P, PACK], BF16, name="v1_grouped", align_bytes=64))
+        half = P // 2
+        v1_grouped = [
+            group_values(
+                v1_turned[:, :, h * half : (h + 1) * half],
+                sb.tile([P, half, PACK], BF16, name="v1_grouped%d" % h, align_bytes=64),
+            )
+            for h in range(2)
+        ]
 
         w = reused.tile([P, NQ, PACK], BF16, name="w", align_bytes=64, offset=LAST_POOL)
         nc.vector.tensor_tensor(
@@ -219,15 +227,19 @@ def tile_attend_soft_cap_srtq128n512t2048_kernel(tc, q_words, q_scales, k_words,
             vs_cols[:].unsqueeze(1).to_broadcast([P, NQ, PACK]),
             ALU.mult,
         )
-        v0_mx = quantise("v0", v0_grouped, v0_codes)
+        parts = [quantise("v0", v0_grouped, v0_codes)]
         w_codes, w_plane = quantise("w", w, w_codes)
         inv_row_sum = held.tile([P, 1], F32, name="inv_row_sum", align_bytes=64, offset=2 * N)
         nc.vector.reciprocal(inv_row_sum[:], row_sum[:])
-        v1_mx = quantise("v1", v1_grouped, v1_codes)
+        for h in range(2):
+            codes = sb.tile([P, half], U32, name="v1_codes%d" % h, align_bytes=64)
+            parts.append(quantise("v1_%d" % h, v1_grouped[h], codes))
 
-        y = sb.tile([P, 2, P], F32, name="y")
-        for h, (v_codes, v_plane) in enumerate((v0_mx, v1_mx)):
-            sums = ps.tile([P, P], F32, name="sums%d" % h, tag="bank%d" % (2 * h + 1))
+        y = sb.tile([P, DV], F32, name="y")
+        first = 0
+        for h, (v_codes, v_plane) in enumerate(parts):
+            count = v_codes.shape[1]
+            sums = ps.tile([P, count], F32, name="sums%d" % h)
             nc.tensor.matmul_mx(
                 out=sums[:],
                 lhsT=w_codes[:].bitcast(FP8X4),
@@ -237,8 +249,10 @@ def tile_attend_soft_cap_srtq128n512t2048_kernel(tc, q_words, q_scales, k_words,
                 start=True,
                 stop=True,
             )
-            if h == 0:
-                nc.scalar.activation(y[:, h, :], sums[:], ACT.Copy, scale=inv_row_sum[:])
+            if h < 2:
+                nc.scalar.activation(y[:, first : first + count], sums[:], ACT.Copy, scale=inv_row_sum[:])
             else:
-                nc.vector.tensor_scalar(y[:, h, :], sums[:], inv_row_sum[:], None, ALU.mult)
-            nc.sync.dma_start(out[0][:, h * P : (h + 1) * P], y[:, h, :])
+                nc.vector.tensor_scalar(y[:, first : first + count], sums[:], inv_row_sum[:], None, ALU.mult)
+            first += count
+            if first % P == 0:
+                nc.sync.dma_start(out[0][:, first - P : first], y[:, first - P : first])

from contextlib import ExitStack

import concourse.mybir as mybir

N, T, D, DV, NQ = 512, 2048, 1024, 256, 128
CAP = 2.0
FLOPS = 2 * NQ * N * (D + DV)

F32 = mybir.dt.float32
BF16 = mybir.dt.bfloat16
I32 = mybir.dt.int32
U32 = mybir.dt.uint32
U16 = mybir.dt.uint16
U8 = mybir.dt.uint8
FP8X4 = mybir.dt.float8_e4m3fn_x4
FP4X4 = mybir.dt.float4_e2m1fn_x4
ACT = mybir.ActivationFunctionType
ALU = mybir.AluOpType

P = 128
PACK = 4
QUADRANT = 32
PASSES = D // (P * PACK)
GROUPS = N // P
COLUMN = 16
VS_ROW = P - 1
QUADRANTS = P // QUADRANT
SCALE_ROW = P - PASSES * PACK * QUADRANTS
OVERLAP = 64
SCALE_POOL = 4 * N
LAST_POOL = SCALE_POOL + T - OVERLAP
VALUE_SPLIT = 768
KEY_SPLIT = 1024
FIRST_VALUES_ON_SCALAR = 192
LAST_VALUES_ON_SCALAR = 224


def tile_attend_soft_cap_srtq128n512t2048_kernel(tc, q_words, q_scales, k_words, k_scales, vT, vs, offs, out):
    nc = tc.nc
    with ExitStack() as ctx:
        sb = ctx.enter_context(tc.tile_pool(name="sb", bufs=1))
        reused = ctx.enter_context(tc.tile_pool(name="reused", bufs=1))
        held = ctx.enter_context(tc.tile_pool(name="held", bufs=1))
        ps = ctx.enter_context(tc.psum_pool(name="ps", bufs=1))

        offsets = sb.tile([P, N // COLUMN], U16, name="offsets")
        k_word_pool = sb.tile([P, T], I32, name="k_word_pool")
        k_scale_pool = reused.tile([P, T], U8, name="k_scale_pool", align_bytes=64, offset=SCALE_POOL)
        k_planes = sb.tile([P, PASSES, N], U8, name="k_planes", align_bytes=64)
        vs_pool = sb.tile([P, T], F32, name="vs_pool")
        q_planes = sb.tile([P, PASSES, NQ], U8, name="q_planes", align_bytes=64)
        ident = sb.tile([P, P], F32, name="ident")

        def listed(pool, first, count):
            return pool.indirect(offsets[:, first // COLUMN : (first + count) // COLUMN])

        nc.vector.memset(q_planes[:].bitcast(I32), 0)
        nc.vector.memset(k_scale_pool[0:SCALE_ROW, :].bitcast(I32), 0)
        nc.vector.memset(vs_pool[0:VS_ROW, :], 0.0)
        nc.vector.memset(k_planes[:].bitcast(I32), 0)
        distance = reused.tile([P, P], F32, name="distance", align_bytes=64, offset=OVERLAP)
        nc.gpsimd.iota(distance[:], [[1, P]], base=0, channel_multiplier=-1, allow_small_or_imprecise_dtypes=True)
        nc.scalar.activation(ident[:], distance[:], ACT.Abs)
        nc.scalar.activation(ident[:], ident[:], ACT.Relu, bias=1.0, scale=-1.0)

        k_word_rows = k_words[0].rearrange("g t b -> g (t b)").bitcast(I32)
        v_pool0 = sb.tile([P, T], F32, name="v_pool0")
        nc.sync.dma_start(k_scale_pool[SCALE_ROW:P, :].bitcast(I32), k_scales.rearrange("o f t -> f o t").bitcast(I32))
        nc.sync.dma_start(offsets[:], offs)
        nc.sync.dma_start(k_word_pool[:, :KEY_SPLIT], k_word_rows[:, :KEY_SPLIT])
        q_rows = sb.tile([PACK, PASSES * QUADRANTS, NQ], U8, name="q_rows", align_bytes=64)
        nc.sync.dma_start(
            q_rows[:].bitcast(I32), q_scales[0].rearrange("o (g r) q -> r (o g) q", r=PACK).bitcast(I32)
        )
        nc.sync.dma_start(vs_pool[VS_ROW : VS_ROW + 1, :], vs[0:1, :])
        nc.sync.dma_start(k_word_pool[:, KEY_SPLIT:], k_word_rows[:, KEY_SPLIT:])
        q_codes = sb.tile([P, PASSES, NQ], I32, name="q_codes", align_bytes=64)
        nc.sync.dma_start(q_codes[:], q_words[0].rearrange("o g q r -> g o (q r)").bitcast(I32))
        nc.sync.dma_start(v_pool0[:, :VALUE_SPLIT], vT[0:P, :VALUE_SPLIT])

        k_picked = sb.tile([P, N], U8, name="k_picked", align_bytes=64)
        nc.vector.tensor_copy(k_picked[:], listed(k_scale_pool[:], 0, N))
        for quad in range(QUADRANTS):
            first = SCALE_ROW + PASSES * PACK * quad
            nc.sync.dma_start(
                k_planes[QUADRANT * quad : QUADRANT * quad + PACK, :, :].bitcast(I32),
                k_picked[first : first + PASSES * PACK, :].bitcast(I32),
            )
        for quad in range(QUADRANTS):
            nc.vector.tensor_copy(
                q_planes[QUADRANT * quad : QUADRANT * quad + PACK, :, :].bitcast(I32),
                q_rows[:, quad::QUADRANTS, :].bitcast(I32),
            )
        v_pool1 = reused.tile([P, T], F32, name="v_pool1", align_bytes=64, offset=LAST_POOL)
        nc.sync.dma_start(v_pool0[:, VALUE_SPLIT:], vT[0:P, VALUE_SPLIT:])
        nc.sync.dma_start(v_pool1[:], vT[P : 2 * P, :])

        vs_picked = reused.tile([P, N], F32, name="vs_picked", align_bytes=64, offset=OVERLAP)
        nc.scalar.activation(vs_picked[:], listed(vs_pool[:], 0, N), ACT.Copy)

        k_pairs = [sb.tile([P, P], U32, name="k_pairs%d" % j, align_bytes=64) for j in range(GROUPS)]
        k_codes = [
            sb.tile([P, PASSES, 2 * P], U8, name="k_codes%d" % j, tag="k_codes%d" % j, align_bytes=64)
            for j in range(GROUPS)
        ]

        def gather_keys(j):
            nc.vector.tensor_copy(k_pairs[j][:], listed(k_word_pool[:].bitcast(U32), j * P, P))

        def part_keys(j):
            nc.vector.tensor_copy(
                k_codes[j][:].bitcast(U16), k_pairs[j][:].bitcast(U16).rearrange("p (n o) -> p o n", o=PASSES)
            )

        gather_keys(0)
        gather_keys(1)
        part_keys(0)
        gather_keys(2)
        part_keys(1)
        gather_keys(3)
        part_keys(2)
        part_keys(3)

        scores = [ps.tile([P, P], F32, name="scores%d" % j, tag="bank%d" % j) for j in range(GROUPS)]
        last = GROUPS - 1
        for j, o in [(j, o) for j in range(GROUPS) for o in range(PASSES)]:
            opens = o == 0
            nc.tensor.matmul_mx(
                out=scores[j][:],
                lhsT=q_codes[:, o, :].bitcast(FP8X4),
                lhsT_scale=q_planes[:, o, :],
                rhs=k_codes[j][:, o, :].bitcast(FP4X4),
                rhs_scale=k_planes[:, o, j * P : (j + 1) * P],
                start=opens,
                stop=not opens,
            )

        capped = held.tile([P, PACK, P], F32, name="capped", align_bytes=64, offset=8 * N)
        width = P // PACK
        for j in range(GROUPS):
            nc.scalar.activation(
                capped[:, :, j * width : (j + 1) * width],
                scores[j][:].rearrange("q (s t) -> q t s", t=PACK),
                ACT.Tanh,
                scale=1.0 / CAP,
            )

        vs_turned = ps.tile([P, PACK, P], F32, name="vs_turned", tag="bank0")
        for t in range(PACK):
            nc.tensor.transpose(vs_turned[:, t, :], vs_picked[:, t:N:PACK], ident[:])

        neg_c = held.tile([P, PACK, P], F32, name="neg_c", align_bytes=64, offset=0)
        neg_m_half = sb.tile([P, 1], F32, name="neg_m_half")
        neg_m = sb.tile([P, 1], F32, name="neg_m")
        half = P // 2
        nc.vector.tensor_scalar(
            neg_c[:, :, :half], capped[:, :, :half], -CAP, None, ALU.mult, ALU.min, accum_out=neg_m_half[:]
        )
        nc.vector.tensor_scalar(
            neg_c[:, :, half:], capped[:, :, half:], -CAP, neg_m_half[:], ALU.mult, ALU.min, accum_out=neg_m[:]
        )

        def turn_values(name, picked, bank):
            slot_pairs = picked[:].bitcast(F32)
            turned = ps.tile([P, 2, P], F32, name=name + "_turned", tag=bank)
            for u in range(2):
                nc.tensor.transpose(turned[:, u, :], slot_pairs[:, u : N // 2 : 2], ident[:])
            return turned

        def group_values(turned, grouped):
            nc.scalar.copy(grouped[:].bitcast(F32), turned.rearrange("s u e -> s e u"))
            return grouped

        def quantise(name, grouped, codes):
            plane = sb.tile([P, codes.shape[1]], U8, name=name + "_plane", align_bytes=64)
            nc.vector.quantize_mx(
                out=codes[:].bitcast(FP8X4), scales=plane[:], in_=grouped[:].rearrange("s c t -> s (c t)")
            )
            return codes, plane

        v0_codes = reused.tile([P, P], U32, name="v0_codes", align_bytes=64, offset=LAST_POOL + 2 * N)
        w_codes = sb.tile([P, P], U32, name="w_codes", align_bytes=64)

        split = FIRST_VALUES_ON_SCALAR
        v0_head = sb.tile([P, split], BF16, name="v0_head", tag="k_codes%d" % last, align_bytes=64)
        nc.scalar.activation(v0_head[:], listed(v_pool0[:], 0, split), ACT.Copy)
        v0_picked = held.tile([P, N], BF16, name="v0_picked", align_bytes=64, offset=8 * N)
        nc.vector.tensor_copy(v0_picked[:, split:], listed(v_pool0[:], split, N - split))
        nc.vector.tensor_copy(v0_picked[:, :split], v0_head[:])

        p_turned = ps.tile([P, PACK, NQ], F32, name="p_turned")
        part_sums = []
        for u in range(2):
            p = sb.tile([P, 2, P], F32, name="p%d" % u, align_bytes=64)
            part_sums.append(sb.tile([P, 1], F32, name="part_sum%d" % u))
            nc.scalar.activation(
                p[:], neg_c[:, 2 * u : 2 * u + 2, :], ACT.Exp, bias=neg_m[:], scale=-1.0, accum_out=part_sums[u][:]
            )
            for t in range(2):
                nc.tensor.transpose(p_turned[:, 2 * u + t, :], p[:, t, :], ident[:])

        vs_cols = held.tile([P, PACK], F32, name="vs_cols", align_bytes=64, offset=2 * N)
        nc.vector.tensor_copy(vs_cols[:], vs_turned[:, :, VS_ROW])
        v0_turned = turn_values("v0", v0_picked, "bank0")

        v1_picked = held.tile([P, N], BF16, name="v1_picked", align_bytes=64, offset=0)
        split = LAST_VALUES_ON_SCALAR
        nc.scalar.activation(v1_picked[:, :split], listed(v_pool1[:], 0, split), ACT.Copy)
        nc.vector.tensor_copy(v1_picked[:, split:], listed(v_pool1[:], split, N - split))
        v0_grouped = group_values(v0_turned[:], reused.tile([P, P, PACK], BF16, name="v0_grouped", align_bytes=64, offset=LAST_POOL + 4 * N))
        row_sum = reused.tile([P, 1], F32, name="row_sum", align_bytes=64, offset=LAST_POOL + 6 * N)
        nc.scalar.activation(row_sum[:], part_sums[0][:], ACT.Identity, bias=part_sums[1][:])
        v1_turned = turn_values("v1", v1_picked, "bank2")
        half = P // 2
        v1_grouped = [
            group_values(
                v1_turned[:, :, h * half : (h + 1) * half],
                sb.tile([P, half, PACK], BF16, name="v1_grouped%d" % h, align_bytes=64),
            )
            for h in range(2)
        ]

        w = reused.tile([P, NQ, PACK], BF16, name="w", align_bytes=64, offset=LAST_POOL)
        nc.vector.tensor_tensor(
            w[:],
            p_turned[:].rearrange("s t q -> s q t"),
            vs_cols[:].unsqueeze(1).to_broadcast([P, NQ, PACK]),
            ALU.mult,
        )
        parts = [quantise("v0", v0_grouped, v0_codes)]
        w_codes, w_plane = quantise("w", w, w_codes)
        inv_row_sum = held.tile([P, 1], F32, name="inv_row_sum", align_bytes=64, offset=2 * N)
        nc.vector.reciprocal(inv_row_sum[:], row_sum[:])
        for h in range(2):
            codes = sb.tile([P, half], U32, name="v1_codes%d" % h, align_bytes=64)
            parts.append(quantise("v1_%d" % h, v1_grouped[h], codes))

        y = sb.tile([P, DV], F32, name="y")
        first = 0
        for h, (v_codes, v_plane) in enumerate(parts):
            count = v_codes.shape[1]
            sums = ps.tile([P, count], F32, name="sums%d" % h)
            nc.tensor.matmul_mx(
                out=sums[:],
                lhsT=w_codes[:].bitcast(FP8X4),
                lhsT_scale=w_plane[:],
                rhs=v_codes[:].bitcast(FP8X4),
                rhs_scale=v_plane[:],
                start=True,
                stop=True,
            )
            if h < 2:
                nc.scalar.activation(y[:, first : first + count], sums[:], ACT.Copy, scale=inv_row_sum[:])
            else:
                nc.vector.tensor_scalar(y[:, first : first + count], sums[:], inv_row_sum[:], None, ALU.mult)
            first += count
            if first % P == 0:
                nc.sync.dma_start(out[0][:, first - P : first], y[:, first - P : first])
